import numpy as np, ml_dtypes
CORES = [78,86,94,102,110,118]
N = 6
BF = ml_dtypes.bfloat16
def gentries(a):
    return np.ascontiguousarray(a.reshape(8, 16, -1).transpose(0, 2, 1)).reshape(8, -1)
def gtable(e):
    e = np.asarray(e); return np.ascontiguousarray(e.reshape(8, -1, 16).transpose(0, 2, 1)).reshape(128, -1).astype(np.int32)
FR, PR, MS, M, NT, KR, H, S = 3, 2, 2048, 4096, 1024, 4, 512, 11
C = 64
SIZES = ((24, 0), (48, 0), (80, 0), (128, 8), (192, 16), (320, 24), (640, 24), (NT, 24))
def sign(rng, shape):
    return 2 * rng.integers(0, 2, shape) - 1
def far(rng, shape):
    return rng.integers(244, 257, shape)
def scene(rng, size, w):
    pm = np.argsort(rng.random((8, M)), axis=1); inv = np.argsort(pm, axis=1); cl = pm % C
    cen = np.rint(rng.integers(16, 241, (8, 16, C)) * size)
    z = np.take_along_axis(cen, cl[:, None, :], 2)[None] + np.rint((2 * rng.random((FR, 8, 16, M)) - 1) * w)
    n0 = rng.integers(0, M, (8, NT)); c0 = np.take_along_axis(cl, n0, 1)
    x0 = np.take_along_axis(cen, c0[:, None, :], 2) + np.rint((2 * rng.random((8, 16, NT)) - 1) * rng.choice(np.array([16.0, 32.0, 48.0]), (8, 1, NT)))
    j = ((M // C) * rng.random((FR, 8, 3, M)) ** 3).astype(np.int64)
    same = inv[np.arange(8)[None, :, None, None], cl[None, :, None, :] + C * j]
    nx = np.where(rng.random((FR, 8, 3, M)) < np.array([0.6, 0.3, 0.3])[:, None], same, rng.integers(0, M, (FR, 8, 3, M)))
    nx[:, :, 1] = np.where(rng.random((FR, 8, M)) < 0.03125, nx[:, :, 0], nx[:, :, 1])
    return {"z": z, "nx": nx, "x0": x0, "n0": n0}
def folk(rng, s):
    return rng.permutation(NT)[:s][(s * rng.random((N, KR, H)) ** 1.5).astype(np.int64)]
def life(rng, d):
    o = rng.permutation(8); d["hy"] = np.zeros((N, 8, KR, H), np.int64); d["u"] = np.zeros((N, 8, FR, KR, H), np.int64)
    for g in range(8):
        s, lo = SIZES[int(o[g])]; d["hy"][:, g] = folk(rng, s); d["u"][:, g] = rng.integers(lo, 64, (N, FR, KR, H))
    return d
def plain(rng):
    return life(rng, scene(rng, np.ones((8, 1, C)), rng.choice(np.array([16.0, 32.0, 48.0, 64.0, 80.0]), (FR, 8, 1, M))))
def deal(rng, s):
    f = rng.permutation(N * H).reshape(N, 1, H) * KR + np.arange(KR)[:, None]
    return rng.permutation(NT)[:s][f % s], f // s
def quad(rng, d, g, near):
    b = rng.permutation(M // 4)[:NT]; d["n0"][g] = 4 * b
    x = rng.integers(32, 129, (16, NT)); d["x0"][g] = x
    for m in range(3): d["nx"][:, g, m] = 4 * (np.arange(M) // 4) + m + 1
    zz = d["z"][:, g]; zz[:] = far(rng, zz.shape)
    safe = np.argsort(rng.random((16, NT)), axis=0) < (16 if near == 3 else rng.integers(5, 17, (1, NT)))
    for m in range(1, near + 1):
        zz[:, :, 4 * b + m] = x + np.where(safe, rng.integers(-16, 17, (FR, 16, NT)), rng.integers(-72, 73, (FR, 16, NT)))
def soft(rng, d):
    q = int(rng.integers(0, N)); e = 3 * KR; k = np.arange(KR)[:, None]
    for g in range(8):
        c = rng.permutation(M)[:e]
        near = np.argsort(rng.random((16, e)), axis=0) < 5; near[:, :KR] = True
        x = np.where(near, rng.integers(96, 161, (16, e)), rng.integers(224, 257, (16, e))).astype(np.float64)
        step = np.full((16, e), 32.0); step[:, :KR] = 4.0 * (1 + rng.permutation(16) % 7)[:, None]
        d["x0"][g][:, :e] = x; d["n0"][g][:e] = c; d["nx"][:, g][:, :, c] = c
        for t in range(FR):
            v = np.where(near, x + sign(rng, (16, e)) * step, np.where(x >= 132, 8.0, 256.0))
            d["z"][t, g][:, c] = v; x = x + 0.25 * (v - x)
        o = rng.permutation(H)[H // 32:]; few = o[:H // 128]
        d["hy"][q, g][:, o] = KR + 2 * k + rng.integers(0, 2, (KR, len(o))); d["hy"][q, g][:, few] = k
        d["u"][q, g][:, :, o] = 63
def pack(d):
    z = np.clip(d["z"], 8, 256) * 0.03125; x = (np.clip(d["x0"], 8, 256) * 0.03125).reshape(1, 128, NT)
    z = np.ascontiguousarray(z.reshape(FR, 8, 16, PR, MS).transpose(0, 3, 1, 2, 4)).reshape(N, 128, MS)
    s = np.ascontiguousarray(d["nx"].reshape(FR, 8, 3, PR, MS).transpose(0, 3, 1, 2, 4)).reshape(N, 24, MS)
    return {"z": z.astype(np.float32).astype(BF), "nx": s.astype(np.int32), "x0": np.ascontiguousarray(np.repeat(x, N, axis=0)).astype(np.float32),
            "n0": np.ascontiguousarray(np.repeat(d["n0"][None], N, axis=0)).astype(np.int32),
            "hyp": np.stack([gtable(a.reshape(8, -1)) for a in d["hy"]]), "uu": np.stack([gtable(a.reshape(8, -1)) for a in d["u"]])}
def setup_inputs(rng):
    return pack(plain(rng))
def setup_inputs_spread(rng):
    d = life(rng, scene(rng, rng.choice(np.array([0.5, 0.75, 1.0, 1.25]), (8, 1, C)), 40 * np.exp2(2 * rng.random((FR, 8, 1, M)) - 1)))
    v = (64 * rng.random(d["u"].shape) ** rng.choice(np.array([0.5, 1.0, 2.0]), (1, 8, 1, 1, 1))).astype(np.int64)
    d["u"] = np.where(rng.random(v.shape) < 0.25, v, d["u"])
    soft(rng, d)
    return pack(d)
def atends(rng, a, hi, share):
    return np.where(rng.random(a.shape) < share, hi * rng.integers(0, 2, a.shape), a)
def setup_inputs_ends(rng):
    d = plain(rng); v = sign(rng, (8, 16, 1)); p = np.array([0.0, 0.0, 0.1, 0.3])
    sz = v[None] * sign(rng, (FR, 8, 1, M)) * np.where(rng.random((FR, 8, 16, M)) < rng.choice(p, (FR, 8, 1, M)), -1, 1)
    sx = v * sign(rng, (8, 1, NT)) * np.where(rng.random((8, 16, NT)) < rng.choice(p, (8, 1, NT)), -1, 1)
    sz[..., 0] = -v[None, :, :, 0]; sz[..., M - 1] = v[None, :, :, 0]; sx[..., 0] = -v[..., 0]; sx[..., NT - 1] = v[..., 0]
    d["z"] = np.where(sz > 0, 256, 8); d["x0"] = np.where(sx > 0, 256, 8)
    d["n0"] = atends(rng, d["n0"], M - 1, 0.8); d["n0"][:, 0] = 0; d["n0"][:, NT - 1] = M - 1
    d["nx"] = atends(rng, d["nx"], M - 1, 0.8); d["nx"][:, :, 0, 0] = 0; d["nx"][:, :, 2, M - 1] = M - 1
    d["nx"][:, 2, :, M - 1] = M - 1; d["nx"][:, 7, :, M - 1] = M - 1
    for g in range(8):
        d["hy"][:, g] = np.where(rng.random((N, KR, H)) < 0.78, (NT - 1) * rng.integers(0, 2, (N, KR, H)), rng.permutation(NT)[:60][rng.integers(0, 60, (N, KR, H))])
    d["u"] = atends(rng, rng.integers(0, 64, d["u"].shape), 63, 0.7)
    d["u"][:, 3] = 0; d["u"][:, 0] = 0; d["u"][N - 1, 0, :, KR - 1, H - 1] = 63; d["hy"][N - 1, 0, KR - 1, H - 1] = NT - 1
    quad(rng, d, 6, 3); hy, oc = deal(rng, NT); d["hy"][:, 6] = hy; d["u"][:, 6, 0] = np.array([0, 16, 32, 63])[oc % 4]
    return pack(d)
def setup_inputs_corners(rng):
    d = plain(rng); r = int(rng.integers(0, 8)); gs = [(r + i) % 8 for i in range(8)]
    for i in (0, 2, 4, 6): d["u"][:, gs[i]] = rng.integers(0, 64, (N, FR, KR, H))
    for i, s, one in ((1, NT, 0), (3, NT, 1), (5, NT - 1, 1)):
        g = gs[i]; quad(rng, d, g, 1); d["hy"][:, g] = deal(rng, s)[0]; d["u"][:, g] = 0
        if one: d["u"][N - 1, g, 0, KR - 1, H - 1] = 63
    g = gs[4]; quad(rng, d, g, 3); hy, oc = deal(rng, NT); d["hy"][:, g] = hy; d["u"][:, g, 0] = np.array([0, 16, 32, 63])[oc % 4]
    g = gs[6]; quad(rng, d, g, 1); hy, oc = deal(rng, NT // 2); d["hy"][:, g] = hy; d["u"][:, g, 0] = 63 * (oc % 2)
    d["z"][:, gs[7]] = far(rng, (FR, 16, M)); d["x0"][gs[7]] = np.minimum(d["x0"][gs[7]], 208)
    return pack(d)
def setup_inputs_crowd(rng):
    d = plain(rng); r = int(rng.integers(0, 8)); gs = [(r + i) % 8 for i in range(8)]
    for i in range(6): quad(rng, d, gs[i], 3)
    for i in range(7): d["u"][:, gs[i]] = rng.integers(0, 64, (N, FR, KR, H))
    a = rng.permutation(NT)
    d["hy"][:, gs[0]] = a[0]; d["u"][:, gs[0]] = 0
    d["hy"][:, gs[1]] = a[1]; d["hy"][N - 1, gs[1], KR - 1, H - 1] = a[2]; d["u"][:, gs[1], 0] = 0
    d["hy"][:, gs[2]] = NT - 1; d["u"][:, gs[2], 0] = 63
    d["hy"][:, gs[3]] = 0
    d["hy"][:, gs[4]] = (NT - 1) * rng.integers(0, 2, (N, KR, H))
    d["u"][:, gs[5], 0] = 0
    for q in range(N):
        f = rng.permutation(KR * H); d["hy"][q, gs[5]] = np.where(f < 256, a[3], np.where(f < 511, a[4], a[5])).reshape(KR, H)
    d["hy"][:, gs[6]] = a[6:9][rng.integers(0, 3, (N, KR, H))]
    return pack(d)
def setup_inputs_calm(rng):
    d = plain(rng); par = int(rng.integers(0, 2)); off = int(rng.integers(0, 4))
    for i in range(4):
        g = (2 * i + 1 + par) % 8; h = (g + 7) % 8; quad(rng, d, g, 1); d["hy"][:, g] = deal(rng, 64)[0]
        for t in range(FR):
            c = ((i + t + off) % 4) * 2 ** S + int(rng.integers(0, 2)) * (2 ** S - 1)
            d["u"][:, g, t] = np.where(rng.permutation(N * KR * H) < c, 0, 63).reshape(N, KR, H)
        d["u"][:, h] = np.where(rng.random((N, FR, KR, H)) < 0.5, rng.choice(np.array([8, 16, 24, 32]), (N, FR, KR, H)), rng.integers(0, 64, (N, FR, KR, H)))
    return pack(d)
def check_ranges(d):
    bad = []
    for k, lo, hi in (("nx", 0, M - 1), ("n0", 0, M - 1), ("hyp", 0, NT - 1), ("uu", 0, 63)):
        if np.min(d[k]) < lo or np.max(d[k]) > hi: bad.append("range of " + k)
    for k in ("z", "x0"):
        v = np.asarray(d[k], np.float64) * 32
        if not np.all((v >= 8) & (v <= 256) & (v == np.rint(v))): bad.append("range of " + k)
    for k in ("x0", "n0"):
        if np.any(np.asarray(d[k]) != np.asarray(d[k])[:1]): bad.append(k + " isn't alike on all ranks")
    return bad
def reference(z, nx, x0, n0, hyp, uu):
    zz = z.astype(np.float64).reshape(FR, PR, 8, 16, MS).transpose(0, 2, 3, 1, 4).reshape(FR, 8, 16, M)
    sx = nx.astype(np.int64).reshape(FR, PR, 8, 3, MS).transpose(0, 2, 3, 1, 4).reshape(FR, 8, 3, M)
    x = x0[0].astype(np.float64).reshape(8, 16, NT); n = n0[0].astype(np.int64)
    tr = np.stack([gentries(a) for a in hyp]).astype(np.int64).reshape(N, 8, KR, H)
    u = np.stack([gentries(a) for a in uu]).astype(np.int64).reshape(N, 8, FR, KR, H)
    live = np.ones((N, 8, KR, H), bool); w0 = np.full(8, 2, np.int64); gi = np.arange(8)[None, :, None]
    ye = np.zeros((N, 8, 16, H)); yx = np.zeros((N, 8, 16, H))
    for t in range(FR):
        nm = np.take_along_axis(sx[t], n[:, None, :], 2)
        zc = np.take_along_axis(zz[t], nm.reshape(8, 1, 3 * NT), 2).reshape(8, 16, 3, NT)
        dist = np.abs(zc - x[:, :, None, :])
        wt = np.maximum(np.add.reduce((dist <= 1).astype(np.int64), axis=1) - 4, 0)
        m = np.zeros((N, 8, KR, H), np.int64); took = np.full((N, 8, KR, H), -1, np.int64)
        for k in range(KR):
            T = tr[:, :, k]
            c = np.stack([nm[gi, i, T] for i in range(3)], axis=2); w = np.stack([wt[gi, i, T] for i in range(3)], axis=2)
            for j in range(k): w = np.where(c == took[:, :, j][:, :, None, :], 0, w)
            p = np.add.accumulate(np.concatenate([np.broadcast_to(w0[None, :, None, None], (N, 8, 1, H)), w], axis=2), axis=2)
            pick = np.argmax(64 * p > u[:, :, t, k][:, :, None, :] * p[:, :, 3:], axis=2)
            m[:, :, k] = pick
            name = np.take_along_axis(c, np.maximum(pick - 1, 0)[:, :, None, :], 2)[:, :, 0]
            took[:, :, k] = np.where(live[:, :, k] & (pick > 0), name, -1)
        pair = 4 * tr + m
        ex = np.exp(-np.concatenate([np.ones((8, 16, 1, NT)), dist], axis=2)).transpose(0, 1, 3, 2).reshape(8, 16, 4 * NT)
        for q in range(N):
            v = np.take_along_axis(ex, pair[q].reshape(8, 1, KR * H), 2).reshape(8, 16, KR, H)
            ye[q] = ye[q] + np.add.reduce(np.where(live[q][:, None], v, 0.0), axis=2)
        miss = np.add.reduce((live & (m == 0)).astype(np.int64), axis=(0, 2, 3))
        w0 = 1 + (np.roll(miss, -1) >> S)
        mark = np.zeros((8, 4 * NT), np.int64)
        for g in range(8): mark[g, pair[:, g][live[:, g]]] = 1
        place = np.add.accumulate(mark, axis=1) - mark
        xn = np.zeros((8, 16, NT)); nn = np.zeros((8, NT), np.int64)
        for g in range(8):
            o = np.nonzero(mark[g])[0][:NT]; T = o >> 2; hit = (o & 3) > 0; i = np.maximum((o & 3) - 1, 0); xo = x[g][:, T]
            xn[g][:, :len(o)] = np.where(hit, xo + 0.25 * (zc[g][:, i, T] - xo), xo)
            nn[g, :len(o)] = np.where(hit, nm[g, i, T], n[g, T])
        new = place[np.arange(8)[None, :, None, None], pair]
        live = live & (new < NT); tr = np.where(live, new, 0); x = xn; n = nn
    for q in range(N):
        v = np.take_along_axis(x, tr[q].reshape(8, 1, KR * H), 2).reshape(8, 16, KR, H)
        yx[q] = np.add.reduce(np.where(live[q][:, None], v, 0.0), axis=2)
    return {"ye": ye.reshape(N, 128, H).astype(np.float32), "yx": yx.reshape(N, 128, H).astype(np.float32)}

def check_inputs(d):
    bad = list(check_ranges(d))
    if not bad:
        for name, y in reference(**d).items():
            for q in range(N):
                v = np.abs(np.asarray(y[q], np.float64)); s = np.sqrt(np.mean(v * v))
                if v.max() > 7 * s or s < 2.0 ** -1: bad.append('%s of rank %d is uneven or too small' % (name, q))
    return bad

@@ -1,0 +1,744 @@
+import numpy as np
+from concourse.bass import DstId, RemoteDMATransfer
+from concourse.mybir import AluOpType, ActivationFunctionType
+
+ALU = AluOpType
+ACT = ActivationFunctionType
+F, B, I, U = "float32", "bfloat16", "int32", "uint16"
+PW = 272
+DW = 6176
+HZ = 688
+MAG = 1.5 * 2.0 ** 23
+NV = (2, 2, 2)
+YV = (True, False)
+PAYAT = (2, 4)
+LCAT = (50, 52)
+NS = 16
+
+SB = {
+    "z0": (4096, B), "z1": (4096, B), "z2": (4096, B),
+    "nxi": (512, I), "nxs": (1024, U), "nxo": (512, F), "nxf": (1024, F), "nxw": (4096, F),
+    "hu": (512, I), "n0w": (1024, I),
+    "D0": (DW, F), "D1": (DW, F), "ind": (6144, B), "OHh": (8192, B), "OHl": (8192, B),
+    "Y": (2048, F), "Y4": (2048, F), "G": (2048, F), "G2": (2048, F), "E": (2048, F),
+    "tab": (1024, F), "pay": (18 * PW, B),
+    "UU": (384, F), "C1": (384, F), "Dc": (256, F), "Vw": (384, F), "le0": (384, F), "le1": (384, F),
+    "N1": (128, F), "Tc": (128, F), "live": (128, F), "took": (128, F), "T1": (128, F),
+    "ta": (128, F), "tb": (128, F), "tc": (128, F), "td": (128, F), "te": (128, F), "I64": (128, B), "pairb": (128, F),
+    "dr": (4 * 320, F), "ne": (6 * 96, F), "W0": (32, F), "e8": (16, F), "th": (16, F),
+    "pick": (128, B), "dead": (128, B), "hi": (128, B), "tl4": (128, B), "lob": (128, B), "lo": (128, B),
+    "miss": (128, B), "mk": (256, B), "incl": (256, B), "X": (336, B), "rst": (256, B), "ib": (256, B), "cn": (256, B),
+    "lvx": (512, B), "Hf": (256, B),
+    "Ln": (128, U), "Ls0": (128, U), "Ls1": (128, U), "Li": (128, U), "LT": (128, U), "Lc": (384, U),
+    "Lp": (20, U), "Lw": (2, U), "Lth": (32, U), "Lx": (32, U),
+    "CI": (128, F), "S4i": (32, F), "Pti": (20, F), "PIi": (4, I), "PJ": (8, I), "PF": (24, F), "BM": (128, F),
+    "Ibf": (128, B), "If": (128, F), "I2k": (128, B), "I8k": (128, B), "I16": (128, B), "Dg": (128, B),
+    "Ones": (128, B), "Tri": (128, B), "B1": (8, B), "SC": (96, F), "Sd": (32, F), "Su": (32, F), "R12": (64, B),
+}
+SCRATCH = {k: ("sbuf", [128, v[0]], v[1]) for k, v in SB.items()}
+SB["nxv"] = (6, F)
+SCRATCH["nxd"] = ("dram", [6, 128, 512], F)
+for _i in range(8):
+    SCRATCH["ps%d" % _i] = ("psum", [128, 512], F)
+SEMAPHORES = (["cV", "cS", "cP", "cG", "lsem", "hin", "dz", "dnx", "dhu", "duu", "dn0", "dx0", "doe", "dox"]
+              + ["zarr%d" % t for t in range(3)] + ["narr%d" % t for t in range(3)]
+              + ["harr%d" % t for t in range(3)] + ["dw%d" % t for t in range(3)] + ["ga%d" % i for i in range(21)])
+
+
+def bits(es):
+    m = 0
+    for e in es:
+        m |= 1 << e
+    return m
+
+
+def helpers_of(T, topo, c):
+    return [h for h in topo.cores_of(c)
+            if T.rank_of(h) is None and all(topo.may_write(h, d) for d in T.cores if d != c)][:3]
+
+
+def dst(topo, c):
+    a = topo.addr(c)
+    return DstId(rid=a[0], pnc=a[1])
+
+
+def hand_masks(T, topo, c):
+    off = topo.engines(c, [d for d in T.cores if d != c][0])
+    rest = [e for e in topo.engines(c, helpers_of(T, topo, c)[0]) if e not in off]
+    h, q = len(rest) // 2, len(rest) // 4
+    return [rest[:h], rest[h:h + q], rest[h + q:]]
+
+
+PIECE = [(0, 0, 688), (680, 8, 688), (1360, 8, 688)]
+
+
+def helper_program(g, core, T, topo):
+    for q, c in enumerate(T.cores):
+        hs = helpers_of(T, topo, c)
+        if core in hs:
+            i = hs.index(core)
+            others = [d for d in T.cores if d != c]
+            es = topo.engines(core, others[0])
+            c0, a, b = PIECE[i]
+            col = 2048 * (q % 2) + c0
+            g.wait_ge(T.sem.hin, len(hand_masks(T, topo, c)[i]))
+            zt = T["z%d" % (q // 2)]
+            g.remote_dma_fused([RemoteDMATransfer(
+                dst_ids=[dst(topo, d) for d in others], dma_engine_mask=bits(es), remote_sem=T.sem["zarr%d" % (q // 2)],
+                srcs=[T.z0[:, a:b]], dsts=[zt[:, col + a:col + b] for _ in others])], local_sem=T.sem.lsem)
+            g.wait_ge(T.sem.lsem, len(es))
+
+
+def rank_program(g, core, T, topo):
+    rank = T.rank_of(core)
+    if rank is None:
+        helper_program(g, core, T, topo)
+        return
+    ops = []
+    Q = {"V": g.vector, "S": g.scalar, "P": g.tensor, "G": g, "Y": g.sync}
+
+    def R(n, a=0, b=None, s=1, p0=0, p1=128):
+        if b is None:
+            b = SB[n][0] if n in SB else 512
+        return (n, a, b, s, p0, p1, None)
+
+    def IND(n, a, b, o, oa, ob):
+        return (n, a, b, 1, 0, 128, (o, oa, ob))
+
+    def ap(x):
+        if not isinstance(x, tuple):
+            return x
+        v = T[x[0]][x[4]:x[5], x[1]:x[2]:x[3]] if x[3] != 1 else T[x[0]][x[4]:x[5], x[1]:x[2]]
+        if x[6] is not None:
+            v = v.indirect(T[x[6][0]][:, x[6][1]:x[6][2]])
+        return v
+
+    def op(e, fn, w, r, sem=None):
+        rr = []
+        for x in r:
+            if isinstance(x, tuple):
+                rr.append(x)
+                if x[6] is not None:
+                    rr.append(R(x[6][0], x[6][1], x[6][2]))
+        ops.append({"e": e, "fn": fn, "w": w, "r": rr, "sem": sem})
+
+    def arrive(sem, val, w):
+        ops.append({"e": None, "w": w, "sem": (sem, val)})
+
+    def ts(o, i, s1, o0, s2=None, o1=None):
+        if o1 is None:
+            op("V", lambda: g.vector.tensor_scalar(ap(o), ap(i), ap(s1), None, o0), [o], [i, s1])
+        else:
+            op("V", lambda: g.vector.tensor_scalar(ap(o), ap(i), ap(s1), ap(s2), o0, o1), [o], [i, s1, s2])
+
+    def tt(o, a, b, o0):
+        op("V", lambda: g.vector.tensor_tensor(ap(o), ap(a), ap(b), o0), [o], [a, b])
+
+    def cp(o, i):
+        op("V", lambda: g.vector.tensor_copy(ap(o), ap(i)), [o], [i])
+
+    def ms(o, v):
+        op("V", lambda: g.vector.memset(ap(o), v), [o], [])
+
+    def scan(o, d0, d1):
+        op("V", lambda: g.vector.tensor_tensor_scan(ap(o), ap(d0), ap(d1), 0.0, ALU.mult, ALU.add), [o], [d0, d1])
+
+    def act(o, i, f, bias=0.0, scale=1.0):
+        op("S", lambda: g.scalar.activation(ap(o), ap(i), f, bias=bias, scale=scale), [o], [i])
+
+    def mm(o, l, r, st=True, sp=True):
+        op("P", lambda: g.tensor.matmul(ap(o), ap(l), ap(r), st, sp), [o], [l, r])
+
+    def dma(e, o, i, sem, val, w, r):
+        op(e, lambda: Q[e].dma_start(o, i), w, r, sem=(sem, val))
+
+    nadd = [0]
+
+    def add(o, i):
+        nadd[0] += 1
+        op("G", lambda: g.dma_start(ap(o), ap(i), accum_op=ALU.add), [o], [o, i], sem=("ga%d" % (nadd[0] - 1), 16))
+
+    def iota(o, pat, cm):
+        if SB[o[0]][1] == I:
+            op("G", lambda: g.iota(ap(o), pat, 0, cm), [o], [])
+        else:
+            op("G", lambda: g.iota(ap(o), pat, 0, cm, allow_small_or_imprecise_dtypes=True), [o], [])
+
+    others = [d for d in T.cores if d != core]
+    off = topo.engines(core, others[0])
+    noff = len(off)
+    lsum = [0]
+
+    def send(src, sem, to=None):
+        lsum[0] += noff
+        op("G", lambda: g.remote_dma_fused([RemoteDMATransfer(
+            dst_ids=[dst(topo, d) for d in others], dma_engine_mask=bits(off), remote_sem=T.sem[sem],
+            srcs=[ap(src)], dsts=[ap(src) if to is None else to for _ in others])], local_sem=T.sem.lsem), [], [src], sem="remote")
+
+    myt, myb = rank // 2, rank % 2
+    zown = R("z%d" % myt, 2048 * myb, 2048 * myb + 2048)
+    col = lambda n, j: R(n, j, j + 1)
+    blk = lambda n, j, w=128: R(n, w * j, w * j + w)
+
+    dma("Y", ap(zown), T.z[:], "dz", 16, [zown], [])
+    dma("S", T.hu[:, 0:128], T.hyp[:], "dhu", 16, [R("hu", 0, 128)], [])
+    dma("S", T.E[:, 0:1024], T.x0[:], "dx0", 16, [R("E", 0, 1024)], [])
+    for gi in range(9):
+        e = "S" if gi % 2 == 0 else "Y"
+        if gi < 7:
+            o, i = T.nxi[16 * gi:16 * gi + 16, :], T.nx[3 * gi:3 * gi + 4, :]
+        elif gi == 7:
+            o, i = T.nxi[112:124, :], T.nx[21:24, :]
+        else:
+            o, i = T.nxi[124:128, :], T.nx[0:1, :]
+        dma(e, o, i, "dnx", 144, [R("nxi")] if gi == 8 else [], [])
+    ms(R("n0w"), 0)
+    dma("Y", T.n0w[0:128:16, :], T.n0[:], "dn0", 16, [R("n0w")], [])
+    dma("Y", T.hu[:, 128:512], T.uu[:], "duu", 16, [R("hu", 128, 512)], [])
+
+    iota(R("PIi", 0, 1), [[1, 1]], 1)
+    iota(R("CI"), [[1, 128]], 0)
+    iota(R("S4i"), [[4, 4], [16, 8]], 0)
+    ts(col("PJ", 0), col("PIi", 0), 15, ALU.bitwise_and)
+    ts(col("PJ", 1), col("PIi", 0), 4, ALU.arith_shift_right)
+    ts(col("PJ", 2), col("PIi", 0), 2, ALU.arith_shift_right, 3, ALU.bitwise_and)
+    ts(col("PJ", 3), col("PIi", 0), 3, ALU.bitwise_and)
+    ts(col("PJ", 4), col("PIi", 0), 2, ALU.arith_shift_right)
+    cp(col("PF", 0), col("PIi", 0))
+    cp(R("PF", 1, 6), R("PJ", 0, 5))
+    ts(R("If"), R("CI"), col("PF", 0), ALU.is_equal)
+    ts(R("SC", 0, 32), R("S4i"), col("PF", 0), ALU.is_equal)
+    ts(R("PF", 12, 16), R("CI", 0, 4), col("PF", 3), ALU.is_equal)
+    ts(col("PF", 7), col("PF", 2), 4.0, ALU.mult, col("PF", 4), ALU.add)
+    ms(R("live"), 1.0)
+    ts(R("Su"), R("CI", 0, 32), col("PF", 7), ALU.is_equal)
+
+    def nx_out():
+        cp(blk("nxs", rank, 512) if myt == 0 else R("nxo"), R("nxi"))
+
+    def sends():
+        hs = helpers_of(T, topo, core)
+        masks = hand_masks(T, topo, core)
+        lsum[0] += sum(len(m) for m in masks)
+        z = T["z%d" % myt]
+        if myt == 0:
+            send(blk("nxs", rank, 512), "narr0")
+        op("G", lambda: g.remote_dma_fused([RemoteDMATransfer(
+            dst_ids=[dst(topo, hs[i])], dma_engine_mask=bits(masks[i]), remote_sem=T.sem.hin,
+            srcs=[z[:, 2048 * myb + PIECE[i][0]:2048 * myb + PIECE[i][0] + HZ]], dsts=[T.z0[:, 0:HZ]]) for i in range(3)],
+            local_sem=T.sem.lsem), [], [zown], sem="remote")
+        if myt > 0:
+            send(R("nxo"), "narr%d" % myt, T.nxd[rank])
+
+    for t in range(3):
+        fz = [q for q in (2 * t, 2 * t + 1) if q != rank]
+        arrive("zarr%d" % t, 3 * noff * len(fz), [blk("z%d" % t, q % 2, 2048) for q in fz])
+        arrive("narr%d" % t, noff * len(fz), [blk("nxs", q, 512) if t == 0 else col("nxv", q) for q in fz])
+    if myt == 0:
+        nx_out()
+        sends()
+    iota(R("Pti", 4, 20), [[64, 4], [1, 4]], 0)
+    iota(R("BM"), [[0, 8], [1, 4], [0, 4]], 0)
+
+    for a in range(4):
+        ts(R("G2", a, 512, 4), R("hu", 0, 128), col("PF", 12 + a), ALU.mult)
+    for k in range(4):
+        mm(R("ps5", k, 128, 4), blk("G2", k), R("Su"))
+    for j in range(4):
+        act(blk("nxw", j, 1024), R("E", 0, 1024), ACT.Copy)
+    cp(R("Ibf"), R("If"))
+    ts(R("Tc"), R("ps5", 0, 128), 1.0, ALU.add)
+    mm(R("ps2", 0, 128), R("Tc"), R("If"))
+    ts(R("T1"), R("ps5", 0, 128), 4.0, ALU.mult, -30.0, ALU.add)
+    ms(R("Ones"), 1.0)
+    ms(R("W0"), 2.0)
+    ts(R("LT"), R("ps2", 0, 128), -1.0, ALU.add)
+    cp(R("G"), IND("n0w", 0, 1024, "LT", 0, 128))
+    for r in range(16):
+        mm(R("ps1", r, 128, 16), R("G", r, 2048, 16), R("SC", 0, 8))
+    for a in range(4):
+        ts(R("G2", 512 + a, 2048, 4), R("hu", 128, 512), col("PF", 12 + a), ALU.mult)
+    ts(R("N1"), R("ps1", 0, 128), 1.0, ALU.add)
+    mm(R("ps2", 0, 128), R("N1"), R("If"))
+    for kk in range(4, 16):
+        bl, k = kk // 4, kk % 4
+        mm(R("ps5", 128 * bl + k, 128 * bl + 128, 4), blk("G2", kk), R("Su"))
+
+    def nx_in(t):
+        if t == 0:
+            cp(R("nxf"), R("nxs"))
+        for b in range(2):
+            q = 2 * t + b
+            if t == 0:
+                i, r = T.nxf[:, 512 * b:512 * b + 512], R("nxf")
+            elif q == rank:
+                i, r = T.nxo[:, :], R("nxo")
+            else:
+                i, r = T.nxd[q], col("nxv", q)
+            dma("Y", T.nxw[t:128:4, 2048 * b:2048 * b + 2048], i, "dw%d" % t, 32, [blk("nxw", b, 2048)], [r])
+
+    ts(R("Ln"), R("ps2", 0, 128), -1.0, ALU.add)
+    act(R("Y"), IND("E", 0, 1024, "LT", 0, 128), ACT.Identity, scale=-1.0)
+    if myt > 0:
+        nx_out()
+        ts(zown, zown, (-4.0) ** myt, ALU.mult)
+    ts(R("UU"), R("ps5", 128, 512), 1.0 / 64, ALU.mult)
+
+    def prep(t):
+        ts(R("hi"), R("T1"), 64 * MAG, ALU.add, 64 * MAG, ALU.subtract)
+        f = [lambda j=j: ts(blk("OHh", j), R("hi"), 64.0 * j, ALU.is_equal) for j in range(64)]
+        f.insert(1, lambda: tt(R("tl4"), R("T1"), R("hi"), ALU.subtract))
+        return f
+
+    def place_list():
+        mm(R("ps2", 256, 384), R("hi"), R("I64"), True, False)
+        mm(R("ps2", 256, 384), R("tl4"), R("I16"), False, True)
+        ts(R("Li"), R("ps2", 256, 384), 480.0, ALU.add, 1023.0, ALU.min)
+
+    def masks():
+        return [lambda: ts(R("dead"), R("live"), -1.0, ALU.mult, 1.0, ALU.add),
+                lambda: ts(R("td"), R("live"), -64.0, ALU.mult, 94.0, ALU.add),
+                lambda: ts(R("te"), R("live"), -8192.0, ALU.mult, 8192.0, ALU.add)]
+
+    def succ_a(t, split):
+        if split:
+            act(R("G", 0, 1024), IND("nxw", 0, 4096, "Ln", 0, 64), ACT.Identity)
+            cp(R("G", 1024, 2048), IND("nxw", 0, 4096, "Ln", 64, 128))
+        else:
+            act(R("G"), IND("nxw", 0, 4096, "Ln", 0, 128), ACT.Identity)
+        for r in range(16):
+            mm(R("ps1", r, 384, 16), R("G", r, 2048, 16), R("SC", 32 * t, 32 * t + 24))
+
+    def succ_b():
+        act(R("C1"), R("ps1", 0, 384), ACT.Identity, bias=1.0)
+        for m in range(3):
+            mm(blk("ps3", m), blk("C1", m), R("If"))
+
+    def lists_c():
+        ts(R("Lc"), R("ps3", 0, 384), -1.0, ALU.add)
+
+    def chunk(t, ch, by_v):
+        d = R("D%d" % (t % 2), 16 + 1024 * ch, 16 + 1024 * ch + 1024)
+        w = IND("z%d" % t, 0, 4096, "Lc", 64 * ch, 64 * ch + 64)
+        if by_v:
+            tt(d, w, blk("Y", ch % 2, 1024), ALU.add)
+        else:
+            act(d, w, ACT.Identity)
+            add(d, blk("Y", ch % 2, 1024))
+
+    def gate(t, m):
+        big = 1.5 * 2.0 ** 24 * 4.0 ** t
+        for ch in (2 * m, 2 * m + 1):
+            if t == 0 and ch >= 3:
+                for _ in range(8):
+                    fill.pop(0)()
+            ts(blk("ind", ch, 1024), R("D%d" % (t % 2), 16 + 1024 * ch, 16 + 1024 * ch + 1024), big, ALU.add, big, ALU.is_equal)
+        for r in range(16):
+            mm(R("ps7", 128 * m + r, 128 * m + 128, 16), R("ind", 2048 * m + r, 2048 * m + 2048, 16), R("B1"))
+
+    def terms_a(t):
+        d = "D%d" % (t % 2)
+        act(R(d, 0, 16), R("Ones", 0, 16), ACT.Copy, scale=4.0 ** t)
+        act(R("E"), IND(d, 0, DW, "Ls%d" % (t % 2), 0, 128), ACT.Abs, scale=4.0 ** -t)
+        if t != 1:
+            act(R(d, 0, 16), R("Ones", 0, 16), ACT.Copy, scale=0.0)
+        if t < 2:
+            act(R("E"), R("E"), ACT.Exp, scale=-1.0)
+
+    def terms_b(t):
+        for k in range(4):
+            mm(R("ps0"), R("If"), R("E", k, 2048, 4), t == 0 and k == 0, t == 2 and k == 3)
+
+    halves = [(64 * gh, 64 * gh + 64) for gh in range(2)]
+
+    def bound(t):
+        for q in range(6):
+            b = (6 * t + q) * PW
+            mm(R("ps4", 0, 256), R("Ibf"), R("pay", b, b + 256), q == 0, q == 5)
+        ts(R("mk"), R("ps4", 0, 256), 1.0, ALU.min)
+        if t < 2:
+            for q in range(6):
+                b = (6 * t + q) * PW
+                mm(R("ps1", 16, 24), R("Ones"), R("pay", b + 256, b + 264), q == 0, q == 5)
+        scan(R("incl"), R("rst"), R("mk"))
+        for p0, p1 in halves:
+            mm(R("ps4", 384, 388, 1, p0, p1), R("Tri", p0, p1, 1, p0, p1), R("incl", 63, 256, 64, p0, p1))
+        if t < 2:
+            ts(R("e8", 0, 8), R("ps1", 16, 24), 1.0 / 2048, ALU.mult, 0.5 + 2.0 ** -12, ALU.add)
+        for gl in range(4):
+            ts(blk("ib", gl, 64), blk("incl", gl, 64), col("ps4", 384 + gl), ALU.add, 1024.0, ALU.is_le)
+        scan(R("cn"), R("rst"), R("ib"))
+        for gh, (p0, p1) in enumerate(halves):
+            mm(R("ps1", 4 * gh, 4 * gh + 4), blk("Hf", gh), R("cn", 63, 256, 64))
+        if t < 2:
+            cp(R("X", 0, 320), IND("incl", 0, 256, "Lp", 0, 20))
+            for tl in range(16):
+                for p0, p1 in halves:
+                    o = R("ps%d" % (5 + tl // 8), 64 * (tl % 8), 64 * (tl % 8) + 64, 1, p0, p1)
+                    mm(o, R("X", 64 + tl, 64 + tl + 253, 4, p0, p1), R("Ibf", p0, p1, 1, p0, p1), True, False)
+                    mm(o, R("X", 0, 64, 1, p0, p1), R("Tri", p0, p1, 1, p0, p1), False, True)
+        cp(R("th", 0, 8), R("ps1", 0, 8))
+        if t < 2:
+            ts(R("W0"), IND("e8", 0, 16, "Lw", 0, 2), MAG, ALU.add, MAG, ALU.subtract)
+            tt(R("live"), IND("th", 0, 16, "Lth", 0, 8), R("pairb"), ALU.is_gt)
+
+    def places_b():
+        act(R("tab", 0, 512), R("ps5"), ACT.Identity, bias=-34.0, scale=4.0)
+        act(R("tab", 512, 1024), R("ps6"), ACT.Identity, bias=-34.0, scale=4.0)
+        act(R("G2"), IND("tab", 0, 1024, "Li", 0, 128), ACT.Identity)
+        for r in range(16):
+            mm(R("ps3", r, 512, 16), R("G2", r, 2048, 16), R("Sd"))
+
+    def places_c(t):
+        for m in range(3):
+            tt(blk("dr", m), blk("ps3", m), blk("le%d" % (t % 2), m), ALU.mult)
+        tt(R("ta"), R("ps3", 384, 512), blk("dr", 0), ALU.add)
+        tt(R("tb"), blk("dr", 1), blk("dr", 2), ALU.add)
+        tt(R("T1"), R("ta"), R("tb"), ALU.add)
+
+    def draw(t, fill):
+        le = "le%d" % (t % 2)
+        sl = lambda n, m, k: R(n, 128 * m + k, 128 * m + 128, 4)
+        lazy = []
+
+        def gap(n):
+            done = 0
+            while lazy and done < n:
+                lazy.pop(0)()
+                done += 1
+            if not done and fill:
+                fill.pop(0)()
+
+        def ne(j, k, m):
+            b = 96 * (j * (7 - j) // 2 + k - j - 1) + 32 * m
+            tt(R("ne", b, b + 32), sl("C1", m, k), sl("took", 0, j), ALU.not_equal)
+
+        def mul(j, k, m):
+            b = 96 * (j * (7 - j) // 2 + k - j - 1) + 32 * m
+            tt(sl("Vw", m, k), sl("Vw", m, k), R("ne", b, b + 32), ALU.mult)
+
+        ts(R("Vw"), R("ps7", 0, 384), -4.0, ALU.add, 0.0, ALU.max)
+        if t > 0:
+            tt(blk("UU", t), blk("UU", t), R("live"), ALU.mult)
+        else:
+            gap(1)
+        for k in range(4):
+            d = lambda i: R("dr", 320 * k + 32 * i, 320 * k + 32 * i + 32)
+            n = 3 if k == 1 else 2
+            tt(d(0), R("W0"), sl("Vw", 0, k), ALU.add)
+            tt(d(1), sl("Vw", 1, k), sl("Vw", 2, k), ALU.add)
+            tt(d(2), d(0), sl("Vw", 1, k), ALU.add)
+            tt(d(3), d(0), d(1), ALU.add)
+            gap(n)
+            tt(d(4), d(3), sl("UU", t, k), ALU.mult)
+            gap(n)
+            tt(sl(le, 0, k), R("W0"), d(4), ALU.is_le)
+            tt(sl(le, 1, k), d(0), d(4), ALU.is_le)
+            tt(sl(le, 2, k), d(2), d(4), ALU.is_le)
+            if t == 2 and k == 3:
+                break
+            tt(d(5), sl(le, 0, k), sl("C1", 0, k), ALU.mult)
+            tt(d(6), sl(le, 1, k), sl("Dc", 0, k), ALU.mult)
+            tt(d(7), sl(le, 2, k), sl("Dc", 1, k), ALU.mult)
+            tt(d(8), d(5), d(6), ALU.add)
+            gap(n)
+            tt(sl("took", 0, k), d(8), d(7), ALU.add)
+            gap(99)
+            if k < 3:
+                for m in range(3):
+                    ne(k, k + 1, m)
+                for m in range(3):
+                    mul(k, k + 1, m)
+                for k2 in range(k + 2, 4):
+                    lazy += [lambda m=m, k2=k2, k=k: ne(k, k2, m) for m in range(3)]
+                for k2 in range(k + 2, 4):
+                    lazy += [lambda m=m, k2=k2, k=k: mul(k, k2, m) for m in range(3)]
+        while fill:
+            fill.pop(0)()
+
+    def marks_out(t):
+        b = (6 * t + rank) * PW
+        n = 264 if t < 2 else 256
+        act(R("pay", b, b + 256), R("ps4", 0, 256), ACT.Sign)
+        if t < 2:
+            act(R("pay", b + 256, b + 264), R("ps4", 256, 264), ACT.Copy)
+        send(R("pay", b, b + n), "harr%d" % t)
+        arrive("harr%d" % t, 5 * noff, [R("pay", (6 * t + q) * PW, (6 * t + q) * PW + n) for q in range(6) if q != rank])
+
+    def after_draw(t):
+        le, ls, dd = "le%d" % (t % 2), "Ls%d" % (t % 2), "D%d" % (t % 2)
+        if t < 2:
+            ts(R("ta"), R("took"), 0.0, ALU.is_equal)
+        tt(R("tb"), blk(le, 0), blk(le, 1), ALU.add)
+        if t < 2:
+            tt(R("tc"), R("ta"), R("N1"), ALU.mult)
+        tt(R("pick"), R("tb"), blk(le, 2), ALU.add)
+        if t < 2:
+            tt(R("N1"), R("tc"), R("took"), ALU.add)
+            mm(R("ps2", 0, 128), R("N1"), R("If"))
+        mm(R("ps2", 128, 256), R("pick"), R("I2k"), True, False)
+        mm(R("ps2", 128, 256), R("dead"), R("I8k"), False, False)
+        mm(R("ps2", 128, 256), R("Ones"), R("Dg"), False, True)
+        if t < 2:
+            tt(R("miss"), R("live"), blk(le, 0), ALU.is_gt)
+        else:
+            places_c(t - 1)
+        if t < 2:
+            ts(R("Ln"), R("ps2", 0, 128), -1.0, ALU.add)
+        ts(R(ls), R("ps2", 128, 256), col("PF", 6), ALU.add, float(DW - 16), ALU.min)
+        if t < 2:
+            for r in range(16):
+                mm(R("ps4", 256, 264), R("Ibf"), R("miss", r, 128, 16), r == 0, r == 15)
+            succ_a(t + 1, t == 0)
+            if not YV[t]:
+                act(blk("Y", 0, 1024), IND(dd, 0, DW, ls, 0, 64), ACT.Identity)
+                add(blk("Y", 0, 1024), blk("Y4", 0, 1024))
+            if t == 1:
+                places_c(0)
+            succ_b()
+            if not YV[t]:
+                act(blk("Y", 1, 1024), IND(dd, 0, DW, ls, 64, 128), ACT.Identity)
+                add(blk("Y", 1, 1024), blk("Y4", 1, 1024))
+        else:
+            terms_a(2)
+        f = prep(t) if t > 0 else []
+        lo = lambda: tt(R("lo"), R("lob"), R("tl4"), ALU.add)
+        f.insert(0, lambda: tt(R("lob"), R("pick"), R("td"), ALU.add))
+        f.insert(min(len(f), 4), lo)
+        ns = NS if t == 2 else 0
+        f += [lambda j=j: ts(blk("OHl", j), R("lo"), float(j), ALU.is_equal) for j in range(64 - ns)]
+        for i, fn in enumerate(f):
+            if t < 2 and i == LCAT[t]:
+                lists_c()
+            fn()
+            if fn is lo and ns:
+                for j in range(64 - ns, 64):
+                    act(blk("OHl", j), R("lo"), ACT.Abs, bias=-float(j))
+                act(R("OHl", 128 * (64 - ns), 8192), R("OHl", 128 * (64 - ns), 8192), ACT.Relu, bias=1.0, scale=-1.0)
+                act(R("E"), R("E"), ACT.Exp, scale=-1.0)
+        for c in range(128):
+            gh, gl = c // 64, c // 16 % 4
+            mm(R("ps4", 64 * gl, 64 * gl + 64, 1, 64 * gh, 64 * gh + 64), R("OHh", c, 8192, 128), R("OHl", c, 8192, 128),
+               c % 16 == 0, c % 16 == 15)
+        if t == 2 or YV[t]:
+            tt(R("Y"), IND(dd, 0, DW, ls, 0, 128), R("Y4"), ALU.add)
+        tt(R("ta"), R("te"), R("hi"), ALU.add)
+        tt(R("pairb"), R("ta"), R("lo"), ALU.add)
+
+    def gates(t):
+        sent = t == 0
+        for i, ch in enumerate(range(NV[t], 6)):
+            if not sent and i == PAYAT[t - 1]:
+                marks_out(t - 1)
+                sent = True
+            chunk(t, ch, False)
+        if not sent:
+            marks_out(t - 1)
+        for ch in range(NV[t]):
+            chunk(t, ch, True)
+        tt(R("Dc"), R("C1", 128, 384), R("C1", 0, 256), ALU.subtract)
+        if t > 0:
+            place_list()
+            terms_a(t - 1)
+        act(R("Y4"), R("Y"), ACT.Copy, scale=-4.0)
+        for m in range(3):
+            gate(t, m)
+
+    fill = prep(0)
+    nx_in(0)
+    for _ in range(28):
+        fill.pop(0)()
+    succ_a(0, True)
+    succ_b()
+    ts(col("PF", 16), col("PF", 0), 16.0, ALU.mult)
+    ts(col("PF", 6), col("PF", 1), -2032.0, ALU.add)
+    ts(col("PF", 17), col("PF", 1), -496.0, ALU.add)
+    ts(col("PF", 8), col("PF", 1), 4.0, ALU.mult)
+    ts(col("PF", 9), col("PF", 3), 1.0, ALU.add)
+    ts(col("PF", 10), col("PF", 0), -1.0, ALU.add)
+    ts(col("PF", 11), col("PF", 0), -2.0, ALU.add)
+    ts(col("PF", 22), col("PF", 4), 4.0, ALU.mult)
+    ts(R("B1"), R("CI", 0, 8), col("PF", 2), ALU.is_equal)
+    for d in ("D0", "D1"):
+        ms(R(d, 0, 16), 0.0)
+        ms(R(d, DW - 16, DW), 4000.0)
+
+    def later_sends():
+        op("G", None, [], [R("z%d" % (myt - 1))])
+        sends()
+
+    def late():
+        ts(R("I16"), R("If"), 16.0, ALU.mult)
+        ts(R("I64"), R("If"), 1.0 / 64, ALU.mult)
+        ms(R("rst"), 1.0)
+        for gh, (p0, p1) in enumerate(halves):
+            ms(R("Hf", 128 * gh, 128 * gh + 128, 1, p0, p1), 1.0)
+            ms(R("Hf", 128 - 128 * gh, 256 - 128 * gh, 1, p0, p1), 0.0)
+        ms(R("X", 320, 336), 0.0)
+        ms(R("e8"), 0.0)
+        ms(R("th"), 0.0)
+        ts(R("PF", 18, 22), R("CI", 0, 4), col("PF", 22), ALU.add)
+        ms(R("rst", 0, 256, 64), 0.0)
+        ts(R("I2k"), R("If"), 2048.0, ALU.mult)
+        ts(R("I8k"), R("If"), 8192.0, ALU.mult)
+        ts(R("Dg"), R("If"), col("PF", 16), ALU.mult)
+        ts(R("Tri"), R("CI"), col("PF", 0), ALU.is_gt)
+        ts(R("SC", 32, 64), R("S4i"), col("PF", 10), ALU.is_equal)
+        ts(R("SC", 64, 96), R("S4i"), col("PF", 11), ALU.is_equal)
+        tt(R("Sd", 0, 24), R("SC", 8, 32), R("SC", 0, 24), ALU.subtract)
+        cp(R("Sd", 24, 32), R("SC", 0, 8))
+        ts(R("Lp", 0, 4), R("CI", 0, 4), 64.0, ALU.mult, 63.0, ALU.add)
+        ts(R("Lp", 4, 20), R("Pti", 4, 20), col("PF", 8), ALU.add)
+        ts(R("ta", 0, 2), R("CI", 0, 2), 4.0, ALU.mult, col("PF", 9), ALU.add)
+        for k in range(4):
+            cp(blk("Lth", k, 8), R("CI", 0, 8))
+        ts(R("ta", 2, 4), R("ta", 0, 2), 8.0, ALU.is_lt)
+        for k in range(4):
+            ts(blk("Lx", k, 8), R("CI", 0, 8), 16.0, ALU.mult, col("PF", 18 + k), ALU.add)
+        tt(R("ta", 4, 6), R("ta", 0, 2), R("ta", 2, 4), ALU.mult)
+        ts(R("BM"), R("BM"), col("PF", 4), ALU.not_equal, 16384.0, ALU.mult)
+        ts(R("R12", 0, 32), R("CI", 0, 32), col("PF", 5), ALU.is_equal, 512.0, ALU.mult)
+        ts(R("R12", 32, 64), R("CI", 0, 32), col("PF", 5), ALU.is_equal, 1024.0, ALU.mult)
+        cp(R("Lw"), R("ta", 4, 6))
+
+    late()
+    fill += masks()
+    lists_c()
+    if myt == 1:
+        later_sends()
+    for t in range(3):
+        gates(t)
+        if t == 0 and myt == 2:
+            later_sends()
+        if t < 2:
+            nx_in(t + 1)
+        if t > 0:
+            bound(t - 1)
+            terms_b(t - 1)
+            places_b()
+            fill += masks()
+        draw(t, fill)
+        after_draw(t)
+
+    marks_out(2)
+    terms_b(2)
+    act(R("tab", 0, 512), R("ps0"), ACT.Copy)
+    dma("Y", T.ye[:], T.tab[:, 0:512], "doe", 16, [], [R("tab", 0, 512)])
+    for k in range(4):
+        tt(R("dr", 384 + 128 * k, 512 + 128 * k), IND("pairb", 0, 128, "Lx", 8 * k, 8 * k + 8), R("BM"), ALU.add)
+    for pr, n in enumerate(("G", "G2")):
+        ms(R(n, 0, 16), 0.0)
+        ts(R(n, 16, 528), R("Y", 2 * pr, 2048, 4), 1.0 / 64, ALU.mult)
+        ts(R(n, 528, 1040), R("Y", 2 * pr + 1, 2048, 4), 1.0 / 64, ALU.mult)
+        tt(R(n, 1040, 1552), R(n, 16, 528), R(n, 528, 1040), ALU.add)
+    bound(2)
+    tt(R("lvx"), IND("th", 0, 16, "Lth", 0, 32), R("dr", 384, 896), ALU.is_gt)
+    for pr in range(2):
+        o = R("ps2", 32 * pr, 32 * pr + 32)
+        mm(o, blk("lvx", 2 * pr), R("R12", 0, 32), True, False)
+        mm(o, blk("lvx", 2 * pr + 1), R("R12", 32, 64), False, False)
+        mm(o, R("Ones"), R("Dg", 0, 32), False, True)
+    ts(R("Ln", 0, 64), R("ps2", 0, 64), col("PF", 17), ALU.add)
+    for h in range(2):
+        act(blk("Y4", h, 256), IND("G", 0, 1552, "Ln", 16 * h, 16 * h + 16), ACT.Identity)
+    for h in range(2):
+        tt(blk("tab", 2 + h, 256), IND("G2", 0, 1552, "Ln", 32 + 16 * h, 48 + 16 * h), blk("Y4", h, 256), ALU.add)
+    dma("Y", T.yx[:], T.tab[:, 512:1024], "dox", 16, [], [R("tab", 512, 1024)])
+
+    emit(g, T, Q, ops, lsum[0])
+
+
+def emit(g, T, Q, ops, lsum):
+    toks = []
+    lw = {n: np.full(v[0], -1, np.int64) for n, v in SB.items()}
+    rd = {n: {} for n in SB}
+    bank = {}
+    clock = {e: {} for e in Q}
+    count = {e: 0 for e in Q}
+    need = {e: set() for e in Q}
+    finals = {}
+    for o in ops:
+        e = o["e"]
+        if e is None:
+            toks.append((o["sem"][0], o["sem"][1], {}))
+            finals[o["sem"][0]] = o["sem"][1]
+            for x in o["w"]:
+                lw[x[0]][x[1]:x[2]] = len(toks) - 1
+            continue
+        deps = set()
+        for x in o["r"] + o["w"]:
+            if x[0] not in SB:
+                for e2, tk in bank.get(x[0], {}).items():
+                    if e2 != e:
+                        deps.add(tk)
+            else:
+                deps.update(np.unique(lw[x[0]][x[1]:x[2]:x[3]]).tolist())
+        for x in o["w"]:
+            if x[0] in SB:
+                for arr in rd[x[0]].values():
+                    deps.update(np.unique(arr[x[1]:x[2]:x[3]]).tolist())
+        deps.discard(-1)
+        waits = {}
+        ck = clock[e]
+        for tk in sorted(deps, reverse=True):
+            key, val, c2 = toks[tk]
+            if o["sem"] is not None and o["sem"] != "remote" and key == o["sem"][0]:
+                continue
+            if ck.get(key, 0) >= val:
+                continue
+            waits[key] = max(waits.get(key, 0), val)
+            ck[key] = val
+            for k2, v2 in c2.items():
+                if ck.get(k2, 0) < v2:
+                    ck[k2] = v2
+        for key, val in waits.items():
+            if key in need:
+                need[key].add(val)
+        o["waits"] = waits
+        if o["fn"] is None or o["sem"] == "remote":
+            continue
+        if o["sem"] is None:
+            count[e] += 1
+            o["idx"] = count[e]
+            toks.append((e, count[e], dict(ck)))
+        else:
+            toks.append((o["sem"][0], o["sem"][1], dict(ck)))
+            finals[o["sem"][0]] = o["sem"][1]
+        tk = len(toks) - 1
+        rk = e if o["sem"] is None else o["sem"][0]
+        for x in o["r"]:
+            if x[0] in SB:
+                if rk not in rd[x[0]]:
+                    rd[x[0]][rk] = np.full(SB[x[0]][0], -1, np.int64)
+                rd[x[0]][rk][x[1]:x[2]:x[3]] = tk
+            else:
+                bank.setdefault(x[0], {})[e] = tk
+        for x in o["w"]:
+            if x[0] in SB:
+                lw[x[0]][x[1]:x[2]:x[3]] = tk
+            else:
+                bank.setdefault(x[0], {})[e] = tk
+    num = {e: {v: i + 1 for i, v in enumerate(sorted(need[e]))} for e in Q}
+    for o in ops:
+        e = o["e"]
+        if e is None:
+            continue
+        for key, val in o["waits"].items():
+            if key in num:
+                Q[e].wait_ge(T.sem["c" + key], num[key][val])
+            else:
+                Q[e].wait_ge(T.sem[key], val)
+        if o["fn"] is None:
+            continue
+        ins = o["fn"]()
+        if o["sem"] is None:
+            if o["idx"] in num[e]:
+                ins.then_inc(T.sem["c" + e], 1)
+        elif o["sem"] != "remote":
+            ins.then_inc(T.sem[o["sem"][0]], 16)
+    for key, val in finals.items():
+        g.wait_ge(T.sem[key], val)
+    for e in ("V", "S", "P", "G"):
+        if need[e]:
+            g.wait_ge(T.sem["c" + e], len(need[e]))
+    g.wait_ge(T.sem.lsem, lsum)

@@ -5,44 +5,50 @@ from concourse.mybir import AluOpType, ActivationFunctionType
 ALU = AluOpType
 ACT = ActivationFunctionType
 F, B, I, U = "float32", "bfloat16", "int32", "uint16"
-PW = 272
+PW = 264
 DW = 6176
 HZ = 688
 MAG = 1.5 * 2.0 ** 23
-NV = (2, 2, 2)
-YV = (True, False)
+DN = ("Db", "D1", "D0")
+NV = (3, 3, 2)
+YV = (False, False)
 PAYAT = (2, 4)
-LCAT = (50, 52)
+LCAT = (56, 70)
+SI = (False, True, True)
+XF = True
+NXAT = 3
+LATE = 42
+HV = 18
 NS = 16
 
 SB = {
     "z0": (4096, B), "z1": (4096, B), "z2": (4096, B),
-    "nxi": (512, I), "nxs": (1024, U), "nxo": (512, F), "nxf": (1024, F), "nxw": (4096, F),
+    "nxi": (512, I), "nxs": (1024, U), "nxo": (512, U), "nxf": (1024, F), "nxw": (4096, F),
     "hu": (512, I), "n0w": (1024, I),
     "D0": (DW, F), "D1": (DW, F), "ind": (6144, B), "OHh": (8192, B), "OHl": (8192, B),
-    "Y": (2048, F), "Y4": (2048, F), "G": (2048, F), "G2": (2048, F), "E": (2048, F),
+    "Y": (2048, F), "Y4": (2048, F), "G": (2048, F), "Db": (DW, B), "E": (2048, F),
     "tab": (1024, F), "pay": (18 * PW, B),
-    "UU": (384, F), "C1": (384, F), "Dc": (256, F), "Vw": (384, F), "le0": (384, F), "le1": (384, F),
-    "N1": (128, F), "Tc": (128, F), "live": (128, F), "took": (128, F), "T1": (128, F),
+    "UU": (384, F), "C1": (384, F), "Dc": (256, F), "Vw": (512, F), "le0": (384, F), "le1": (384, F),
+    "N1": (128, F), "live": (128, F), "took": (128, F), "T1": (128, F),
     "ta": (128, F), "tb": (128, F), "tc": (128, F), "td": (128, F), "te": (128, F), "I64": (128, B), "pairb": (128, F),
-    "dr": (4 * 320, F), "ne": (6 * 96, F), "W0": (32, F), "e8": (16, F), "th": (16, F),
+    "dr": (3 * 384, F), "ne": (6 * 96, F), "e8": (16, F), "th": (16, F),
     "pick": (128, B), "dead": (128, B), "hi": (128, B), "tl4": (128, B), "lob": (128, B), "lo": (128, B),
-    "miss": (128, B), "mk": (256, B), "incl": (256, B), "X": (336, B), "rst": (256, B), "ib": (256, B), "cn": (256, B),
-    "lvx": (512, B), "Hf": (256, B),
+    "miss": (128, B), "mk": (256, B), "incl": (256, B), "X": (336, B), "rst": (256, B), "ib": (256, B),
+    "Hf": (256, B),
     "Ln": (128, U), "Ls0": (128, U), "Ls1": (128, U), "Li": (128, U), "LT": (128, U), "Lc": (384, U),
-    "Lp": (20, U), "Lw": (2, U), "Lth": (32, U), "Lx": (32, U),
+    "Lp": (20, U), "Lw": (8, U), "rs4": (128, B), "Lth": (32, U), "Lx": (32, U),
     "CI": (128, F), "S4i": (32, F), "Pti": (20, F), "PIi": (4, I), "PJ": (8, I), "PF": (24, F), "BM": (128, F),
     "Ibf": (128, B), "If": (128, F), "I2k": (128, B), "I8k": (128, B), "I16": (128, B), "Dg": (128, B),
-    "Ones": (128, B), "Tri": (128, B), "B1": (8, B), "SC": (96, F), "Sd": (32, F), "Su": (32, F), "R12": (64, B),
+    "Ones": (128, B), "Tri": (128, B), "B1": (8, B), "Bh": (8, B), "SC": (96, F), "Sd": (32, F), "Su": (32, F), "R12": (64, B),
 }
 SCRATCH = {k: ("sbuf", [128, v[0]], v[1]) for k, v in SB.items()}
 SB["nxv"] = (6, F)
-SCRATCH["nxd"] = ("dram", [6, 128, 512], F)
+SCRATCH["nxd"] = ("dram", [6, 128, 512], U)
 for _i in range(8):
     SCRATCH["ps%d" % _i] = ("psum", [128, 512], F)
 SEMAPHORES = (["cV", "cS", "cP", "cG", "lsem", "hin", "dz", "dnx", "dhu", "duu", "dn0", "dx0", "doe", "dox"]
               + ["zarr%d" % t for t in range(3)] + ["narr%d" % t for t in range(3)]
-              + ["harr%d" % t for t in range(3)] + ["dw%d" % t for t in range(3)] + ["ga%d" % i for i in range(21)])
+              + ["harr%d" % t for t in range(3)] + ["dw%d" % t for t in range(3)] + ["earr0", "earr1", "dox2", "go", "dv1", "dv2"] + ["rl%d" % q for q in range(6)] + ["ga%d" % i for i in range(21)])
 
 
 def bits(es):
@@ -72,21 +78,56 @@ def hand_masks(T, topo, c):
 PIECE = [(0, 0, 688), (680, 8, 688), (1360, 8, 688)]
 
 
+def routes(T, topo, c):
+    near = lambda a, b: topo.mates(topo.chip(a), topo.chip(b)) or topo.same_plane(topo.chip(a), topo.chip(b))
+    via = {}
+    for d in T.cores:
+        if d != c and not near(c, d):
+            mid = [x for x in T.cores if x not in (c, d) and near(c, x) and near(x, d)]
+            mid = [x for x in mid if topo.mates(topo.chip(x), topo.chip(d))] + mid
+            if mid:
+                via[d] = mid[0]
+    return via
+
+
 def helper_program(g, core, T, topo):
+    mine = [c for c in T.cores if core in helpers_of(T, topo, c)]
+    if not mine:
+        return
+    me = mine[0]
+    i = helpers_of(T, topo, me).index(core)
+    c0, a, b = PIECE[i]
+    es = topo.engines(core, [d for d in T.cores if d != me][0])
+    rest = [e for e in topo.engines(core, me) if e not in es]
+    sent = 0
     for q, c in enumerate(T.cores):
-        hs = helpers_of(T, topo, c)
-        if core in hs:
-            i = hs.index(core)
-            others = [d for d in T.cores if d != c]
-            es = topo.engines(core, others[0])
-            c0, a, b = PIECE[i]
-            col = 2048 * (q % 2) + c0
+        via = routes(T, topo, c)
+        col = 2048 * (q % 2) + c0
+        home, arr = T["z%d" % (q // 2)][:, col + a:col + b], T.sem["zarr%d" % (q // 2)]
+        slot = T.ind[:, HZ * q + a:HZ * q + b]
+        if c == me:
             g.wait_ge(T.sem.hin, len(hand_masks(T, topo, c)[i]))
-            zt = T["z%d" % (q // 2)]
+            if q >= 2:
+                g.wait_ge(T.sem.go, 1)
+            relays = sorted(set(via.values()))
+            direct = [d for d in T.cores if d != c and d not in via and d not in relays]
             g.remote_dma_fused([RemoteDMATransfer(
-                dst_ids=[dst(topo, d) for d in others], dma_engine_mask=bits(es), remote_sem=T.sem["zarr%d" % (q // 2)],
-                srcs=[T.z0[:, a:b]], dsts=[zt[:, col + a:col + b] for _ in others])], local_sem=T.sem.lsem)
-            g.wait_ge(T.sem.lsem, len(es))
+                dst_ids=[dst(topo, helpers_of(T, topo, d)[i]) for d in relays], dma_engine_mask=bits(es),
+                remote_sem=T.sem["rl%d" % q], srcs=[T.z0[:, a:b]], dsts=[slot for _ in relays])], local_sem=T.sem.lsem)
+            g.remote_dma_fused([RemoteDMATransfer(
+                dst_ids=[dst(topo, d) for d in direct], dma_engine_mask=bits(es), remote_sem=arr,
+                srcs=[T.z0[:, a:b]], dsts=[home for _ in direct])], local_sem=T.sem.lsem)
+            sent += 2 * len(es)
+        elif me in via.values():
+            on = [d for d in via if via[d] == me]
+            g.wait_ge(T.sem["rl%d" % q], len(es))
+            g.remote_dma_fused([
+                RemoteDMATransfer(dst_ids=[dst(topo, d) for d in on], dma_engine_mask=bits(es), remote_sem=arr,
+                                  srcs=[slot], dsts=[home for _ in on]),
+                RemoteDMATransfer(dst_ids=[dst(topo, me)], dma_engine_mask=bits(rest), remote_sem=arr,
+                                  srcs=[slot], dsts=[home])], local_sem=T.sem.lsem)
+            sent += len(es) + len(rest)
+    g.wait_ge(T.sem.lsem, sent)
 
 
 def rank_program(g, core, T, topo):
@@ -214,7 +255,7 @@ def rank_program(g, core, T, topo):
     ts(R("Su"), R("CI", 0, 32), col("PF", 7), ALU.is_equal)
 
     def nx_out():
-        cp(blk("nxs", rank, 512) if myt == 0 else R("nxo"), R("nxi"))
+        cp(R("nxo"), R("nxi"))
 
     def sends():
         hs = helpers_of(T, topo, core)
@@ -222,13 +263,11 @@ def rank_program(g, core, T, topo):
         lsum[0] += sum(len(m) for m in masks)
         z = T["z%d" % myt]
         if myt == 0:
-            send(blk("nxs", rank, 512), "narr0")
+            send(R("nxo"), "narr0", ap(blk("nxs", rank, 512)))
         op("G", lambda: g.remote_dma_fused([RemoteDMATransfer(
             dst_ids=[dst(topo, hs[i])], dma_engine_mask=bits(masks[i]), remote_sem=T.sem.hin,
             srcs=[z[:, 2048 * myb + PIECE[i][0]:2048 * myb + PIECE[i][0] + HZ]], dsts=[T.z0[:, 0:HZ]]) for i in range(3)],
             local_sem=T.sem.lsem), [], [zown], sem="remote")
-        if myt > 0:
-            send(R("nxo"), "narr%d" % myt, T.nxd[rank])
 
     for t in range(3):
         fz = [q for q in (2 * t, 2 * t + 1) if q != rank]
@@ -236,52 +275,52 @@ def rank_program(g, core, T, topo):
         arrive("narr%d" % t, noff * len(fz), [blk("nxs", q, 512) if t == 0 else col("nxv", q) for q in fz])
     if myt == 0:
         nx_out()
-        sends()
+    sends()
     iota(R("Pti", 4, 20), [[64, 4], [1, 4]], 0)
     iota(R("BM"), [[0, 8], [1, 4], [0, 4]], 0)
 
     for a in range(4):
-        ts(R("G2", a, 512, 4), R("hu", 0, 128), col("PF", 12 + a), ALU.mult)
+        ts(R("D1", a, 512, 4), R("hu", 0, 128), col("PF", 12 + a), ALU.mult)
     for k in range(4):
-        mm(R("ps5", k, 128, 4), blk("G2", k), R("Su"))
+        mm(R("ps5", k, 128, 4), blk("D1", k), R("Su"))
     for j in range(4):
         act(blk("nxw", j, 1024), R("E", 0, 1024), ACT.Copy)
     cp(R("Ibf"), R("If"))
-    ts(R("Tc"), R("ps5", 0, 128), 1.0, ALU.add)
-    mm(R("ps2", 0, 128), R("Tc"), R("If"))
+    ts(R("took"), R("ps5", 0, 128), 1.0, ALU.add)
+    mm(R("ps2", 0, 128), R("took"), R("If"))
     ts(R("T1"), R("ps5", 0, 128), 4.0, ALU.mult, -30.0, ALU.add)
     ms(R("Ones"), 1.0)
-    ms(R("W0"), 2.0)
+    ms(R("Vw", 0, 512, 4), 2.0)
     ts(R("LT"), R("ps2", 0, 128), -1.0, ALU.add)
     cp(R("G"), IND("n0w", 0, 1024, "LT", 0, 128))
     for r in range(16):
         mm(R("ps1", r, 128, 16), R("G", r, 2048, 16), R("SC", 0, 8))
     for a in range(4):
-        ts(R("G2", 512 + a, 2048, 4), R("hu", 128, 512), col("PF", 12 + a), ALU.mult)
+        ts(R("D1", 512 + a, 2048, 4), R("hu", 128, 512), col("PF", 12 + a), ALU.mult)
     ts(R("N1"), R("ps1", 0, 128), 1.0, ALU.add)
     mm(R("ps2", 0, 128), R("N1"), R("If"))
     for kk in range(4, 16):
         bl, k = kk // 4, kk % 4
-        mm(R("ps5", 128 * bl + k, 128 * bl + 128, 4), blk("G2", kk), R("Su"))
+        mm(R("ps5", 128 * bl + k, 128 * bl + 128, 4), blk("D1", kk), R("Su"))
 
     def nx_in(t):
-        if t == 0:
-            cp(R("nxf"), R("nxs"))
+        for b in range(2):
+            cp(blk("nxf", b, 512), blk("nxs", b, 512))
+            dma("Y", T.nxw[t:128:4, 2048 * b:2048 * b + 2048], T.nxf[:, 512 * b:512 * b + 512], "dw%d" % t, 32,
+                [blk("nxw", b, 2048)], [blk("nxf", b, 512)])
+
+    def nx_stage(t):
         for b in range(2):
             q = 2 * t + b
-            if t == 0:
-                i, r = T.nxf[:, 512 * b:512 * b + 512], R("nxf")
-            elif q == rank:
-                i, r = T.nxo[:, :], R("nxo")
-            else:
-                i, r = T.nxd[q], col("nxv", q)
-            dma("Y", T.nxw[t:128:4, 2048 * b:2048 * b + 2048], i, "dw%d" % t, 32, [blk("nxw", b, 2048)], [r])
+            i, r = (T.nxo[:, :], R("nxo")) if q == rank else (T.nxd[q], col("nxv", q))
+            dma("Y", T.nxs[:, 512 * b:512 * b + 512], i, "dv%d" % t, 32, [blk("nxs", b, 512)], [r])
 
     ts(R("Ln"), R("ps2", 0, 128), -1.0, ALU.add)
     act(R("Y"), IND("E", 0, 1024, "LT", 0, 128), ACT.Identity, scale=-1.0)
     if myt > 0:
         nx_out()
-        ts(zown, zown, (-4.0) ** myt, ALU.mult)
+    else:
+        cp(blk("nxs", rank, 512), R("nxo"))
     ts(R("UU"), R("ps5", 128, 512), 1.0 / 64, ALU.mult)
 
     def prep(t):
@@ -318,7 +357,7 @@ def rank_program(g, core, T, topo):
         ts(R("Lc"), R("ps3", 0, 384), -1.0, ALU.add)
 
     def chunk(t, ch, by_v):
-        d = R("D%d" % (t % 2), 16 + 1024 * ch, 16 + 1024 * ch + 1024)
+        d = R(DN[t], 16 + 1024 * ch, 16 + 1024 * ch + 1024)
         w = IND("z%d" % t, 0, 4096, "Lc", 64 * ch, 64 * ch + 64)
         if by_v:
             tt(d, w, blk("Y", ch % 2, 1024), ALU.add)
@@ -327,20 +366,28 @@ def rank_program(g, core, T, topo):
             add(d, blk("Y", ch % 2, 1024))
 
     def gate(t, m):
-        big = 1.5 * 2.0 ** 24 * 4.0 ** t
+        big = 2 * MAG
+        wp = lambda m, r: R("ps7", 128 * (r % 4) + 4 * (r // 4) + m + 1, 128 * (r % 4) + 128, 16)
+        if m == 0 and SI[t]:
+            for ch in range(2):
+                act(blk("E", ch, 1024), R(DN[t], 16 + 1024 * ch, 16 + 1024 * ch + 1024), ACT.Abs)
+                act(blk("ind", ch, 1024), blk("E", ch, 1024), ACT.Sign, bias=1.0 + 2.0 ** -12, scale=-1.0)
+            return
+        if m == 3:
+            if SI[t]:
+                for r in range(16):
+                    mm(wp(0, r), R("ind", r, 2048, 16), R("Bh"))
+            return
         for ch in (2 * m, 2 * m + 1):
-            if t == 0 and ch >= 3:
-                for _ in range(8):
-                    fill.pop(0)()
-            ts(blk("ind", ch, 1024), R("D%d" % (t % 2), 16 + 1024 * ch, 16 + 1024 * ch + 1024), big, ALU.add, big, ALU.is_equal)
+            ts(blk("ind", ch, 1024), R(DN[t], 16 + 1024 * ch, 16 + 1024 * ch + 1024), big, ALU.add, big, ALU.is_equal)
         for r in range(16):
-            mm(R("ps7", 128 * m + r, 128 * m + 128, 16), R("ind", 2048 * m + r, 2048 * m + 2048, 16), R("B1"))
+            mm(wp(m, r), R("ind", 2048 * m + r, 2048 * m + 2048, 16), R("B1"))
 
     def terms_a(t):
-        d = "D%d" % (t % 2)
-        act(R(d, 0, 16), R("Ones", 0, 16), ACT.Copy, scale=4.0 ** t)
-        act(R("E"), IND(d, 0, DW, "Ls%d" % (t % 2), 0, 128), ACT.Abs, scale=4.0 ** -t)
-        if t != 1:
+        d = DN[t]
+        act(R(d, 0, 16), R("Ones", 0, 16), ACT.Copy)
+        act(R("E"), IND(d, 0, DW, "Ls%d" % (t % 2), 0, 128), ACT.Abs)
+        if t == 2:
             act(R(d, 0, 16), R("Ones", 0, 16), ACT.Copy, scale=0.0)
         if t < 2:
             act(R("E"), R("E"), ACT.Exp, scale=-1.0)
@@ -356,38 +403,51 @@ def rank_program(g, core, T, topo):
             b = (6 * t + q) * PW
             mm(R("ps4", 0, 256), R("Ibf"), R("pay", b, b + 256), q == 0, q == 5)
         ts(R("mk"), R("ps4", 0, 256), 1.0, ALU.min)
-        if t < 2:
-            for q in range(6):
-                b = (6 * t + q) * PW
-                mm(R("ps1", 16, 24), R("Ones"), R("pay", b + 256, b + 264), q == 0, q == 5)
         scan(R("incl"), R("rst"), R("mk"))
         for p0, p1 in halves:
             mm(R("ps4", 384, 388, 1, p0, p1), R("Tri", p0, p1, 1, p0, p1), R("incl", 63, 256, 64, p0, p1))
-        if t < 2:
-            ts(R("e8", 0, 8), R("ps1", 16, 24), 1.0 / 2048, ALU.mult, 0.5 + 2.0 ** -12, ALU.add)
-        for gl in range(4):
-            ts(blk("ib", gl, 64), blk("incl", gl, 64), col("ps4", 384 + gl), ALU.add, 1024.0, ALU.is_le)
-        scan(R("cn"), R("rst"), R("ib"))
-        for gh, (p0, p1) in enumerate(halves):
-            mm(R("ps1", 4 * gh, 4 * gh + 4), blk("Hf", gh), R("cn", 63, 256, 64))
-        if t < 2:
-            cp(R("X", 0, 320), IND("incl", 0, 256, "Lp", 0, 20))
-            for tl in range(16):
+
+        def table(tls):
+            for tl in tls:
                 for p0, p1 in halves:
                     o = R("ps%d" % (5 + tl // 8), 64 * (tl % 8), 64 * (tl % 8) + 64, 1, p0, p1)
                     mm(o, R("X", 64 + tl, 64 + tl + 253, 4, p0, p1), R("Ibf", p0, p1, 1, p0, p1), True, False)
                     mm(o, R("X", 0, 64, 1, p0, p1), R("Tri", p0, p1, 1, p0, p1), False, True)
+        n0 = 6 if XF else 0
+        if t < 2 and XF:
+            cp(R("X", 0, 320), IND("incl", 0, 256, "Lp", 0, 20))
+            table(range(n0))
+        for gl in range(4):
+            ts(blk("ib", gl, 64), blk("incl", gl, 64), col("ps4", 384 + gl), ALU.add, 1024.0, ALU.is_le)
+        scan(R("mk"), R("rst"), R("ib"))
+        for gh, (p0, p1) in enumerate(halves):
+            mm(R("ps1", 4 * gh, 4 * gh + 4), blk("Hf", gh), R("mk", 63, 256, 64))
+        if t < 2:
+            if not XF:
+                cp(R("X", 0, 320), IND("incl", 0, 256, "Lp", 0, 20))
+            table(range(n0, 16))
         cp(R("th", 0, 8), R("ps1", 0, 8))
         if t < 2:
-            ts(R("W0"), IND("e8", 0, 16, "Lw", 0, 2), MAG, ALU.add, MAG, ALU.subtract)
             tt(R("live"), IND("th", 0, 16, "Lth", 0, 8), R("pairb"), ALU.is_gt)
+
+    def misses_out(t):
+        b = (6 * t + rank) * PW + 256
+        act(R("pay", b, b + 8), R("ps4", 256, 264), ACT.Copy)
+        send(R("pay", b, b + 8), "earr%d" % t)
+        arrive("earr%d" % t, 5 * noff, [R("pay", (6 * t + q) * PW + 256, (6 * t + q) * PW + 264) for q in range(6) if q != rank])
+
+    def miss_weight(t):
+        for q in range(6):
+            b = (6 * t + q) * PW
+            mm(R("ps1", 16, 24), R("Ones"), R("pay", b + 256, b + 264), q == 0, q == 5)
+        ts(R("e8", 0, 8), R("ps1", 16, 24), 1.0 / 2048, ALU.mult, 0.5 + 2.0 ** -12, ALU.add)
 
     def places_b():
         act(R("tab", 0, 512), R("ps5"), ACT.Identity, bias=-34.0, scale=4.0)
         act(R("tab", 512, 1024), R("ps6"), ACT.Identity, bias=-34.0, scale=4.0)
-        act(R("G2"), IND("tab", 0, 1024, "Li", 0, 128), ACT.Identity)
+        act(R("G"), IND("tab", 0, 1024, "Li", 0, 128), ACT.Identity)
         for r in range(16):
-            mm(R("ps3", r, 512, 16), R("G2", r, 2048, 16), R("Sd"))
+            mm(R("ps3", r, 512, 16), R("G", r, 2048, 16), R("Sd"))
 
     def places_c(t):
         for m in range(3):
@@ -396,7 +456,7 @@ def rank_program(g, core, T, topo):
         tt(R("tb"), blk("dr", 1), blk("dr", 2), ALU.add)
         tt(R("T1"), R("ta"), R("tb"), ALU.add)
 
-    def draw(t, fill):
+    def draw(t, fill, between):
         le = "le%d" % (t % 2)
         sl = lambda n, m, k: R(n, 128 * m + k, 128 * m + 128, 4)
         lazy = []
@@ -409,64 +469,74 @@ def rank_program(g, core, T, topo):
             if not done and fill:
                 fill.pop(0)()
 
-        def ne(j, k, m):
+        def ne(j, k, m, x=None, y=None):
             b = 96 * (j * (7 - j) // 2 + k - j - 1) + 32 * m
-            tt(R("ne", b, b + 32), sl("C1", m, k), sl("took", 0, j), ALU.not_equal)
+            tt(R("ne", b, b + 32), x or sl("C1", m, k), y or sl("took", 0, j), ALU.not_equal)
 
         def mul(j, k, m):
             b = 96 * (j * (7 - j) // 2 + k - j - 1) + 32 * m
-            tt(sl("Vw", m, k), sl("Vw", m, k), R("ne", b, b + 32), ALU.mult)
+            v = R("Vw", 128 * k + m + 1, 128 * k + 128, 4)
+            tt(v, v, R("ne", b, b + 32), ALU.mult)
 
-        ts(R("Vw"), R("ps7", 0, 384), -4.0, ALU.add, 0.0, ALU.max)
         if t > 0:
-            tt(blk("UU", t), blk("UU", t), R("live"), ALU.mult)
-        else:
-            gap(1)
+            ts(R("Vw", 0, 512, 4), IND("e8", 0, 16, "Lw", 0, 8), MAG, ALU.add, MAG, ALU.subtract)
+        for m in range(3):
+            ts(R("Vw", m + 1, 512, 4), R("ps7", m + 1, 512, 4), 4.0 if SI[t] and m == 0 else -4.0, ALU.add, 0.0, ALU.max)
+        gap(1)
         for k in range(4):
-            d = lambda i: R("dr", 320 * k + 32 * i, 320 * k + 32 * i + 32)
-            n = 3 if k == 1 else 2
-            tt(d(0), R("W0"), sl("Vw", 0, k), ALU.add)
-            tt(d(1), sl("Vw", 1, k), sl("Vw", 2, k), ALU.add)
-            tt(d(2), d(0), sl("Vw", 1, k), ALU.add)
-            tt(d(3), d(0), d(1), ALU.add)
+            b0 = 384 * (k % 3)
+            d = lambda i: R("dr", b0 + 32 * i, b0 + 32 * i + 32)
+            pm = lambda m: R("dr", b0 + m, b0 + 128, 4)
+            n = 3 * k
+            scan(R("dr", b0, b0 + 128), R("rs4"), blk("Vw", k))
             gap(n)
-            tt(d(4), d(3), sl("UU", t, k), ALU.mult)
+            tt(d(4), pm(3), sl("UU", t, k), ALU.mult)
             gap(n)
-            tt(sl(le, 0, k), R("W0"), d(4), ALU.is_le)
-            tt(sl(le, 1, k), d(0), d(4), ALU.is_le)
-            tt(sl(le, 2, k), d(2), d(4), ALU.is_le)
+            for m in range(3):
+                tt(sl(le, m, k), pm(m), d(4), ALU.is_le)
             if t == 2 and k == 3:
                 break
             tt(d(5), sl(le, 0, k), sl("C1", 0, k), ALU.mult)
             tt(d(6), sl(le, 1, k), sl("Dc", 0, k), ALU.mult)
             tt(d(7), sl(le, 2, k), sl("Dc", 1, k), ALU.mult)
             tt(d(8), d(5), d(6), ALU.add)
-            gap(n)
-            tt(sl("took", 0, k), d(8), d(7), ALU.add)
-            gap(99)
-            if k < 3:
+            if k == 0 and t > 0:
+                tt(sl("took", 0, k), d(8), d(7), ALU.add)
+                between()
+                tt(sl("took", 0, 0), sl("took", 0, 0), sl("live", 0, 0), ALU.mult)
+                tt(blk("UU", t), blk("UU", t), R("live"), ALU.mult)
                 for m in range(3):
                     ne(k, k + 1, m)
                 for m in range(3):
                     mul(k, k + 1, m)
-                for k2 in range(k + 2, 4):
-                    lazy += [lambda m=m, k2=k2, k=k: ne(k, k2, m) for m in range(3)]
-                for k2 in range(k + 2, 4):
-                    lazy += [lambda m=m, k2=k2, k=k: mul(k, k2, m) for m in range(3)]
+                gap(1)
+            elif k < 3:
+                for m in range(3):
+                    tt(d(9 + m), sl("C1", m, k + 1), d(7), ALU.subtract)
+                for m in range(3):
+                    ne(k, k + 1, m, d(9 + m), d(8))
+                for m in range(3):
+                    mul(k, k + 1, m)
+                tt(sl("took", 0, k), d(8), d(7), ALU.add)
+            else:
+                gap(1)
+                tt(sl("took", 0, k), d(8), d(7), ALU.add)
+            for k2 in range(k + 2, 4):
+                lazy += [lambda m=m, k2=k2, k=k: ne(k, k2, m) for m in range(3)]
+                lazy += [lambda m=m, k2=k2, k=k: mul(k, k2, m) for m in range(3)]
+        assert not lazy
         while fill:
             fill.pop(0)()
 
     def marks_out(t):
         b = (6 * t + rank) * PW
-        n = 264 if t < 2 else 256
+        n = 256
         act(R("pay", b, b + 256), R("ps4", 0, 256), ACT.Sign)
-        if t < 2:
-            act(R("pay", b + 256, b + 264), R("ps4", 256, 264), ACT.Copy)
         send(R("pay", b, b + n), "harr%d" % t)
         arrive("harr%d" % t, 5 * noff, [R("pay", (6 * t + q) * PW, (6 * t + q) * PW + n) for q in range(6) if q != rank])
 
     def after_draw(t):
-        le, ls, dd = "le%d" % (t % 2), "Ls%d" % (t % 2), "D%d" % (t % 2)
+        le, ls, dd = "le%d" % (t % 2), "Ls%d" % (t % 2), DN[t]
         if t < 2:
             ts(R("ta"), R("took"), 0.0, ALU.is_equal)
         tt(R("tb"), blk(le, 0), blk(le, 1), ALU.add)
@@ -490,14 +560,15 @@ def rank_program(g, core, T, topo):
             for r in range(16):
                 mm(R("ps4", 256, 264), R("Ibf"), R("miss", r, 128, 16), r == 0, r == 15)
             succ_a(t + 1, t == 0)
+            misses_out(t)
             if not YV[t]:
-                act(blk("Y", 0, 1024), IND(dd, 0, DW, ls, 0, 64), ACT.Identity)
+                act(blk("Y4", 0, 1024), IND(dd, 0, DW, ls, 0, 64), ACT.Identity, scale=-0.25)
                 add(blk("Y", 0, 1024), blk("Y4", 0, 1024))
             if t == 1:
                 places_c(0)
             succ_b()
             if not YV[t]:
-                act(blk("Y", 1, 1024), IND(dd, 0, DW, ls, 64, 128), ACT.Identity)
+                act(blk("Y4", 1, 1024), IND(dd, 0, DW, ls, 64, 128), ACT.Identity, scale=-0.25)
                 add(blk("Y", 1, 1024), blk("Y4", 1, 1024))
         else:
             terms_a(2)
@@ -520,8 +591,8 @@ def rank_program(g, core, T, topo):
             gh, gl = c // 64, c // 16 % 4
             mm(R("ps4", 64 * gl, 64 * gl + 64, 1, 64 * gh, 64 * gh + 64), R("OHh", c, 8192, 128), R("OHl", c, 8192, 128),
                c % 16 == 0, c % 16 == 15)
-        if t == 2 or YV[t]:
-            tt(R("Y"), IND(dd, 0, DW, ls, 0, 128), R("Y4"), ALU.add)
+        if t == 2:
+            ts(R("Y4"), IND(dd, 0, DW, ls, 0, 128), 0.25, ALU.mult)
         tt(R("ta"), R("te"), R("hi"), ALU.add)
         tt(R("pairb"), R("ta"), R("lo"), ALU.add)
 
@@ -534,22 +605,21 @@ def rank_program(g, core, T, topo):
             chunk(t, ch, False)
         if not sent:
             marks_out(t - 1)
+        tt(R("Dc"), R("C1", 128, 384), R("C1", 0, 256), ALU.subtract)
         for ch in range(NV[t]):
             chunk(t, ch, True)
-        tt(R("Dc"), R("C1", 128, 384), R("C1", 0, 256), ALU.subtract)
         if t > 0:
             place_list()
-            terms_a(t - 1)
-        act(R("Y4"), R("Y"), ACT.Copy, scale=-4.0)
-        for m in range(3):
+            miss_weight(t - 1)
+        for m in (0, 1, 3, 2):
             gate(t, m)
+        if t > 0:
+            terms_a(t - 1)
 
     fill = prep(0)
     nx_in(0)
-    for _ in range(28):
+    for _ in range(HV):
         fill.pop(0)()
-    succ_a(0, True)
-    succ_b()
     ts(col("PF", 16), col("PF", 0), 16.0, ALU.mult)
     ts(col("PF", 6), col("PF", 1), -2032.0, ALU.add)
     ts(col("PF", 17), col("PF", 1), -496.0, ALU.add)
@@ -559,17 +629,27 @@ def rank_program(g, core, T, topo):
     ts(col("PF", 11), col("PF", 0), -2.0, ALU.add)
     ts(col("PF", 22), col("PF", 4), 4.0, ALU.mult)
     ts(R("B1"), R("CI", 0, 8), col("PF", 2), ALU.is_equal)
-    for d in ("D0", "D1"):
+    for d in DN:
         ms(R(d, 0, 16), 0.0)
         ms(R(d, DW - 16, DW), 4000.0)
+    succ_a(0, True)
+    succ_b()
 
     def later_sends():
         op("G", None, [], [R("z%d" % (myt - 1))])
-        sends()
+        hs, one = helpers_of(T, topo, core), hand_masks(T, topo, core)
+        lsum[0] += 3
+        op("G", lambda: g.remote_dma_fused([RemoteDMATransfer(
+            dst_ids=[dst(topo, hs[i])], dma_engine_mask=bits(one[i][:1]), remote_sem=T.sem.go) for i in range(3)],
+            local_sem=T.sem.lsem), [], [], sem="remote")
+        send(R("nxo"), "narr%d" % myt, T.nxd[rank])
 
     def late():
+        ms(R("rs4"), 1.0)
         ts(R("I16"), R("If"), 16.0, ALU.mult)
+        ms(R("rs4", 0, 128, 4), 0.0)
         ts(R("I64"), R("If"), 1.0 / 64, ALU.mult)
+        ts(R("Bh"), R("B1"), 0.5, ALU.mult)
         ms(R("rst"), 1.0)
         for gh, (p0, p1) in enumerate(halves):
             ms(R("Hf", 128 * gh, 128 * gh + 128, 1, p0, p1), 1.0)
@@ -599,25 +679,39 @@ def rank_program(g, core, T, topo):
         ts(R("BM"), R("BM"), col("PF", 4), ALU.not_equal, 16384.0, ALU.mult)
         ts(R("R12", 0, 32), R("CI", 0, 32), col("PF", 5), ALU.is_equal, 512.0, ALU.mult)
         ts(R("R12", 32, 64), R("CI", 0, 32), col("PF", 5), ALU.is_equal, 1024.0, ALU.mult)
-        cp(R("Lw"), R("ta", 4, 6))
+        for k in range(4):
+            cp(blk("Lw", k, 2), R("ta", 4, 6))
 
+    n0 = len(ops)
     late()
-    fill += masks()
+    rest = ops[n0 + LATE:]
+    del ops[n0 + LATE:]
+    j0 = 64 - len(fill)
+    fill = masks() + [lambda o=o: ops.append(o) for o in rest]
     lists_c()
     if myt == 1:
         later_sends()
     for t in range(3):
         gates(t)
+        if t == 0:
+            for j in range(j0, 64):
+                act(blk("OHh", j), R("hi"), ACT.Abs, bias=-float(j), scale=1.0 / 64)
+            act(R("OHh", 128 * j0, 8192), R("OHh", 128 * j0, 8192), ACT.Relu, bias=1.0, scale=-1.0)
         if t == 0 and myt == 2:
             later_sends()
         if t < 2:
-            nx_in(t + 1)
-        if t > 0:
+            nx_stage(t + 1)
+        if t == 0:
+            fill.insert(NXAT, lambda: nx_in(1))
+
+        def between():
+            if t == 1:
+                nx_in(2)
             bound(t - 1)
             terms_b(t - 1)
             places_b()
-            fill += masks()
-        draw(t, fill)
+            fill.extend(masks())
+        draw(t, fill, between)
         after_draw(t)
 
     marks_out(2)
@@ -626,24 +720,25 @@ def rank_program(g, core, T, topo):
     dma("Y", T.ye[:], T.tab[:, 0:512], "doe", 16, [], [R("tab", 0, 512)])
     for k in range(4):
         tt(R("dr", 384 + 128 * k, 512 + 128 * k), IND("pairb", 0, 128, "Lx", 8 * k, 8 * k + 8), R("BM"), ALU.add)
-    for pr, n in enumerate(("G", "G2")):
+    for pr, n in enumerate(("G", "D1")):
         ms(R(n, 0, 16), 0.0)
-        ts(R(n, 16, 528), R("Y", 2 * pr, 2048, 4), 1.0 / 64, ALU.mult)
-        ts(R(n, 528, 1040), R("Y", 2 * pr + 1, 2048, 4), 1.0 / 64, ALU.mult)
+        tt(R(n, 16, 528), R("Y4", 2 * pr, 2048, 4), R("Y", 2 * pr, 2048, 4), ALU.subtract)
+        tt(R(n, 528, 1040), R("Y4", 2 * pr + 1, 2048, 4), R("Y", 2 * pr + 1, 2048, 4), ALU.subtract)
         tt(R(n, 1040, 1552), R(n, 16, 528), R(n, 528, 1040), ALU.add)
     bound(2)
-    tt(R("lvx"), IND("th", 0, 16, "Lth", 0, 32), R("dr", 384, 896), ALU.is_gt)
+    tt(R("OHh", 0, 512), IND("th", 0, 16, "Lth", 0, 32), R("dr", 384, 896), ALU.is_gt)
     for pr in range(2):
         o = R("ps2", 32 * pr, 32 * pr + 32)
-        mm(o, blk("lvx", 2 * pr), R("R12", 0, 32), True, False)
-        mm(o, blk("lvx", 2 * pr + 1), R("R12", 32, 64), False, False)
+        mm(o, blk("OHh", 2 * pr), R("R12", 0, 32), True, False)
+        mm(o, blk("OHh", 2 * pr + 1), R("R12", 32, 64), False, False)
         mm(o, R("Ones"), R("Dg", 0, 32), False, True)
     ts(R("Ln", 0, 64), R("ps2", 0, 64), col("PF", 17), ALU.add)
     for h in range(2):
         act(blk("Y4", h, 256), IND("G", 0, 1552, "Ln", 16 * h, 16 * h + 16), ACT.Identity)
     for h in range(2):
-        tt(blk("tab", 2 + h, 256), IND("G2", 0, 1552, "Ln", 32 + 16 * h, 48 + 16 * h), blk("Y4", h, 256), ALU.add)
-    dma("Y", T.yx[:], T.tab[:, 512:1024], "dox", 16, [], [R("tab", 512, 1024)])
+        tt(blk("tab", 2 + h, 256), IND("D1", 0, 1552, "Ln", 32 + 16 * h, 48 + 16 * h), blk("Y4", h, 256), ALU.add)
+        dma("YS"[h], T.yx[:, 256 * h:256 * h + 256], T.tab[:, 512 + 256 * h:768 + 256 * h], ("dox", "dox2")[h], 16, [],
+            [blk("tab", 2 + h, 256)])
 
     emit(g, T, Q, ops, lsum[0])
 

@@ -1,3 +1,4 @@
+import math
 import numpy as np
 from concourse.bass import DstId, RemoteDMATransfer
 from concourse.mybir import AluOpType, ActivationFunctionType
@@ -9,46 +10,81 @@ PW = 264
 DW = 6176
 HZ = 688
 MAG = 1.5 * 2.0 ** 23
-DN = ("Db", "D1", "D0")
-NV = (3, 3, 2)
-YV = (False, False)
-PAYAT = (2, 4)
-LCAT = (56, 70)
+DN = ("Db", "D1", "D1")
+NV = (3, 3, 3)
+PAYAT = (2, 3)
+LCAT = (32, 80)
 SI = (False, True, True)
-XF = True
-NXAT = 3
-LATE = 42
-HV = 18
-NS = 16
+XF = 0
+WL = (32, 64, 32)
+MKS = False
+VWS = False
+SUB = True
+Y4A = ((0, 128), (0, 24))
+CORES_IN_ALL = 128
+XR = True
+WHOLE = (False, True, True)
+DIR = True
+HZ1 = (2, 0, 0)
+XS = True
+MWAT = 2
+VW0 = (2, 2, 2)
+TB1 = 6
+TB0 = 0
+PLM = True
+DB = (1, 1, 0)
+NXE = False
+GA = 0
+MH = True
+TWO = False
+ORD = (0, 1, 2)
+GON = "G"
+OWN = False
+NXD = True
+ZA = (640, 768, 768)
+LATE = 70
+SPL = (0, 128)
+HU = 24
+HV = 12
+HX = 24
+HW = 0
+PF1 = (True, False, True)
+PLK = (0, 0, 0)
+UK = True
+NS0 = (8, 0)
+NS = (32, 0, 10)
 
 SB = {
     "z0": (4096, B), "z1": (4096, B), "z2": (4096, B),
-    "nxi": (512, I), "nxs": (1024, U), "nxo": (512, U), "nxf": (1024, F), "nxw": (4096, F),
-    "hu": (512, I), "n0w": (1024, I),
-    "D0": (DW, F), "D1": (DW, F), "ind": (6144, B), "OHh": (8192, B), "OHl": (8192, B),
+    "nxi": (512, I), "nxs": (1024, U), "nxp": (1024, B), "nxf": (1024, F), "nxw": (4096, F), "nxb": (4096, B), "Gb": (2048, B),
+    "SCb": (24, B),
+    "hu": (512, I), "n0l": (64, I),
+    "D1": (DW, F), "ind": (6144, B), "OHh": (16384, B), "OHl": (4096, B),
     "Y": (2048, F), "Y4": (2048, F), "G": (2048, F), "Db": (DW, B), "E": (2048, F),
     "tab": (1024, F), "pay": (18 * PW, B),
-    "UU": (384, F), "C1": (384, F), "Dc": (256, F), "Vw": (512, F), "le0": (384, F), "le1": (384, F),
-    "N1": (128, F), "live": (128, F), "took": (128, F), "T1": (128, F),
-    "ta": (128, F), "tb": (128, F), "tc": (128, F), "td": (128, F), "te": (128, F), "I64": (128, B), "pairb": (128, F),
+    "U5": (1920, B), "C1": (384, F), "Dc": (256, F), "Vw": (640, B), "Pm": (640, F), "le0": (384, B), "le1": (384, B),
+    "N1": (128, F), "live": (128, B), "took": (128, F), "T1": (128, F),
+    "ta": (128, F), "tc": (128, F), "td": (128, B), "pairb": (128, F), "tabb": (1024, B),
     "dr": (3 * 384, F), "ne": (6 * 96, F), "e8": (16, F), "th": (16, F),
-    "pick": (128, B), "dead": (128, B), "hi": (128, B), "tl4": (128, B), "lob": (128, B), "lo": (128, B),
-    "miss": (128, B), "mk": (256, B), "incl": (256, B), "X": (336, B), "rst": (256, B), "ib": (256, B),
-    "Hf": (256, B),
+    "pd": (160, F), "pb": (384, B), "hi": (128, B), "lo": (128, B),
+    "miss": (384, B), "mk": (256, B), "incl": (288, B), "X": (528, B), "rst32": (256, B), "rst64": (256, B), "ib": (256, B),
+    "C32": (128, B), "mc": (32, F), "Lm": (32, U), "Hf": (256, B),
     "Ln": (128, U), "Ls0": (128, U), "Ls1": (128, U), "Li": (128, U), "LT": (128, U), "Lc": (384, U),
-    "Lp": (20, U), "Lw": (8, U), "rs4": (128, B), "Lth": (32, U), "Lx": (32, U),
-    "CI": (128, F), "S4i": (32, F), "Pti": (20, F), "PIi": (4, I), "PJ": (8, I), "PF": (24, F), "BM": (128, F),
-    "Ibf": (128, B), "If": (128, F), "I2k": (128, B), "I8k": (128, B), "I16": (128, B), "Dg": (128, B),
-    "Ones": (128, B), "Tri": (128, B), "B1": (8, B), "Bh": (8, B), "SC": (96, F), "Sd": (32, F), "Su": (32, F), "R12": (64, B),
+    "Lp32": (32, U), "Lp64": (32, U), "Lw": (8, U), "Lth": (32, U), "Lx": (32, U),
+    "CI": (128, F), "S4i": (32, F), "Pti": (152, F), "PIi": (4, I), "PJ": (8, I), "PF": (28, F), "BM": (128, F),
+    "Ibf": (128, B), "If": (128, F), "I2k": (128, B), "I32": (384, B), "I64": (384, B), "Dg": (128, B),
+    "Ones": (128, B), "Tri": (128, B), "B1": (8, B), "Bh": (8, B), "SC": (32, F), "Sd": (32, B), "Su": (32, F), "R12": (64, B),
 }
 SCRATCH = {k: ("sbuf", [128, v[0]], v[1]) for k, v in SB.items()}
 SB["nxv"] = (6, F)
-SCRATCH["nxd"] = ("dram", [6, 128, 512], U)
+SCRATCH["nxd"] = ("dram", [6, 2, 128, 512], B)
+SCRATCH["nxe"] = ("dram", [6, 128, 1024], B)
 for _i in range(8):
     SCRATCH["ps%d" % _i] = ("psum", [128, 512], F)
-SEMAPHORES = (["cV", "cS", "cP", "cG", "lsem", "hin", "dz", "dnx", "dhu", "duu", "dn0", "dx0", "doe", "dox"]
+SEMAPHORES = (["cV", "cS", "cP", "cG", "lsem", "dz", "dnx", "dhu", "duu", "dn0", "dx0", "doe", "dox"]
               + ["zarr%d" % t for t in range(3)] + ["narr%d" % t for t in range(3)]
-              + ["harr%d" % t for t in range(3)] + ["dw%d" % t for t in range(3)] + ["earr0", "earr1", "dox2", "go", "dv1", "dv2"] + ["rl%d" % q for q in range(6)] + ["ga%d" % i for i in range(21)])
+              + ["harr%d" % t for t in range(3)] + ["dw%d" % t for t in range(3)] + ["earr0", "earr1", "dox2", "go", "hm0", "hm1"] + ["h" + n for n in ("n", "z0", "z1", "z2")]
+              + ["r%s_%d_%d" % (n, q, j) for n in ("n", "z0", "z1", "z2") for q in range(6) for j in range(2)] + ["ga%d" % i for i in range(21)])
 
 
 def bits(es):
@@ -59,8 +95,9 @@ def bits(es):
 
 
 def helpers_of(T, topo, c):
-    return [h for h in topo.cores_of(c)
-            if T.rank_of(h) is None and all(topo.may_write(h, d) for d in T.cores if d != c)][:3]
+    hs = [h for h in topo.cores_of(c) if h != c and T.rank_of(h) is None and all(topo.may_write(h, d) for d in T.cores if d != c)]
+    far = [h for h in hs if topo.die(h) != topo.die(c)]
+    return [far[0], [h for h in hs if h not in far][0], far[1]]
 
 
 def dst(topo, c):
@@ -68,66 +105,140 @@ def dst(topo, c):
     return DstId(rid=a[0], pnc=a[1])
 
 
-def hand_masks(T, topo, c):
-    off = topo.engines(c, [d for d in T.cores if d != c][0])
-    rest = [e for e in topo.engines(c, helpers_of(T, topo, c)[0]) if e not in off]
-    h, q = len(rest) // 2, len(rest) // 4
-    return [rest[:h], rest[h:h + q], rest[h + q:]]
+PIECE = [[(0, a), (a, 2 * a), (2 * a, 2048)] for a in ZA]
 
 
-PIECE = [(0, 0, 688), (680, 8, 688), (1360, 8, 688)]
+def spread(T, topo, c):
+    mate = lambda a, b: topo.mates(topo.chip(a), topo.chip(b))
+    plane = [x for x in T.cores if topo.same_plane(topo.chip(x), topo.chip(c))]
+    mates = [x for x in T.cores if mate(x, c)]
+    far = [x for x in T.cores if x != c and x not in plane + mates]
+    lone = [f for f in far if not any(mate(f, p) for p in plane)]
+    if WHOLE[T.rank_of(c) // 2]:
+        way = {p: {2: [f for f in far if mate(f, p)]} for p in plane}
+        way.update({twin(T, topo, f): {2: [f]} for f in lone})
+        way.update({x: {2: []} for x in mates})
+        return dict(sorted(way.items(), key=lambda x: not x[1][2]))
+    else:
+        way = {p: {j: [x for x in plane if x != p] + sorted((f for f in far if f not in lone), key=lambda f: mate(f, p))}
+               for j, p in enumerate(plane)}
+    if XR:
+        for x in mates:
+            way[x] = {j: [] for j in range(2)}
+        for f in lone:
+            way[twin(T, topo, f)] = {j: [f] for j in range(2)}
+        return way
+    for x in mates or lone:
+        way[x] = {j: lone if mates else [] for j in range(len(plane))}
+    return way
 
 
-def routes(T, topo, c):
-    near = lambda a, b: topo.mates(topo.chip(a), topo.chip(b)) or topo.same_plane(topo.chip(a), topo.chip(b))
-    via = {}
-    for d in T.cores:
-        if d != c and not near(c, d):
-            mid = [x for x in T.cores if x not in (c, d) and near(c, x) and near(x, d)]
-            mid = [x for x in mid if topo.mates(topo.chip(x), topo.chip(d))] + mid
-            if mid:
-                via[d] = mid[0]
-    return via
+def twin(T, topo, c):
+    for k in range(CORES_IN_ALL):
+        if topo.mates(topo.chip(k), topo.chip(c)):
+            return topo.cores_of(k)[topo.cores_of(c).index(c)]
+
+
+def loads_of(T, q):
+    t, out = q // 2, []
+    part = lambda x, a, w: lambda j: x[:, a + w * (j % 2):a + w * (j % 2) + w * (1 + j // 2)]
+    if t == 0:
+        half = part(T.nxs, 512 * q, 256)
+        out.append((1, "n", half, half, half, "narr0"))
+    else:
+        out.append((DB[t], "n", part(T.nxp, 0, 512), part(T.nxb, 1024 * (q - 2), 512),
+                    lambda j: T.nxd[q, j] if j < 2 else T.nxe[q], "narr%d" % t))
+    for i, (a, b) in enumerate(PIECE[t]):
+        w = (b - a) // 2
+        home = part(T["z%d" % t], 2048 * (q % 2) + a, w)
+        out.append(((0, HZ1[t], DB[t])[i], "z%d" % i, home, part(T.OHh, 2048 * q + a, w), home, "zarr%d" % t))
+    return out
+
+
+def first_frame(T, q, step, die):
+    if step == 0:
+        return "rn_%d_0" % q, T.nxs[:, 512 * q + 256 * die:512 * q + 256 * die + 256], "narr0"
+    a = 2048 * q + 1024 * (step - 1) + 512 * die
+    return "rz%d_%d_0" % (step - 1, q), T.z0[:, a:a + 512], "zarr0"
+
+
+def first_step(g, T, topo, core, c, load):
+    die, name, src, mid, home, arr = load
+    way = spread(T, topo, c)
+    es = topo.engines(core, [d for d in T.cores if d != c][0])
+    h = len(es) // 2
+    to = lambda j: [x for x in way if j in way[x]]
+    g.remote_dma_fused([RemoteDMATransfer(
+        dst_ids=[dst(topo, helpers_of(T, topo, x)[die]) for x in to(j)], dma_engine_mask=bits(es[h * j:h * j + h] if j < 2 else es),
+        remote_sem=T.sem["r%s_%d_%d" % (name, T.rank_of(c), j % 2)], srcs=[src(j)], dsts=[mid(j) for _ in to(j)]) for j in range(3) if to(j)],
+        local_sem=T.sem.lsem)
+    return len(es)
 
 
 def helper_program(g, core, T, topo):
-    mine = [c for c in T.cores if core in helpers_of(T, topo, c)]
+    mine = [c for c in T.cores + [twin(T, topo, x) for x in T.cores] if core in helpers_of(T, topo, c)]
     if not mine:
         return
     me = mine[0]
-    i = helpers_of(T, topo, me).index(core)
-    c0, a, b = PIECE[i]
+    die = helpers_of(T, topo, me).index(core)
+    home_rank = me in T.cores
     es = topo.engines(core, [d for d in T.cores if d != me][0])
     rest = [e for e in topo.engines(core, me) if e not in es]
     sent = 0
-    for q, c in enumerate(T.cores):
-        via = routes(T, topo, c)
-        col = 2048 * (q % 2) + c0
-        home, arr = T["z%d" % (q // 2)][:, col + a:col + b], T.sem["zarr%d" % (q // 2)]
-        slot = T.ind[:, HZ * q + a:HZ * q + b]
-        if c == me:
-            g.wait_ge(T.sem.hin, len(hand_masks(T, topo, c)[i]))
-            if q >= 2:
-                g.wait_ge(T.sem.go, 1)
-            relays = sorted(set(via.values()))
-            direct = [d for d in T.cores if d != c and d not in via and d not in relays]
-            g.remote_dma_fused([RemoteDMATransfer(
-                dst_ids=[dst(topo, helpers_of(T, topo, d)[i]) for d in relays], dma_engine_mask=bits(es),
-                remote_sem=T.sem["rl%d" % q], srcs=[T.z0[:, a:b]], dsts=[slot for _ in relays])], local_sem=T.sem.lsem)
-            g.remote_dma_fused([RemoteDMATransfer(
-                dst_ids=[dst(topo, d) for d in direct], dma_engine_mask=bits(es), remote_sem=arr,
-                srcs=[T.z0[:, a:b]], dsts=[home for _ in direct])], local_sem=T.sem.lsem)
-            sent += 2 * len(es)
-        elif me in via.values():
-            on = [d for d in via if via[d] == me]
-            g.wait_ge(T.sem["rl%d" % q], len(es))
-            g.remote_dma_fused([
-                RemoteDMATransfer(dst_ids=[dst(topo, d) for d in on], dma_engine_mask=bits(es), remote_sem=arr,
-                                  srcs=[slot], dsts=[home for _ in on]),
-                RemoteDMATransfer(dst_ids=[dst(topo, me)], dma_engine_mask=bits(rest), remote_sem=arr,
-                                  srcs=[slot], dsts=[home])], local_sem=T.sem.lsem)
-            sent += len(es) + len(rest)
-    g.wait_ge(T.sem.lsem, sent)
+    for step in range(1 if NXD else 0, 3 if TWO and die < 2 else 0):
+        for q in range(2):
+            c = T.cores[q]
+            if me in (c, twin(T, topo, c)):
+                name, x, arr = first_frame(T, q, step, die)
+                to = [d for d in T.cores if d != c and (d == me or topo.same_plane(topo.chip(d), topo.chip(me)))]
+                g.wait_ge(T.sem[name], len(es) // 2)
+                tr = [RemoteDMATransfer(dst_ids=[dst(topo, d) for d in ds], dma_engine_mask=bits(e), remote_sem=T.sem[arr],
+                                        srcs=[x], dsts=[x for _ in ds])
+                      for ds, e in (([d for d in to if d != me], es), ([d for d in to if d == me], rest)) if ds]
+                g.remote_dma_fused(tr, local_sem=T.sem.lsem)
+                sent += len(es) * len(tr)
+    if DIR and me in T.cores[:2]:
+        for _, name, src, mid, home, arr in [x for x in loads_of(T, T.rank_of(me))[1:] if x[0] == die]:
+            q = T.rank_of(me)
+            to = sorted(T.cores[q + 1:] + T.cores[:q], key=lambda d: topo.same_plane(topo.chip(d), topo.chip(me)) == (die == 0))
+            a, b = PIECE[0][int(name[1])]
+            x = T.z0[:, 2048 * q + a:2048 * q + b]
+            g.wait_ge(T.sem["h" + name], len(rest) // (2 if name in ("z0", "z1") else 1))
+            g.remote_dma_fused([RemoteDMATransfer(dst_ids=[dst(topo, d) for d in to], dma_engine_mask=bits(es), remote_sem=T.sem[arr],
+                                                  srcs=[x], dsts=[x for _ in to])], local_sem=T.sem.lsem)
+            sent += len(es)
+    for t in range(1 if TWO or DIR else 0, 3):
+        pair = [(T.cores[q], [x for x in loads_of(T, q) if x[0] == die]) for q in (2 * t, 2 * t + 1)]
+        for c, loads in pair:
+            if c == me and (t > 0 or die != 1 or not OWN):
+                for load in loads[1 if t == 0 and die == 1 else 0:]:
+                    if (TWO or DIR) and t == 1 and (load[1] != "n" or not NXE):
+                        g.wait_ge(T.sem.go, 1)
+                    g.wait_ge(T.sem["h" + load[1]], len(rest) // (2 if load[1] in ("z0", "z1") else 1))
+                    sent += first_step(g, T, topo, core, c, load)
+        for li in range(len(pair[0][1])):
+            for c, loads in pair:
+                _, name, src, mid, home, arr = loads[li]
+                if arr == "narr0" and NXD:
+                    continue
+                for j, on in spread(T, topo, c).get(me, {}).items():
+                    g.wait_ge(T.sem["r%s_%d_%d" % (name, T.rank_of(c), j % 2)], len(es) // (2 - j // 2))
+                    tr = [RemoteDMATransfer(dst_ids=[dst(topo, me)], dma_engine_mask=bits(rest), remote_sem=T.sem[arr],
+                                            srcs=[mid(j)], dsts=[home(j)])] if home_rank else []
+                    if on:
+                        tr.append(RemoteDMATransfer(dst_ids=[dst(topo, d) for d in on], dma_engine_mask=bits(es), remote_sem=T.sem[arr],
+                                                    srcs=[mid(j)], dsts=[home(j) for _ in on]))
+                    g.remote_dma_fused(tr, local_sem=T.sem.lsem)
+                    sent += (len(rest) if home_rank else 0) + (len(es) if on else 0)
+    for t in range(2 if MH and die == 1 and home_rank else 0):
+        q = T.rank_of(me)
+        x, to = T.pay[:, (6 * t + q) * PW + 256:(6 * t + q) * PW + 264], T.cores[q + 1:] + T.cores[:q]
+        g.wait_ge(T.sem["hm%d" % t], len(rest))
+        g.remote_dma_fused([RemoteDMATransfer(dst_ids=[dst(topo, d) for d in to], dma_engine_mask=bits(es), remote_sem=T.sem["earr%d" % t],
+                                              srcs=[x], dsts=[x for _ in to])], local_sem=T.sem.lsem)
+        sent += len(es)
+    if sent:
+        g.wait_ge(T.sem.lsem, sent)
 
 
 def rank_program(g, core, T, topo):
@@ -185,7 +296,10 @@ def rank_program(g, core, T, topo):
         op("V", lambda: g.vector.tensor_tensor_scan(ap(o), ap(d0), ap(d1), 0.0, ALU.mult, ALU.add), [o], [d0, d1])
 
     def act(o, i, f, bias=0.0, scale=1.0):
-        op("S", lambda: g.scalar.activation(ap(o), ap(i), f, bias=bias, scale=scale), [o], [i])
+        op("S", lambda: g.scalar.activation(ap(o), ap(i), f, bias=ap(bias), scale=ap(scale)), [o], [i, bias, scale])
+
+    def sel(o, i, pat, cmp, base, cm):
+        op("G", lambda: g.affine_select(ap(o), ap(i), pat, cmp, 0.0, base, cm), [o], [i])
 
     def mm(o, l, r, st=True, sp=True):
         op("P", lambda: g.tensor.matmul(ap(o), ap(l), ap(r), st, sp), [o], [l, r])
@@ -199,13 +313,13 @@ def rank_program(g, core, T, topo):
         nadd[0] += 1
         op("G", lambda: g.dma_start(ap(o), ap(i), accum_op=ALU.add), [o], [o, i], sem=("ga%d" % (nadd[0] - 1), 16))
 
-    def iota(o, pat, cm):
+    def iota(o, pat, cm, base=0):
         if SB[o[0]][1] == I:
-            op("G", lambda: g.iota(ap(o), pat, 0, cm), [o], [])
+            op("G", lambda: g.iota(ap(o), pat, base, cm), [o], [])
         else:
-            op("G", lambda: g.iota(ap(o), pat, 0, cm, allow_small_or_imprecise_dtypes=True), [o], [])
+            op("G", lambda: g.iota(ap(o), pat, base, cm, allow_small_or_imprecise_dtypes=True), [o], [])
 
-    others = [d for d in T.cores if d != core]
+    others = T.cores[rank + 1:] + T.cores[:rank]
     off = topo.engines(core, others[0])
     noff = len(off)
     lsum = [0]
@@ -221,25 +335,36 @@ def rank_program(g, core, T, topo):
     col = lambda n, j: R(n, j, j + 1)
     blk = lambda n, j, w=128: R(n, w * j, w * j + w)
 
-    dma("Y", ap(zown), T.z[:], "dz", 16, [zown], [])
+    def load_nx():
+        for gi in range(9):
+            e = "S" if gi % 2 == 0 else "Y"
+            if gi < 7:
+                o, i = T.nxi[16 * gi:16 * gi + 16, :], T.nx[3 * gi:3 * gi + 4, :]
+            elif gi == 7:
+                o, i = T.nxi[112:124, :], T.nx[21:24, :]
+            else:
+                o, i = T.nxi[124:128, :], T.nx[0:1, :]
+            dma(e, o, i, "dnx", 144, [R("nxi")] if gi == 8 else [], [])
+
+    if myt == 0:
+        load_nx()
+        dma("Y", ap(zown), T.z[:], "dz", 16, [zown], [])
     dma("S", T.hu[:, 0:128], T.hyp[:], "dhu", 16, [R("hu", 0, 128)], [])
     dma("S", T.E[:, 0:1024], T.x0[:], "dx0", 16, [R("E", 0, 1024)], [])
-    for gi in range(9):
-        e = "S" if gi % 2 == 0 else "Y"
-        if gi < 7:
-            o, i = T.nxi[16 * gi:16 * gi + 16, :], T.nx[3 * gi:3 * gi + 4, :]
-        elif gi == 7:
-            o, i = T.nxi[112:124, :], T.nx[21:24, :]
-        else:
-            o, i = T.nxi[124:128, :], T.nx[0:1, :]
-        dma(e, o, i, "dnx", 144, [R("nxi")] if gi == 8 else [], [])
-    ms(R("n0w"), 0)
-    dma("Y", T.n0w[0:128:16, :], T.n0[:], "dn0", 16, [R("n0w")], [])
-    dma("Y", T.hu[:, 128:512], T.uu[:], "duu", 16, [R("hu", 128, 512)], [])
+    dma("Y", T.n0l[:, :], T.n0[:], "dn0", 16, [R("n0l")], [])
+    if myt > 0:
+        dma("Y", ap(zown), T.z[:], "dz", 16, [zown], [])
+        load_nx()
 
     iota(R("PIi", 0, 1), [[1, 1]], 1)
     iota(R("CI"), [[1, 128]], 0)
     iota(R("S4i"), [[4, 4], [16, 8]], 0)
+    iota(blk("nxw", 0, 1024), [[1, 1024]], 0, 64)
+
+    def g_early():
+        dma("G", T.hu[:, 128:512], T.uu[:], "duu", 16, [R("hu", 128, 512)], [])
+    if myt > 0:
+        g_early()
     ts(col("PJ", 0), col("PIi", 0), 15, ALU.bitwise_and)
     ts(col("PJ", 1), col("PIi", 0), 4, ALU.arith_shift_right)
     ts(col("PJ", 2), col("PIi", 0), 2, ALU.arith_shift_right, 3, ALU.bitwise_and)
@@ -248,113 +373,162 @@ def rank_program(g, core, T, topo):
     cp(col("PF", 0), col("PIi", 0))
     cp(R("PF", 1, 6), R("PJ", 0, 5))
     ts(R("If"), R("CI"), col("PF", 0), ALU.is_equal)
-    ts(R("SC", 0, 32), R("S4i"), col("PF", 0), ALU.is_equal)
+    ts(R("SC", 0, 24), R("S4i", 0, 24), col("PF", 0), ALU.is_equal)
     ts(R("PF", 12, 16), R("CI", 0, 4), col("PF", 3), ALU.is_equal)
     ts(col("PF", 7), col("PF", 2), 4.0, ALU.mult, col("PF", 4), ALU.add)
     ms(R("live"), 1.0)
     ts(R("Su"), R("CI", 0, 32), col("PF", 7), ALU.is_equal)
 
     def nx_out():
-        cp(R("nxo"), R("nxi"))
+        if myt == 0:
+            cp(blk("nxs", rank, 512), R("nxi"))
+        else:
+            ts(R("nxp", 0, 512), R("nxi"), 64 * MAG, ALU.add, 64 * MAG, ALU.subtract)
+            tt(R("nxp", 512, 1024), R("nxi"), R("nxp", 0, 512), ALU.subtract)
+            hand([(DB[myt], "hn", R("nxp"))])
+
+    hs = helpers_of(T, topo, core)
+    rest = [e for e in topo.engines(core, hs[0]) if e not in off]
+
+    def hand(what):
+        n = len(rest) // len(what)
+        lsum[0] += len(rest)
+        op("G", lambda: g.remote_dma_fused([RemoteDMATransfer(
+            dst_ids=[dst(topo, hs[d])], dma_engine_mask=bits(rest[n * i:n * i + n]), remote_sem=T.sem[sm], srcs=[ap(x)], dsts=[ap(x)])
+            for i, (d, sm, x) in enumerate(what)], local_sem=T.sem.lsem), [], [x for _, _, x in what], sem="remote")
 
     def sends():
-        hs = helpers_of(T, topo, core)
-        masks = hand_masks(T, topo, core)
-        lsum[0] += sum(len(m) for m in masks)
-        z = T["z%d" % myt]
-        if myt == 0:
-            send(R("nxo"), "narr0", ap(blk("nxs", rank, 512)))
-        op("G", lambda: g.remote_dma_fused([RemoteDMATransfer(
-            dst_ids=[dst(topo, hs[i])], dma_engine_mask=bits(masks[i]), remote_sem=T.sem.hin,
-            srcs=[z[:, 2048 * myb + PIECE[i][0]:2048 * myb + PIECE[i][0] + HZ]], dsts=[T.z0[:, 0:HZ]]) for i in range(3)],
-            local_sem=T.sem.lsem), [], [zown], sem="remote")
+        piece = lambda i: R(zown[0], zown[1] + PIECE[myt][i][0], zown[1] + PIECE[myt][i][1])
+        loads = loads_of(T, rank)
+
+        def own(load, x):
+            lsum[0] += noff
+            op("G", lambda: first_step(g, T, topo, core, core, load), [], [x], sem="remote")
+        if myt == 0 and TWO:
+            h = noff // 2
+            for step in ORD:
+                if step == 0 and NXD:
+                    send(blk("nxs", rank, 512), "narr0")
+                    continue
+                lsum[0] += 2 * noff
+                op("G", lambda step=step: g.remote_dma_fused([RemoteDMATransfer(
+                    dst_ids=[dst(topo, helpers_of(T, topo, at)[d])], dma_engine_mask=bits(es[h * d:h * d + h]),
+                    remote_sem=T.sem[first_frame(T, rank, step, d)[0]], srcs=[first_frame(T, rank, step, d)[1]],
+                    dsts=[first_frame(T, rank, step, d)[1]]) for at, es in ((core, rest), (twin(T, topo, core), off)) for d in range(2)],
+                    local_sem=T.sem.lsem), [], [zown if step else blk("nxs", rank, 512)], sem="remote")
+            return
+        if myt == 0 and NXD:
+            send(blk("nxs", rank, 512), "narr0")
+        elif myt == 0:
+            own(loads[0], blk("nxs", rank, 512))
+        hand([(0, "hz0", piece(0)), (HZ1[myt], "hz1", piece(1))])
+        if myt == 0 and OWN:
+            own(loads[3], piece(2))
+        else:
+            hand([(DB[myt], "hz2", piece(2))])
 
     for t in range(3):
         fz = [q for q in (2 * t, 2 * t + 1) if q != rank]
-        arrive("zarr%d" % t, 3 * noff * len(fz), [blk("z%d" % t, q % 2, 2048) for q in fz])
-        arrive("narr%d" % t, noff * len(fz), [blk("nxs", q, 512) if t == 0 else col("nxv", q) for q in fz])
+        arrive("zarr%d" % t, (4 if t == 0 and TWO else 3 if t == 0 and DIR or WHOLE[t] else 6) * noff * len(fz), [blk("z%d" % t, q % 2, 2048) for q in fz])
+        arrive("narr%d" % t, (1 if t == 0 and NXD or WHOLE[t] else 2) * noff * len(fz), [blk("nxs", q, 512) if t == 0 else col("nxv", q) for q in fz])
     if myt == 0:
         nx_out()
     sends()
-    iota(R("Pti", 4, 20), [[64, 4], [1, 4]], 0)
+    if myt == 0:
+        g_early()
+    iota(R("Pti", 0, 32), [[32, 8], [1, 4]], 0)
+    iota(R("Pti", 32, 64), [[1, 8], [8, 4]], 0, 256)
+    iota(R("Pti", 64, 80), [[64, 4], [1, 4]], 0)
+    iota(R("Pti", 80, 112), [[0, 4], [1, 8]], 0)
+    iota(R("Pti", 112, 144), [[1, 4], [16, 8]], 0)
+    iota(R("Pti", 144, 152), [[0, 4], [4, 2]], 0)
     iota(R("BM"), [[0, 8], [1, 4], [0, 4]], 0)
 
     for a in range(4):
         ts(R("D1", a, 512, 4), R("hu", 0, 128), col("PF", 12 + a), ALU.mult)
     for k in range(4):
         mm(R("ps5", k, 128, 4), blk("D1", k), R("Su"))
-    for j in range(4):
-        act(blk("nxw", j, 1024), R("E", 0, 1024), ACT.Copy)
+    for j in range(1, 4):
+        act(blk("nxw", j, 1024), blk("nxw", 0, 1024), ACT.Identity, bias=1024.0 * j)
     cp(R("Ibf"), R("If"))
-    ts(R("took"), R("ps5", 0, 128), 1.0, ALU.add)
+    ts(R("took"), R("ps5", 0, 128), -31.5, ALU.add)
     mm(R("ps2", 0, 128), R("took"), R("If"))
-    ts(R("T1"), R("ps5", 0, 128), 4.0, ALU.mult, -30.0, ALU.add)
+    ts(R("pairb"), R("ps5", 0, 128), 4.0, ALU.mult, -15.5, ALU.add)
+    ts(R("C32"), R("CI"), 32.0, ALU.mult)
+    ts(R("hi"), R("pairb"), 32 * MAG, ALU.add, 32 * MAG, ALU.subtract)
+    ts(R("T1"), R("ps5", 0, 128), 4.0, ALU.mult, 4.0, ALU.add)
+    ts(R("LT"), R("ps2", 0, 128), 31.5, ALU.add)
+    ts(R("ta"), R("ps2", 0, 128), 64 * MAG, ALU.add, 64 * MAG, ALU.subtract)
+    ts(R("tc"), R("ps2", 0, 128), 16.0, ALU.mult, 504.0, ALU.add)
+    ts(R("ta"), R("ta"), -1023.0 / 64, ALU.mult)
     ms(R("Ones"), 1.0)
-    ms(R("Vw", 0, 512, 4), 2.0)
-    ts(R("LT"), R("ps2", 0, 128), -1.0, ALU.add)
-    cp(R("G"), IND("n0w", 0, 1024, "LT", 0, 128))
-    for r in range(16):
-        mm(R("ps1", r, 128, 16), R("G", r, 2048, 16), R("SC", 0, 8))
-    for a in range(4):
-        ts(R("D1", 512 + a, 2048, 4), R("hu", 128, 512), col("PF", 12 + a), ALU.mult)
-    ts(R("N1"), R("ps1", 0, 128), 1.0, ALU.add)
-    mm(R("ps2", 0, 128), R("N1"), R("If"))
-    for kk in range(4, 16):
-        bl, k = kk // 4, kk % 4
-        mm(R("ps5", 128 * bl + k, 128 * bl + 128, 4), blk("D1", kk), R("Su"))
+    tt(R("tc"), R("tc"), R("ta"), ALU.add)
+    ms(R("Vw", 0, 640, 5), 2.0)
+    ms(R("Vw", 4, 640, 5), 0.0)
+    cp(R("Li"), R("tc"))
+    cp(R("Ln", 0, 64), R("n0l"))
+
+    def u_in():
+        for a in range(4):
+            ts(R("D1", 512 + a, 2048, 4), R("hu", 128, 512), col("PF", 12 + a), ALU.mult)
+        for kk in range(4, 16):
+            bl, k = kk // 4, kk % 4
+            mm(blk("ps5", kk, 32), blk("D1", kk), R("Su"))
 
     def nx_in(t):
         for b in range(2):
-            cp(blk("nxf", b, 512), blk("nxs", b, 512))
-            dma("Y", T.nxw[t:128:4, 2048 * b:2048 * b + 2048], T.nxf[:, 512 * b:512 * b + 512], "dw%d" % t, 32,
-                [blk("nxw", b, 2048)], [blk("nxf", b, 512)])
-
-    def nx_stage(t):
-        for b in range(2):
             q = 2 * t + b
-            i, r = (T.nxo[:, :], R("nxo")) if q == rank else (T.nxd[q], col("nxv", q))
-            dma("Y", T.nxs[:, 512 * b:512 * b + 512], i, "dv%d" % t, 32, [blk("nxs", b, 512)], [r])
+            if t == 0:
+                ts(blk("nxf", b, 512), blk("nxs", b, 512), 64.0, ALU.add)
+                dma("Y", T.nxw[0:128:4, 2048 * b:2048 * b + 2048], T.nxf[:, 512 * b:512 * b + 512], "dw0", 32,
+                    [blk("nxw", b, 2048)], [blk("nxf", b, 512)])
+                continue
+            for i in range(2):
+                src, r = (T.nxp[:, 512 * i:512 * i + 512], R("nxp")) if q == rank else (T.nxe[q, :, 512 * i:512 * i + 512] if WHOLE[t] else T.nxd[q, i], col("nxv", q))
+                dma("Y", T.nxb[i:128:4, 2048 * b:2048 * b + 2048], src, "dw%d" % t, 64, [blk("nxb", b, 2048)], [r])
 
-    ts(R("Ln"), R("ps2", 0, 128), -1.0, ALU.add)
     act(R("Y"), IND("E", 0, 1024, "LT", 0, 128), ACT.Identity, scale=-1.0)
-    if myt > 0:
-        nx_out()
-    else:
-        cp(blk("nxs", rank, 512), R("nxo"))
-    ts(R("UU"), R("ps5", 128, 512), 1.0 / 64, ALU.mult)
 
-    def prep(t):
-        ts(R("hi"), R("T1"), 64 * MAG, ALU.add, 64 * MAG, ALU.subtract)
-        f = [lambda j=j: ts(blk("OHh", j), R("hi"), 64.0 * j, ALU.is_equal) for j in range(64)]
-        f.insert(1, lambda: tt(R("tl4"), R("T1"), R("hi"), ALU.subtract))
-        return f
+    def hots():
+        return [lambda c=c: ts(blk("OHh", c), R("C32"), col("hi", c), ALU.is_equal) for c in range(128)]
 
-    def place_list():
-        mm(R("ps2", 256, 384), R("hi"), R("I64"), True, False)
-        mm(R("ps2", 256, 384), R("tl4"), R("I16"), False, True)
-        ts(R("Li"), R("ps2", 256, 384), 480.0, ALU.add, 1023.0, ALU.min)
+    def hots_s(c0, c1=128):
+        for c in range(c0, c1):
+            act(blk("OHh", c), R("C32"), ACT.Abs, bias=col("hi", c), scale=-1.0)
+            if c % 8 == 7:
+                a = max(c0, c - 7)
+                act(R("OHh", 128 * a, 128 * c + 128), R("OHh", 128 * a, 128 * c + 128), ACT.Relu, bias=1.0, scale=-1.0)
 
-    def masks():
-        return [lambda: ts(R("dead"), R("live"), -1.0, ALU.mult, 1.0, ALU.add),
-                lambda: ts(R("td"), R("live"), -64.0, ALU.mult, 94.0, ALU.add),
-                lambda: ts(R("te"), R("live"), -8192.0, ALU.mult, 8192.0, ALU.add)]
+    def place_list(t):
+        w = WL[t]
+        mm(R("ps2", 256, 384), R("hi"), blk("I%d" % w, 0), True, False)
+        mm(R("ps2", 256, 384), R("lo"), blk("I%d" % w, 1), False, False)
+        for m in range(3):
+            mm(R("ps2", 256, 384), blk("le%d" % (t % 2), m), blk("I%d" % w, 2), False, m == 2)
+        ts(R("Li"), R("ps2", 256, 384), 512.0 - 512.0 / w, ALU.add, 1023.0, ALU.min)
+
+    def masks(t):
+        return [lambda: ts(R("td"), R("live"), -16384.0, ALU.mult, 16384.0 - 3.5 - WL[t] / 2, ALU.add)]
 
     def succ_a(t, split):
+        w, n, l, o, sel = ("nxb", 4096, "Ln", "Gb", "SCb") if t > 0 else ("tab", 1024, "Li", "G", "SC")
+        if t == 0:
+            act(R("tab", 0, 512), IND("nxw", 0, 4096, "Ln", 0, 32), ACT.Identity)
+            cp(R("tab", 512, 1024), IND("nxw", 0, 4096, "Ln", 32, 64))
         if split:
-            act(R("G", 0, 1024), IND("nxw", 0, 4096, "Ln", 0, 64), ACT.Identity)
-            cp(R("G", 1024, 2048), IND("nxw", 0, 4096, "Ln", 64, 128))
-        else:
-            act(R("G"), IND("nxw", 0, 4096, "Ln", 0, 128), ACT.Identity)
+            act(R(o, 0, 16 * split), IND(w, 0, n, l, 0, split), ACT.Identity)
+        if split < 128:
+            cp(R(o, 16 * split, 2048), IND(w, 0, n, l, split, 128))
         for r in range(16):
-            mm(R("ps1", r, 384, 16), R("G", r, 2048, 16), R("SC", 32 * t, 32 * t + 24))
+            mm(R("ps1", r, 16 * SB[sel][0], 16), R(o, r, 2048, 16), R(sel))
 
     def succ_b():
-        act(R("C1"), R("ps1", 0, 384), ACT.Identity, bias=1.0)
+        act(R("C1"), R("ps1", 0, 384), ACT.Copy)
         for m in range(3):
             mm(blk("ps3", m), blk("C1", m), R("If"))
 
     def lists_c():
-        ts(R("Lc"), R("ps3", 0, 384), -1.0, ALU.add)
+        ts(R("Lc"), R("ps3", 0, 384), -64.0, ALU.add)
 
     def chunk(t, ch, by_v):
         d = R(DN[t], 16 + 1024 * ch, 16 + 1024 * ch + 1024)
@@ -370,8 +544,8 @@ def rank_program(g, core, T, topo):
         wp = lambda m, r: R("ps7", 128 * (r % 4) + 4 * (r // 4) + m + 1, 128 * (r % 4) + 128, 16)
         if m == 0 and SI[t]:
             for ch in range(2):
-                act(blk("E", ch, 1024), R(DN[t], 16 + 1024 * ch, 16 + 1024 * ch + 1024), ACT.Abs)
-                act(blk("ind", ch, 1024), blk("E", ch, 1024), ACT.Sign, bias=1.0 + 2.0 ** -12, scale=-1.0)
+                act(blk("G", ch, 1024), R(DN[t], 16 + 1024 * ch, 16 + 1024 * ch + 1024), ACT.Abs)
+                act(blk("ind", ch, 1024), blk("G", ch, 1024), ACT.Sign, bias=1.0 + 2.0 ** -12, scale=-1.0)
             return
         if m == 3:
             if SI[t]:
@@ -379,82 +553,120 @@ def rank_program(g, core, T, topo):
                     mm(wp(0, r), R("ind", r, 2048, 16), R("Bh"))
             return
         for ch in (2 * m, 2 * m + 1):
+            if ch == 5:
+                weights(t, 0, VW0[t])
             ts(blk("ind", ch, 1024), R(DN[t], 16 + 1024 * ch, 16 + 1024 * ch + 1024), big, ALU.add, big, ALU.is_equal)
         for r in range(16):
             mm(wp(m, r), R("ind", 2048 * m + r, 2048 * m + 2048, 16), R("B1"))
 
+    def weights(t, a, b):
+        for i in range(a, b):
+            if i == 0 and t > 0:
+                ts(R("e8", 0, 8), R("ps1", 16, 24), 1.0 / 2048, ALU.mult, 0.5 + 2.0 ** -12, ALU.add)
+            elif i == 1 and t > 0:
+                ts(R("Vw", 0, 640, 5), IND("e8", 0, 16, "Lw", 0, 8), MAG, ALU.add, MAG, ALU.subtract)
+            elif i > 1:
+                m = (1, 0, 2)[i - 2]
+                ts(R("Vw", m + 1, 640, 5), R("ps7", m + 1, 512, 4), 4.0 if SI[t] and m == 0 else -4.0, ALU.add, 0.0, ALU.max)
+
     def terms_a(t):
-        d = DN[t]
-        act(R(d, 0, 16), R("Ones", 0, 16), ACT.Copy)
-        act(R("E"), IND(d, 0, DW, "Ls%d" % (t % 2), 0, 128), ACT.Abs)
-        if t == 2:
-            act(R(d, 0, 16), R("Ones", 0, 16), ACT.Copy, scale=0.0)
-        if t < 2:
-            act(R("E"), R("E"), ACT.Exp, scale=-1.0)
+        act(R("E"), R("Y4"), ACT.Abs, scale=4.0)
+        act(R("E"), R("E"), ACT.Exp, scale=-1.0)
 
-    def terms_b(t):
-        for k in range(4):
-            mm(R("ps0"), R("If"), R("E", k, 2048, 4), t == 0 and k == 0, t == 2 and k == 3)
+    def terms_b(t, a=0, b=8):
+        for i in range(a, b):
+            k, h = i // 2, i % 2
+            if t == 0 and k == 0:
+                if h == 0:
+                    mm(R("ps0"), R("If"), R("E", 0, 2048, 4), True, False)
+            else:
+                mm(blk("ps0", h, 256), R("If"), R("E", 1024 * h + k, 1024 * h + 1024, 4), False, False)
 
-    halves = [(64 * gh, 64 * gh + 64) for gh in range(2)]
+    def terms_c():
+        for i in range(12):
+            mm(R("ps1", 32, 64), R("Ibf"), R("miss", 128 * (i // 4) + i % 4, 128 * (i // 4) + 128, 4), i == 0, i == 11)
+        act(R("mc"), R("ps1", 32, 64), ACT.Identity, scale=math.exp(-1.0) - 1.0)
+        act(R("nxf", 0, 512), IND("mc", 0, 32, "Lm", 0, 32), ACT.Identity)
+        terms_b(2)
+
+    def terms_d():
+        for sl in range(4):
+            mm(R("ps0", sl, 512, 4), blk("nxf", sl), R("If"), False, sl == 3)
 
     def bound(t):
         for q in range(6):
             b = (6 * t + q) * PW
             mm(R("ps4", 0, 256), R("Ibf"), R("pay", b, b + 256), q == 0, q == 5)
-        ts(R("mk"), R("ps4", 0, 256), 1.0, ALU.min)
-        scan(R("incl"), R("rst"), R("mk"))
-        for p0, p1 in halves:
-            mm(R("ps4", 384, 388, 1, p0, p1), R("Tri", p0, p1, 1, p0, p1), R("incl", 63, 256, 64, p0, p1))
+        w = WL[t]
+        n = 256 // w
+        parts = [(0, 128)] if w == 32 else [(0, 64), (64, 128)]
+        rst = R("rst%d" % w)
+        if MKS:
+            act(R("mk"), R("ps4", 0, 256), ACT.Sign)
+        else:
+            ts(R("mk"), R("ps4", 0, 256), 1.0, ALU.min)
+        scan(R("incl", 0, 256), rst, R("mk"))
+        pre = R("ps4", 384, 384 + n)
+        for p0, p1 in parts:
+            mm(R("ps4", 384, 384 + n, 1, p0, p1), R("Tri", p0, p1, 1, p0, p1), R("incl", w - 1, 256, w, p0, p1))
 
-        def table(tls):
-            for tl in tls:
-                for p0, p1 in halves:
-                    o = R("ps%d" % (5 + tl // 8), 64 * (tl % 8), 64 * (tl % 8) + 64, 1, p0, p1)
-                    mm(o, R("X", 64 + tl, 64 + tl + 253, 4, p0, p1), R("Ibf", p0, p1, 1, p0, p1), True, False)
-                    mm(o, R("X", 0, 64, 1, p0, p1), R("Tri", p0, p1, 1, p0, p1), False, True)
-        n0 = 6 if XF else 0
-        if t < 2 and XF:
-            cp(R("X", 0, 320), IND("incl", 0, 256, "Lp", 0, 20))
-            table(range(n0))
-        for gl in range(4):
-            ts(blk("ib", gl, 64), blk("incl", gl, 64), col("ps4", 384 + gl), ALU.add, 1024.0, ALU.is_le)
-        scan(R("mk"), R("rst"), R("ib"))
-        for gh, (p0, p1) in enumerate(halves):
-            mm(R("ps1", 4 * gh, 4 * gh + 4), blk("Hf", gh), R("mk", 63, 256, 64))
+        def digits():
+            ts(R("incl", 256, 256 + n), pre, 32 * MAG, ALU.add, 32 * MAG, ALU.subtract)
+            tt(R("incl", 264, 264 + n), pre, R("incl", 256, 256 + n), ALU.subtract)
+            if XS:
+                act(R("X", 0, 512), IND("incl", 0, 288, "Lp%d" % w, 0, 32), ACT.Identity)
+            else:
+                cp(R("X", 0, 512), IND("incl", 0, 288, "Lp%d" % w, 0, 32))
+
+        def table():
+            for tl in range(w // 4):
+                for p0, p1 in parts:
+                    c, st = (p1 - p0) * tl, w // 8
+                    mm(R("ps%d" % (5 + c // 512), c % 512, c % 512 + p1 - p0, 1, p0, p1),
+                       R("X", tl, tl + 512 - st + 1, st, p0, p1), R("Ibf", p0, p1, 1, p0, p1))
+        if t < 2 and XF == 0:
+            digits()
+        for gi in range(n):
+            ts(blk("ib", gi, w), blk("incl", gi, w), col("ps4", 384 + gi), ALU.add, 1024.0, ALU.is_le)
+        scan(R("mk"), rst, R("ib"))
+        for h, (p0, p1) in enumerate(parts):
+            mm(R("ps1", n * h, n * h + n), R("Ones") if w == 32 else blk("Hf", h), R("mk", w - 1, 256, w))
+        if t < 2 and XF == 1:
+            digits()
         if t < 2:
-            if not XF:
-                cp(R("X", 0, 320), IND("incl", 0, 256, "Lp", 0, 20))
-            table(range(n0, 16))
+            terms_b(t, 0, TB0)
+            table()
         cp(R("th", 0, 8), R("ps1", 0, 8))
         if t < 2:
             tt(R("live"), IND("th", 0, 16, "Lth", 0, 8), R("pairb"), ALU.is_gt)
 
+
     def misses_out(t):
         b = (6 * t + rank) * PW + 256
         act(R("pay", b, b + 8), R("ps4", 256, 264), ACT.Copy)
-        send(R("pay", b, b + 8), "earr%d" % t)
+        if MH:
+            hand([(1, "hm%d" % t, R("pay", b, b + 8))])
+        else:
+            send(R("pay", b, b + 8), "earr%d" % t)
         arrive("earr%d" % t, 5 * noff, [R("pay", (6 * t + q) * PW + 256, (6 * t + q) * PW + 264) for q in range(6) if q != rank])
 
     def miss_weight(t):
         for q in range(6):
             b = (6 * t + q) * PW
             mm(R("ps1", 16, 24), R("Ones"), R("pay", b + 256, b + 264), q == 0, q == 5)
-        ts(R("e8", 0, 8), R("ps1", 16, 24), 1.0 / 2048, ALU.mult, 0.5 + 2.0 ** -12, ALU.add)
 
     def places_b():
-        act(R("tab", 0, 512), R("ps5"), ACT.Identity, bias=-34.0, scale=4.0)
-        act(R("tab", 512, 1024), R("ps6"), ACT.Identity, bias=-34.0, scale=4.0)
-        act(R("G"), IND("tab", 0, 1024, "Li", 0, 128), ACT.Identity)
+        act(R("tabb", 0, 512), R("ps5"), ACT.Copy)
+        act(R("tabb", 512, 1024), R("ps6"), ACT.Copy)
+        act(R("Gb"), IND("tabb", 0, 1024, "Li", 0, 128), ACT.Identity)
         for r in range(16):
-            mm(R("ps3", r, 512, 16), R("G", r, 2048, 16), R("Sd"))
+            mm(R("ps3", r, 384, 16), R("Gb", r, 2048, 16), R("Sd", 0, 24))
+        mm(R("ps6", 0, 128), R("Ibf"), R("td"), True, False)
+        for r in range(16):
+            mm(R("ps6", r, 128, 16), R("Gb", r, 2048, 16), R("Sd", 24, 32), False, False)
 
     def places_c(t):
-        for m in range(3):
-            tt(blk("dr", m), blk("ps3", m), blk("le%d" % (t % 2), m), ALU.mult)
-        tt(R("ta"), R("ps3", 384, 512), blk("dr", 0), ALU.add)
-        tt(R("tb"), blk("dr", 1), blk("dr", 2), ALU.add)
-        tt(R("T1"), R("ta"), R("tb"), ALU.add)
+        tt(R("pb"), R("ps3", 0, 384), R("le%d" % (t % 2)), ALU.mult)
 
     def draw(t, fill, between):
         le = "le%d" % (t % 2)
@@ -475,46 +687,57 @@ def rank_program(g, core, T, topo):
 
         def mul(j, k, m):
             b = 96 * (j * (7 - j) // 2 + k - j - 1) + 32 * m
-            v = R("Vw", 128 * k + m + 1, 128 * k + 128, 4)
+            v = R("Vw", 160 * k + m + 1, 160 * k + 160, 5)
             tt(v, v, R("ne", b, b + 32), ALU.mult)
 
-        if t > 0:
-            ts(R("Vw", 0, 512, 4), IND("e8", 0, 16, "Lw", 0, 8), MAG, ALU.add, MAG, ALU.subtract)
-        for m in range(3):
-            ts(R("Vw", m + 1, 512, 4), R("ps7", m + 1, 512, 4), 4.0 if SI[t] and m == 0 else -4.0, ALU.add, 0.0, ALU.max)
+        weights(t, VW0[t], 5)
         gap(1)
         for k in range(4):
             b0 = 384 * (k % 3)
             d = lambda i: R("dr", b0 + 32 * i, b0 + 32 * i + 32)
-            pm = lambda m: R("dr", b0 + m, b0 + 128, 4)
-            n = 3 * k
-            scan(R("dr", b0, b0 + 128), R("rs4"), blk("Vw", k))
-            gap(n)
-            tt(d(4), pm(3), sl("UU", t, k), ALU.mult)
-            gap(n)
+            pm = lambda m: R("Pm", 160 * k + m, 160 * k + 160, 5)
+            n = 2 * k
+            scan(blk("Pm", k, 160), blk("U5", 4 * t + k, 160), blk("Vw", k, 160))
+            gap(n + GA)
+            if t > 0 and k == 3 and PLK[t] == 4:
+                places_c(t - 1)
             for m in range(3):
-                tt(sl(le, m, k), pm(m), d(4), ALU.is_le)
+                tt(sl(le, m, k), pm(m), pm(4), ALU.is_le)
             if t == 2 and k == 3:
+                if PLK[t] == 3:
+                    places_c(t - 1)
                 break
             tt(d(5), sl(le, 0, k), sl("C1", 0, k), ALU.mult)
             tt(d(6), sl(le, 1, k), sl("Dc", 0, k), ALU.mult)
             tt(d(7), sl(le, 2, k), sl("Dc", 1, k), ALU.mult)
+            if 0 < k < 3:
+                gap(n - GA)
             tt(d(8), d(5), d(6), ALU.add)
             if k == 0 and t > 0:
                 tt(sl("took", 0, k), d(8), d(7), ALU.add)
                 between()
                 tt(sl("took", 0, 0), sl("took", 0, 0), sl("live", 0, 0), ALU.mult)
-                tt(blk("UU", t), blk("UU", t), R("live"), ALU.mult)
+                u5 = lambda k2: R("U5", 640 * t + 160 * k2 + 4, 640 * t + 160 * k2 + 160, 5)
+                um = lambda k2: tt(u5(k2), u5(k2), sl("live", 0, k2), ALU.mult)
+                um(1)
                 for m in range(3):
                     ne(k, k + 1, m)
                 for m in range(3):
                     mul(k, k + 1, m)
-                gap(1)
+                um(2)
+            elif k < 3 and not SUB:
+                tt(sl("took", 0, k), d(8), d(7), ALU.add)
+                for m in range(3):
+                    ne(k, k + 1, m)
+                for m in range(3):
+                    mul(k, k + 1, m)
             elif k < 3:
                 for m in range(3):
                     tt(d(9 + m), sl("C1", m, k + 1), d(7), ALU.subtract)
                 for m in range(3):
                     ne(k, k + 1, m, d(9 + m), d(8))
+                if k > 0:
+                    gap(n)
                 for m in range(3):
                     mul(k, k + 1, m)
                 tt(sl("took", 0, k), d(8), d(7), ALU.add)
@@ -524,6 +747,9 @@ def rank_program(g, core, T, topo):
             for k2 in range(k + 2, 4):
                 lazy += [lambda m=m, k2=k2, k=k: ne(k, k2, m) for m in range(3)]
                 lazy += [lambda m=m, k2=k2, k=k: mul(k, k2, m) for m in range(3)]
+            if t > 0 and k == PLK[t] > 0:
+                places_c(t - 1)
+
         assert not lazy
         while fill:
             fill.pop(0)()
@@ -531,70 +757,103 @@ def rank_program(g, core, T, topo):
     def marks_out(t):
         b = (6 * t + rank) * PW
         n = 256
-        act(R("pay", b, b + 256), R("ps4", 0, 256), ACT.Sign)
+        if t == 2:
+            ts(R("pay", b, b + 256), R("ps4", 0, 256), 1.0, ALU.min)
+        else:
+            act(R("pay", b, b + 256), R("ps4", 0, 256), ACT.Sign)
         send(R("pay", b, b + n), "harr%d" % t)
         arrive("harr%d" % t, 5 * noff, [R("pay", (6 * t + q) * PW, (6 * t + q) * PW + n) for q in range(6) if q != rank])
 
     def after_draw(t):
         le, ls, dd = "le%d" % (t % 2), "Ls%d" % (t % 2), DN[t]
+        w = WL[t]
+        pr = R("ps6", 0, 128)
+
+        def pair_sum():
+            parts = [(R("If"), R("T1")), (R("Ibf"), R("td"))] if t == 0 else []
+            parts += [(R("Ibf"), blk(le, m)) for m in range(3)] + [(R("Ibf"), blk("pb", m)) for m in range(3 if t > 0 else 0)]
+            for i, (a, b) in enumerate(parts):
+                mm(pr, a, b, i == 0 and t == 0, i == len(parts) - 1)
+        if PLK[t] or t == 0:
+            pair_sum()
         if t < 2:
-            ts(R("ta"), R("took"), 0.0, ALU.is_equal)
-        tt(R("tb"), blk(le, 0), blk(le, 1), ALU.add)
-        if t < 2:
-            tt(R("tc"), R("ta"), R("N1"), ALU.mult)
-        tt(R("pick"), R("tb"), blk(le, 2), ALU.add)
-        if t < 2:
-            tt(R("N1"), R("tc"), R("took"), ALU.add)
-            mm(R("ps2", 0, 128), R("N1"), R("If"))
-        mm(R("ps2", 128, 256), R("pick"), R("I2k"), True, False)
-        mm(R("ps2", 128, 256), R("dead"), R("I8k"), False, False)
+            tt(blk("miss", t), R("live"), blk(le, 0), ALU.is_gt)
+            tt(R("tc"), blk("miss", t), R("N1"), ALU.mult)
+        for m in range(3):
+            mm(R("ps2", 128, 256), blk(le, m), R("I2k"), m == 0, False)
+        mm(R("ps2", 128, 256), R("td"), R("Ibf"), False, False)
         mm(R("ps2", 128, 256), R("Ones"), R("Dg"), False, True)
         if t < 2:
-            tt(R("miss"), R("live"), blk(le, 0), ALU.is_gt)
-        else:
+            mm(R("ps2", 0, 128), R("took"), R("If"), True, False)
+            mm(R("ps2", 0, 128), R("tc"), R("If"), False, True)
+
+        if t > 0 and not PLK[t]:
             places_c(t - 1)
+            pair_sum()
+        if t > 0:
+            terms_b(t - 1, TB1)
+
+        def pairs():
+            if t > 0:
+                ts(R("hi"), pr, w * MAG, ALU.add, w * MAG, ALU.subtract)
+            tt(R("lo"), pr, R("hi"), ALU.subtract)
+        if PF1[t]:
+            pairs()
         if t < 2:
-            ts(R("Ln"), R("ps2", 0, 128), -1.0, ALU.add)
-        ts(R(ls), R("ps2", 128, 256), col("PF", 6), ALU.add, float(DW - 16), ALU.min)
+            ts(R("Ln"), R("ps2", 0, 128), -64.0, ALU.add)
+        ts(R(ls), R("ps2", 128, 256), col("PF", 6 if w == 32 else 25), ALU.add, float(DW - 16), ALU.min)
         if t < 2:
             for r in range(16):
-                mm(R("ps4", 256, 264), R("Ibf"), R("miss", r, 128, 16), r == 0, r == 15)
-            succ_a(t + 1, t == 0)
+                mm(R("ps4", 256, 264), R("Ibf"), R("miss", 128 * t + r, 128 * t + 128, 16), r == 0, r == 15)
+            y0 = [0]
+
+            def y4(y1):
+                for a, b in ((y0[0], min(y1, 64)), (max(y0[0], 64), y1)):
+                    if a < b:
+                        act(R("Y4", 16 * a, 16 * b), IND(dd, 0, DW, ls, a, b), ACT.Identity, scale=-0.25)
+                        if b % 64 == 0:
+                            add(blk("Y", b // 64 - 1, 1024), blk("Y4", b // 64 - 1, 1024))
+                y0[0] = y1
+            y4(Y4A[t][0])
+            succ_a(t + 1, SPL[t])
             misses_out(t)
-            if not YV[t]:
-                act(blk("Y4", 0, 1024), IND(dd, 0, DW, ls, 0, 64), ACT.Identity, scale=-0.25)
-                add(blk("Y", 0, 1024), blk("Y4", 0, 1024))
-            if t == 1:
-                places_c(0)
+            y4(Y4A[t][1])
             succ_b()
-            if not YV[t]:
-                act(blk("Y4", 1, 1024), IND(dd, 0, DW, ls, 64, 128), ACT.Identity, scale=-0.25)
-                add(blk("Y", 1, 1024), blk("Y4", 1, 1024))
+            y4(128)
+        if not PF1[t]:
+            pairs()
+        c0 = 128 - len(hot) if t == 0 else 0
+        if w == 32:
+            f = [lambda j=j: ts(blk("OHl", j), R("lo"), j - 15.5, ALU.is_equal) for j in range(32)]
+            f += hots()[c0:128 - NS[t]]
         else:
+            f = [lambda j=j: ts(blk("OHh", j), R("hi"), 64.0 * j, ALU.is_equal) for j in range(64)]
+            f += [lambda j=j: ts(blk("OHh", 64 + j), R("lo"), j - 31.5, ALU.is_equal) for j in range(64)]
+        if t > 0:
+            hots_s(128 - NS[t])
+        if t == 2:
+            act(R("Y4"), IND(dd, 0, DW, ls, 0, 128), ACT.Identity, scale=-0.25)
+            add(R("Y"), R("Y4"))
             terms_a(2)
-        f = prep(t) if t > 0 else []
-        lo = lambda: tt(R("lo"), R("lob"), R("tl4"), ALU.add)
-        f.insert(0, lambda: tt(R("lob"), R("pick"), R("td"), ALU.add))
-        f.insert(min(len(f), 4), lo)
-        ns = NS if t == 2 else 0
-        f += [lambda j=j: ts(blk("OHl", j), R("lo"), float(j), ALU.is_equal) for j in range(64 - ns)]
         for i, fn in enumerate(f):
             if t < 2 and i == LCAT[t]:
                 lists_c()
             fn()
-            if fn is lo and ns:
-                for j in range(64 - ns, 64):
-                    act(blk("OHl", j), R("lo"), ACT.Abs, bias=-float(j))
-                act(R("OHl", 128 * (64 - ns), 8192), R("OHl", 128 * (64 - ns), 8192), ACT.Relu, bias=1.0, scale=-1.0)
-                act(R("E"), R("E"), ACT.Exp, scale=-1.0)
-        for c in range(128):
-            gh, gl = c // 64, c // 16 % 4
-            mm(R("ps4", 64 * gl, 64 * gl + 64, 1, 64 * gh, 64 * gh + 64), R("OHh", c, 8192, 128), R("OHl", c, 8192, 128),
-               c % 16 == 0, c % 16 == 15)
+        if t < 2 and LCAT[t] >= len(f):
+            lists_c()
+        late_g = [gi for gi in range(8) if 16 * gi + 16 > c0 and 16 * gi < 128 - NS[t]] if t == 0 else []
+        for c in [16 * gi + r for gi in sorted(range(8), key=lambda gi: gi in late_g) for r in range(16)]:
+            if w == 32:
+                mm(R("ps4", 32 * (c // 16), 32 * (c // 16) + 32), blk("OHh", c), R("OHl", c, 4096, 128), c % 16 == 0, c % 16 == 15)
+            else:
+                gh, gl = c // 64, c // 16 % 4
+                mm(R("ps4", 64 * gl, 64 * gl + 64, 1, 64 * gh, 64 * gh + 64), R("OHh", c, 8192, 128),
+                   R("OHh", 8192 + c, 16384, 128), c % 16 == 0, c % 16 == 15)
         if t == 2:
-            ts(R("Y4"), IND(dd, 0, DW, ls, 0, 128), 0.25, ALU.mult)
-        tt(R("ta"), R("te"), R("hi"), ALU.add)
-        tt(R("pairb"), R("ta"), R("lo"), ALU.add)
+            tt(blk("miss", t), R("live"), blk(le, 0), ALU.is_gt)
+        ts(R("pairb"), pr, w / 2 - 0.5, ALU.add)
+        if t == 0:
+            tt(R("N1"), R("tc"), R("took"), ALU.add)
 
     def gates(t):
         sent = t == 0
@@ -605,127 +864,148 @@ def rank_program(g, core, T, topo):
             chunk(t, ch, False)
         if not sent:
             marks_out(t - 1)
-        tt(R("Dc"), R("C1", 128, 384), R("C1", 0, 256), ALU.subtract)
-        for ch in range(NV[t]):
+        tt(R("Dc"), R("ps1", 128, 384), R("C1", 0, 256), ALU.subtract)
+        for ch in sorted(range(NV[t]), key=lambda ch: ch % 2):
             chunk(t, ch, True)
-        if t > 0:
-            place_list()
-            miss_weight(t - 1)
-        for m in (0, 1, 3, 2):
+        for i, m in enumerate((0, 1, 3, 2)):
+            if t > 0 and i == MWAT:
+                place_list(t - 1)
+                miss_weight(t - 1)
             gate(t, m)
         if t > 0:
             terms_a(t - 1)
 
-    fill = prep(0)
-    nx_in(0)
-    for _ in range(HV):
-        fill.pop(0)()
+    hot = hots()
+    ts(col("PF", 24), col("PF", 0), -3.0, ALU.add)
     ts(col("PF", 16), col("PF", 0), 16.0, ALU.mult)
-    ts(col("PF", 6), col("PF", 1), -2032.0, ALU.add)
+    ts(col("PF", 6), col("PF", 1), 19.5 - 2032.0, ALU.add)
+    ts(col("PF", 25), col("PF", 1), 35.5 - 2032.0, ALU.add)
+    ts(col("PF", 26), col("PF", 0), -2.0, ALU.add)
     ts(col("PF", 17), col("PF", 1), -496.0, ALU.add)
-    ts(col("PF", 8), col("PF", 1), 4.0, ALU.mult)
+    ts(col("PF", 23), col("PF", 1), 8.0, ALU.is_lt)
+    ts(col("PF", 27), col("PF", 1), 8.0, ALU.is_ge)
     ts(col("PF", 9), col("PF", 3), 1.0, ALU.add)
-    ts(col("PF", 10), col("PF", 0), -1.0, ALU.add)
-    ts(col("PF", 11), col("PF", 0), -2.0, ALU.add)
+    ts(col("PF", 10), col("PF", 5), 4.0, ALU.mult)
+    ts(col("PF", 11), col("PF", 4), 3.0, ALU.is_lt)
     ts(col("PF", 22), col("PF", 4), 4.0, ALU.mult)
+    ts(col("PF", 8), col("PF", 1), 4.0, ALU.mult)
     ts(R("B1"), R("CI", 0, 8), col("PF", 2), ALU.is_equal)
-    for d in DN:
+    for d in DN[:2]:
         ms(R(d, 0, 16), 0.0)
         ms(R(d, DW - 16, DW), 4000.0)
-    succ_a(0, True)
-    succ_b()
+    ts(R("SC", 24, 32), R("S4i", 0, 8), col("PF", 24), ALU.is_equal)
 
-    def later_sends():
-        op("G", None, [], [R("z%d" % (myt - 1))])
-        hs, one = helpers_of(T, topo, core), hand_masks(T, topo, core)
-        lsum[0] += 3
-        op("G", lambda: g.remote_dma_fused([RemoteDMATransfer(
-            dst_ids=[dst(topo, hs[i])], dma_engine_mask=bits(one[i][:1]), remote_sem=T.sem.go) for i in range(3)],
-            local_sem=T.sem.lsem), [], [], sem="remote")
-        send(R("nxo"), "narr%d" % myt, T.nxd[rank])
 
     def late():
-        ms(R("rs4"), 1.0)
-        ts(R("I16"), R("If"), 16.0, ALU.mult)
-        ms(R("rs4", 0, 128, 4), 0.0)
-        ts(R("I64"), R("If"), 1.0 / 64, ALU.mult)
-        ts(R("Bh"), R("B1"), 0.5, ALU.mult)
-        ms(R("rst"), 1.0)
-        for gh, (p0, p1) in enumerate(halves):
-            ms(R("Hf", 128 * gh, 128 * gh + 128, 1, p0, p1), 1.0)
-            ms(R("Hf", 128 - 128 * gh, 256 - 128 * gh, 1, p0, p1), 0.0)
-        ms(R("X", 320, 336), 0.0)
-        ms(R("e8"), 0.0)
-        ms(R("th"), 0.0)
-        ts(R("PF", 18, 22), R("CI", 0, 4), col("PF", 22), ALU.add)
-        ms(R("rst", 0, 256, 64), 0.0)
-        ts(R("I2k"), R("If"), 2048.0, ALU.mult)
-        ts(R("I8k"), R("If"), 8192.0, ALU.mult)
-        ts(R("Dg"), R("If"), col("PF", 16), ALU.mult)
-        ts(R("Tri"), R("CI"), col("PF", 0), ALU.is_gt)
-        ts(R("SC", 32, 64), R("S4i"), col("PF", 10), ALU.is_equal)
-        ts(R("SC", 64, 96), R("S4i"), col("PF", 11), ALU.is_equal)
-        tt(R("Sd", 0, 24), R("SC", 8, 32), R("SC", 0, 24), ALU.subtract)
-        cp(R("Sd", 24, 32), R("SC", 0, 8))
-        ts(R("Lp", 0, 4), R("CI", 0, 4), 64.0, ALU.mult, 63.0, ALU.add)
-        ts(R("Lp", 4, 20), R("Pti", 4, 20), col("PF", 8), ALU.add)
-        ts(R("ta", 0, 2), R("CI", 0, 2), 4.0, ALU.mult, col("PF", 9), ALU.add)
-        for k in range(4):
-            cp(blk("Lth", k, 8), R("CI", 0, 8))
-        ts(R("ta", 2, 4), R("ta", 0, 2), 8.0, ALU.is_lt)
-        for k in range(4):
-            ts(blk("Lx", k, 8), R("CI", 0, 8), 16.0, ALU.mult, col("PF", 18 + k), ALU.add)
-        tt(R("ta", 4, 6), R("ta", 0, 2), R("ta", 2, 4), ALU.mult)
+        iota(R("ib"), [[0, 256]], 0, 1)
+        for n, a, b in (("X", 512, 528), ("incl", 256, 288), ("e8", 0, 16), ("th", 0, 16)):
+            iota(R(n, a, b), [[0, b - a]], 0)
+        sel(R("Tri"), R("ib", 0, 128), [[1, 128]], ALU.is_gt, 0, -1)
+        for w in sorted(set(WL)):
+            sel(R("rst%d" % w), R("ib"), [[0, 256 // w], [1, w]], ALU.is_gt, 0, 0)
+        if 64 in WL:
+            sel(blk("Hf", 0), R("ib", 0, 128), [[0, 128]], ALU.is_gt, 64, -1)
+            sel(blk("Hf", 1), R("ib", 0, 128), [[0, 128]], ALU.is_ge, -64, 1)
+        ts(R("Lm"), R("S4i"), 0.25, ALU.mult)
+        ts(R("SCb"), R("S4i", 0, 24), col("PF", 10), ALU.is_equal, col("PF", 11), ALU.mult)
+        ts(R("pd", 0, 32), R("S4i"), col("PF", 0), ALU.is_equal, 4.0, ALU.mult)
+        ts(R("pd", 32, 48), R("S4i", 0, 16), col("PF", 26), ALU.is_equal, 4.0, ALU.mult)
+        tt(R("Sd", 0, 24), R("pd", 8, 32), R("pd", 0, 24), ALU.subtract)
+        tt(R("pd", 48, 56), R("pd", 32, 40), R("pd", 40, 48), ALU.add)
+        ts(R("pd", 64, 96), R("Pti", 0, 32), col("PF", 8), ALU.add, col("PF", 23), ALU.mult)
+        ts(R("pd", 96, 128), R("Pti", 32, 64), col("PF", 27), ALU.mult)
+        tt(R("Sd", 24, 32), R("pd", 48, 56), R("pd", 0, 8), ALU.add)
+        tt(R("pd", 128, 160), R("pd", 64, 96), R("pd", 96, 128), ALU.add)
+        if 64 in WL:
+            ts(R("Lp64", 0, 32, 2), R("Pti", 64, 80), col("PF", 8), ALU.add)
+            cp(R("Lp64", 1, 32, 2), R("Pti", 32, 48))
+        cp(R("Lp32"), R("pd", 128, 160))
+        ts(R("ta", 0, 8), R("Pti", 144, 152), col("PF", 9), ALU.add)
+        cp(R("Lth"), R("Pti", 80, 112))
+        ts(R("ta", 8, 16), R("ta", 0, 8), 8.0, ALU.is_lt)
+        ts(R("Lx"), R("Pti", 112, 144), col("PF", 22), ALU.add)
+        tt(R("ta", 16, 24), R("ta", 0, 8), R("ta", 8, 16), ALU.mult)
         ts(R("BM"), R("BM"), col("PF", 4), ALU.not_equal, 16384.0, ALU.mult)
         ts(R("R12", 0, 32), R("CI", 0, 32), col("PF", 5), ALU.is_equal, 512.0, ALU.mult)
         ts(R("R12", 32, 64), R("CI", 0, 32), col("PF", 5), ALU.is_equal, 1024.0, ALU.mult)
-        for k in range(4):
-            cp(blk("Lw", k, 2), R("ta", 4, 6))
+        cp(R("Lw"), R("ta", 16, 24))
 
-    n0 = len(ops)
     late()
-    rest = ops[n0 + LATE:]
-    del ops[n0 + LATE:]
-    j0 = 64 - len(fill)
-    fill = masks() + [lambda o=o: ops.append(o) for o in rest]
-    lists_c()
+    hots_s(128 - NS0[0], 128)
     if myt == 1:
-        later_sends()
+        nx_out()
+    for _ in range(HU if myt > 1 else 0):
+        hot.pop(0)()
+    nx_in(0)
+
+    def go():
+        if myt != 1 or not (TWO or DIR):
+            return
+        op("G", None, [], [R(GON)])
+        told = sorted(set(x[0] for x in loads_of(T, rank)))
+        lsum[0] += len(told)
+        op("G", lambda: g.remote_dma_fused([RemoteDMATransfer(
+            dst_ids=[dst(topo, hs[i])], dma_engine_mask=bits(rest[i:i + 1]), remote_sem=T.sem.go) for i in told],
+            local_sem=T.sem.lsem), [], [], sem="remote")
+    u_in()
+    for _ in range(HV):
+        hot.pop(0)()
+    succ_a(0, 64)
+    for j in range(2):
+        act(blk("U5", j, 960), R("E", 0, 960), ACT.Identity, bias=1.0, scale=0.0)
+    hots_s(128 - NS0[0] - NS0[1], 128 - NS0[0])
+    succ_b()
+    act(R("U5", 0, 1920, 5), R("E", 0, 384), ACT.Identity, scale=0.0)
+    go()
+    act(R("N1"), R("ps1", 384, 512), ACT.Copy)
+    act(R("U5", 4, 1920, 5), R("ps5", 128, 512), ACT.Identity, scale=1.0 / 64)
+    if myt > 1:
+        nx_out()
+    for _ in range(HX + (24 if myt < 2 else 0)):
+        hot.pop(0)()
+    fill = masks(0)
+    lists_c()
+    for _ in range(HW):
+        hot.pop(0)()
     for t in range(3):
         gates(t)
         if t == 0:
-            for j in range(j0, 64):
-                act(blk("OHh", j), R("hi"), ACT.Abs, bias=-float(j), scale=1.0 / 64)
-            act(R("OHh", 128 * j0, 8192), R("OHh", 128 * j0, 8192), ACT.Relu, bias=1.0, scale=-1.0)
-        if t == 0 and myt == 2:
-            later_sends()
-        if t < 2:
-            nx_stage(t + 1)
+            for j in range(4):
+                act(blk("nxb", j, 1024), R("E", 0, 1024), ACT.Identity, bias=64.0, scale=0.0)
+            act(R("I2k"), R("Ibf"), ACT.Identity, scale=2048.0)
+            act(R("Dg"), R("Ibf"), ACT.Identity, scale=col("PF", 16))
+            act(R("Bh"), R("B1"), ACT.Identity, scale=0.5)
+            for w in sorted(set(WL)):
+                for j, v in enumerate((1.0 / w, 1024.0 / w, -1024.0 / w)):
+                    act(blk("I%d" % w, j), R("Ibf"), ACT.Identity, scale=v)
+            hots_s(128 - NS[0], 128 - NS0[0] - NS0[1])
         if t == 0:
-            fill.insert(NXAT, lambda: nx_in(1))
+            nx_in(1)
 
         def between():
             if t == 1:
+                op("Y", None, [], [R("Vw")])
                 nx_in(2)
             bound(t - 1)
-            terms_b(t - 1)
+            terms_b(t - 1, TB0, TB1)
+            masks(t)[0]()
             places_b()
-            fill.extend(masks())
         draw(t, fill, between)
         after_draw(t)
 
     marks_out(2)
-    terms_b(2)
-    act(R("tab", 0, 512), R("ps0"), ACT.Copy)
-    dma("Y", T.ye[:], T.tab[:, 0:512], "doe", 16, [], [R("tab", 0, 512)])
+    terms_c()
     for k in range(4):
         tt(R("dr", 384 + 128 * k, 512 + 128 * k), IND("pairb", 0, 128, "Lx", 8 * k, 8 * k + 8), R("BM"), ALU.add)
     for pr, n in enumerate(("G", "D1")):
         ms(R(n, 0, 16), 0.0)
-        tt(R(n, 16, 528), R("Y4", 2 * pr, 2048, 4), R("Y", 2 * pr, 2048, 4), ALU.subtract)
-        tt(R(n, 528, 1040), R("Y4", 2 * pr + 1, 2048, 4), R("Y", 2 * pr + 1, 2048, 4), ALU.subtract)
+        act(R(n, 16, 528), R("Y", 2 * pr, 2048, 4), ACT.Identity, scale=-1.0)
+        ts(R(n, 528, 1040), R("Y", 2 * pr + 1, 2048, 4), -1.0, ALU.mult)
         tt(R(n, 1040, 1552), R(n, 16, 528), R(n, 528, 1040), ALU.add)
     bound(2)
+    terms_d()
+    act(R("tab", 0, 512), R("ps0"), ACT.Copy)
+    dma("Y", T.ye[:], T.tab[:, 0:512], "doe", 16, [], [R("tab", 0, 512)])
     tt(R("OHh", 0, 512), IND("th", 0, 16, "Lth", 0, 32), R("dr", 384, 896), ALU.is_gt)
     for pr in range(2):
         o = R("ps2", 32 * pr, 32 * pr + 32)
@@ -748,6 +1028,7 @@ def emit(g, T, Q, ops, lsum):
     lw = {n: np.full(v[0], -1, np.int64) for n, v in SB.items()}
     rd = {n: {} for n in SB}
     bank = {}
+    pw = {}
     clock = {e: {} for e in Q}
     count = {e: 0 for e in Q}
     need = {e: set() for e in Q}
@@ -766,6 +1047,8 @@ def emit(g, T, Q, ops, lsum):
                 for e2, tk in bank.get(x[0], {}).items():
                     if e2 != e:
                         deps.add(tk)
+                if e != "P" and (x[0], e) in pw:
+                    deps.update(np.unique(pw[x[0], e][x[1]:x[2]:x[3]]).tolist())
             else:
                 deps.update(np.unique(lw[x[0]][x[1]:x[2]:x[3]]).tolist())
         for x in o["w"]:
@@ -813,6 +1096,7 @@ def emit(g, T, Q, ops, lsum):
                 lw[x[0]][x[1]:x[2]:x[3]] = tk
             else:
                 bank.setdefault(x[0], {})[e] = tk
+                pw.setdefault((x[0], e), np.full(512, -1, np.int64))[x[1]:x[2]:x[3]] = tk
     num = {e: {v: i + 1 for i, v in enumerate(sorted(need[e]))} for e in Q}
     for o in ops:
         e = o["e"]

@@ -8,51 +8,30 @@ ACT = ActivationFunctionType
 F, B, I, U = "float32", "bfloat16", "int32", "uint16"
 PW = 264
 DW = 6176
-HZ = 688
 MAG = 1.5 * 2.0 ** 23
-DN = ("Db", "D1", "D1")
-NV = (3, 3, 3)
-PAYAT = (2, 3)
-LCAT = (32, 80)
-SI = (False, True, True)
-XF = 0
-WL = (32, 64, 32)
-MKS = False
-VWS = False
-SUB = True
-Y4A = ((0, 128), (0, 24))
 CORES_IN_ALL = 128
-XR = True
-WHOLE = (False, True, True)
-DIR = True
-HZ1 = (2, 0, 0)
-XS = True
-MWAT = 2
-VW0 = (2, 2, 2)
-TB1 = 6
-TB0 = 0
-PLM = True
-DB = (1, 1, 0)
-NXE = False
-GA = 0
-MH = True
-TWO = False
-ORD = (0, 1, 2)
-GON = "G"
-OWN = False
-NXD = True
+DN = ("Db", "D1", "D1")
+WL = (32, 64, 32)
 ZA = (640, 768, 768)
-LATE = 70
-SPL = (0, 128)
+CARRY = ((0, 2, 1), (0, 0, 1), (0, 0, 0))
+NV = (3, 3, 3)
+NVH = (12, 12, 0)
+SI = (False, True, True)
+PAYAT = (2, 3)
+LCAT = (99, 86)
+Y4A = ((64, 96), (0, 24))
+SPL = (32, 128)
+PG = 16
 HU = 24
 HV = 12
 HX = 24
-HW = 0
-PF1 = (True, False, True)
-PLK = (0, 0, 0)
-UK = True
-NS0 = (8, 0)
-NS = (32, 0, 10)
+HF = 3
+LO0 = 8
+NS0 = 8
+NS = (32, 0, 6)
+TB1 = 6
+TBH = 2
+TB2 = 7
 
 SB = {
     "z0": (4096, B), "z1": (4096, B), "z2": (4096, B),
@@ -70,21 +49,22 @@ SB = {
     "miss": (384, B), "mk": (256, B), "incl": (288, B), "X": (528, B), "rst32": (256, B), "rst64": (256, B), "ib": (256, B),
     "C32": (128, B), "mc": (32, F), "Lm": (32, U), "Hf": (256, B),
     "Ln": (128, U), "Ls0": (128, U), "Ls1": (128, U), "Li": (128, U), "LT": (128, U), "Lc": (384, U),
-    "Lp32": (32, U), "Lp64": (32, U), "Lw": (8, U), "Lth": (32, U), "Lx": (32, U),
+    "Lp32": (32, U), "Lp64": (32, U), "Lw": (8, U), "Lg": (8, U), "Lth": (32, U), "Lx": (32, U),
     "CI": (128, F), "S4i": (32, F), "Pti": (152, F), "PIi": (4, I), "PJ": (8, I), "PF": (28, F), "BM": (128, F),
     "Ibf": (128, B), "If": (128, F), "I2k": (128, B), "I32": (384, B), "I64": (384, B), "Dg": (128, B),
-    "Ones": (128, B), "Tri": (128, B), "B1": (8, B), "Bh": (8, B), "SC": (32, F), "Sd": (32, B), "Su": (32, F), "R12": (64, B),
+    "Ones": (128, B), "Tri": (128, B), "B1": (8, B), "Bh": (8, B), "SC": (32, F), "Sd": (32, B), "Su": (32, F), "R12": (32, F),
+    "B16": (128, B), "Z3": (192, F), "r3": (192, B),
 }
 SCRATCH = {k: ("sbuf", [128, v[0]], v[1]) for k, v in SB.items()}
 SB["nxv"] = (6, F)
-SCRATCH["nxd"] = ("dram", [6, 2, 128, 512], B)
-SCRATCH["nxe"] = ("dram", [6, 128, 1024], B)
+SCRATCH["nxd"] = ("dram", [6, 128, 1024], B)
 for _i in range(8):
     SCRATCH["ps%d" % _i] = ("psum", [128, 512], F)
 SEMAPHORES = (["cV", "cS", "cP", "cG", "lsem", "dz", "dnx", "dhu", "duu", "dn0", "dx0", "doe", "dox"]
               + ["zarr%d" % t for t in range(3)] + ["narr%d" % t for t in range(3)]
-              + ["harr%d" % t for t in range(3)] + ["dw%d" % t for t in range(3)] + ["earr0", "earr1", "dox2", "go", "hm0", "hm1"] + ["h" + n for n in ("n", "z0", "z1", "z2")]
-              + ["r%s_%d_%d" % (n, q, j) for n in ("n", "z0", "z1", "z2") for q in range(6) for j in range(2)] + ["ga%d" % i for i in range(21)])
+              + ["harr%d" % t for t in range(3)] + ["dw%d" % t for t in range(3)]
+              + ["earr0", "earr1", "dox2", "go", "hm0", "hm1"] + ["h" + n for n in ("n", "z0", "z1", "z2")]
+              + ["r%s_%d" % (n, q) for n in ("n", "z0", "z1", "z2") for q in range(2, 6)] + ["ga%d" % i for i in range(14)])
 
 
 def bits(es):
@@ -114,23 +94,10 @@ def spread(T, topo, c):
     mates = [x for x in T.cores if mate(x, c)]
     far = [x for x in T.cores if x != c and x not in plane + mates]
     lone = [f for f in far if not any(mate(f, p) for p in plane)]
-    if WHOLE[T.rank_of(c) // 2]:
-        way = {p: {2: [f for f in far if mate(f, p)]} for p in plane}
-        way.update({twin(T, topo, f): {2: [f]} for f in lone})
-        way.update({x: {2: []} for x in mates})
-        return dict(sorted(way.items(), key=lambda x: not x[1][2]))
-    else:
-        way = {p: {j: [x for x in plane if x != p] + sorted((f for f in far if f not in lone), key=lambda f: mate(f, p))}
-               for j, p in enumerate(plane)}
-    if XR:
-        for x in mates:
-            way[x] = {j: [] for j in range(2)}
-        for f in lone:
-            way[twin(T, topo, f)] = {j: [f] for j in range(2)}
-        return way
-    for x in mates or lone:
-        way[x] = {j: lone if mates else [] for j in range(len(plane))}
-    return way
+    way = {p: [f for f in far if mate(f, p)] for p in plane}
+    way.update({twin(T, topo, f): [f] for f in lone})
+    way.update({x: [] for x in mates})
+    return dict(sorted(way.items(), key=lambda x: not x[1]))
 
 
 def twin(T, topo, c):
@@ -141,38 +108,12 @@ def twin(T, topo, c):
 
 def loads_of(T, q):
     t, out = q // 2, []
-    part = lambda x, a, w: lambda j: x[:, a + w * (j % 2):a + w * (j % 2) + w * (1 + j // 2)]
-    if t == 0:
-        half = part(T.nxs, 512 * q, 256)
-        out.append((1, "n", half, half, half, "narr0"))
-    else:
-        out.append((DB[t], "n", part(T.nxp, 0, 512), part(T.nxb, 1024 * (q - 2), 512),
-                    lambda j: T.nxd[q, j] if j < 2 else T.nxe[q], "narr%d" % t))
+    if t > 0:
+        out.append((CARRY[t][2], "n", T.nxp[:, :], T.nxb[:, 1024 * (q - 2):1024 * (q - 1)], T.nxd[q], "narr%d" % t))
     for i, (a, b) in enumerate(PIECE[t]):
-        w = (b - a) // 2
-        home = part(T["z%d" % t], 2048 * (q % 2) + a, w)
-        out.append(((0, HZ1[t], DB[t])[i], "z%d" % i, home, part(T.OHh, 2048 * q + a, w), home, "zarr%d" % t))
+        home = T["z%d" % t][:, 2048 * (q % 2) + a:2048 * (q % 2) + b]
+        out.append((CARRY[t][i], "z%d" % i, home, T.OHh[:, 2048 * q + a:2048 * q + b], home, "zarr%d" % t))
     return out
-
-
-def first_frame(T, q, step, die):
-    if step == 0:
-        return "rn_%d_0" % q, T.nxs[:, 512 * q + 256 * die:512 * q + 256 * die + 256], "narr0"
-    a = 2048 * q + 1024 * (step - 1) + 512 * die
-    return "rz%d_%d_0" % (step - 1, q), T.z0[:, a:a + 512], "zarr0"
-
-
-def first_step(g, T, topo, core, c, load):
-    die, name, src, mid, home, arr = load
-    way = spread(T, topo, c)
-    es = topo.engines(core, [d for d in T.cores if d != c][0])
-    h = len(es) // 2
-    to = lambda j: [x for x in way if j in way[x]]
-    g.remote_dma_fused([RemoteDMATransfer(
-        dst_ids=[dst(topo, helpers_of(T, topo, x)[die]) for x in to(j)], dma_engine_mask=bits(es[h * j:h * j + h] if j < 2 else es),
-        remote_sem=T.sem["r%s_%d_%d" % (name, T.rank_of(c), j % 2)], srcs=[src(j)], dsts=[mid(j) for _ in to(j)]) for j in range(3) if to(j)],
-        local_sem=T.sem.lsem)
-    return len(es)
 
 
 def helper_program(g, core, T, topo):
@@ -180,65 +121,41 @@ def helper_program(g, core, T, topo):
     if not mine:
         return
     me = mine[0]
-    die = helpers_of(T, topo, me).index(core)
-    home_rank = me in T.cores
+    which = helpers_of(T, topo, me).index(core)
+    rank = T.rank_of(me)
     es = topo.engines(core, [d for d in T.cores if d != me][0])
     rest = [e for e in topo.engines(core, me) if e not in es]
-    sent = 0
-    for step in range(1 if NXD else 0, 3 if TWO and die < 2 else 0):
-        for q in range(2):
-            c = T.cores[q]
-            if me in (c, twin(T, topo, c)):
-                name, x, arr = first_frame(T, q, step, die)
-                to = [d for d in T.cores if d != c and (d == me or topo.same_plane(topo.chip(d), topo.chip(me)))]
-                g.wait_ge(T.sem[name], len(es) // 2)
-                tr = [RemoteDMATransfer(dst_ids=[dst(topo, d) for d in ds], dma_engine_mask=bits(e), remote_sem=T.sem[arr],
-                                        srcs=[x], dsts=[x for _ in ds])
-                      for ds, e in (([d for d in to if d != me], es), ([d for d in to if d == me], rest)) if ds]
-                g.remote_dma_fused(tr, local_sem=T.sem.lsem)
-                sent += len(es) * len(tr)
-    if DIR and me in T.cores[:2]:
-        for _, name, src, mid, home, arr in [x for x in loads_of(T, T.rank_of(me))[1:] if x[0] == die]:
-            q = T.rank_of(me)
-            to = sorted(T.cores[q + 1:] + T.cores[:q], key=lambda d: topo.same_plane(topo.chip(d), topo.chip(me)) == (die == 0))
-            a, b = PIECE[0][int(name[1])]
-            x = T.z0[:, 2048 * q + a:2048 * q + b]
+    sent = [0]
+
+    def write(*parts):
+        parts = [x for x in parts if x[0]]
+        g.remote_dma_fused([RemoteDMATransfer(dst_ids=[dst(topo, d) for d in to], dma_engine_mask=bits(e), remote_sem=T.sem[sm],
+                                              srcs=[a], dsts=[b for _ in to]) for to, e, sm, a, b in parts], local_sem=T.sem.lsem)
+        sent[0] += sum(len(x[1]) for x in parts)
+
+    for t in range(3):
+        pair = [(T.cores[q], [x for x in loads_of(T, q) if x[0] == which]) for q in (2 * t, 2 * t + 1)]
+        for _, name, src, mid, home, arr in dict(pair).get(me, []):
+            if t == 1:
+                g.wait_ge(T.sem.go, 1)
             g.wait_ge(T.sem["h" + name], len(rest) // (2 if name in ("z0", "z1") else 1))
-            g.remote_dma_fused([RemoteDMATransfer(dst_ids=[dst(topo, d) for d in to], dma_engine_mask=bits(es), remote_sem=T.sem[arr],
-                                                  srcs=[x], dsts=[x for _ in to])], local_sem=T.sem.lsem)
-            sent += len(es)
-    for t in range(1 if TWO or DIR else 0, 3):
-        pair = [(T.cores[q], [x for x in loads_of(T, q) if x[0] == die]) for q in (2 * t, 2 * t + 1)]
-        for c, loads in pair:
-            if c == me and (t > 0 or die != 1 or not OWN):
-                for load in loads[1 if t == 0 and die == 1 else 0:]:
-                    if (TWO or DIR) and t == 1 and (load[1] != "n" or not NXE):
-                        g.wait_ge(T.sem.go, 1)
-                    g.wait_ge(T.sem["h" + load[1]], len(rest) // (2 if load[1] in ("z0", "z1") else 1))
-                    sent += first_step(g, T, topo, core, c, load)
-        for li in range(len(pair[0][1])):
+            if t == 0:
+                to = sorted(T.cores[rank + 1:] + T.cores[:rank], key=lambda d: topo.same_plane(topo.chip(d), topo.chip(me)) == (which == 0))
+                write((to, es, arr, src, home))
+            else:
+                write(([helpers_of(T, topo, x)[which] for x in spread(T, topo, me)], es, "r%s_%d" % (name, rank), src, mid))
+        for li in range(len(pair[0][1]) if t > 0 else 0):
             for c, loads in pair:
                 _, name, src, mid, home, arr = loads[li]
-                if arr == "narr0" and NXD:
-                    continue
-                for j, on in spread(T, topo, c).get(me, {}).items():
-                    g.wait_ge(T.sem["r%s_%d_%d" % (name, T.rank_of(c), j % 2)], len(es) // (2 - j // 2))
-                    tr = [RemoteDMATransfer(dst_ids=[dst(topo, me)], dma_engine_mask=bits(rest), remote_sem=T.sem[arr],
-                                            srcs=[mid(j)], dsts=[home(j)])] if home_rank else []
-                    if on:
-                        tr.append(RemoteDMATransfer(dst_ids=[dst(topo, d) for d in on], dma_engine_mask=bits(es), remote_sem=T.sem[arr],
-                                                    srcs=[mid(j)], dsts=[home(j) for _ in on]))
-                    g.remote_dma_fused(tr, local_sem=T.sem.lsem)
-                    sent += (len(rest) if home_rank else 0) + (len(es) if on else 0)
-    for t in range(2 if MH and die == 1 and home_rank else 0):
-        q = T.rank_of(me)
-        x, to = T.pay[:, (6 * t + q) * PW + 256:(6 * t + q) * PW + 264], T.cores[q + 1:] + T.cores[:q]
+                if me in spread(T, topo, c):
+                    g.wait_ge(T.sem["r%s_%d" % (name, T.rank_of(c))], len(es))
+                    write(([me] if rank is not None else [], rest, arr, mid, home), (spread(T, topo, c)[me], es, arr, mid, home))
+    for t in range(2 if which == 1 and rank is not None else 0):
+        x = T.pay[:, (6 * t + rank) * PW + 256:(6 * t + rank) * PW + 264]
         g.wait_ge(T.sem["hm%d" % t], len(rest))
-        g.remote_dma_fused([RemoteDMATransfer(dst_ids=[dst(topo, d) for d in to], dma_engine_mask=bits(es), remote_sem=T.sem["earr%d" % t],
-                                              srcs=[x], dsts=[x for _ in to])], local_sem=T.sem.lsem)
-        sent += len(es)
-    if sent:
-        g.wait_ge(T.sem.lsem, sent)
+        write((T.cores[rank + 1:] + T.cores[:rank], es, "earr%d" % t, x, x))
+    if sent[0]:
+        g.wait_ge(T.sem.lsem, sent[0])
 
 
 def rank_program(g, core, T, topo):
@@ -324,11 +241,11 @@ def rank_program(g, core, T, topo):
     noff = len(off)
     lsum = [0]
 
-    def send(src, sem, to=None):
+    def send(src, sem):
         lsum[0] += noff
         op("G", lambda: g.remote_dma_fused([RemoteDMATransfer(
             dst_ids=[dst(topo, d) for d in others], dma_engine_mask=bits(off), remote_sem=T.sem[sem],
-            srcs=[ap(src)], dsts=[ap(src) if to is None else to for _ in others])], local_sem=T.sem.lsem), [], [src], sem="remote")
+            srcs=[ap(src)], dsts=[ap(src) for _ in others])], local_sem=T.sem.lsem), [], [src], sem="remote")
 
     myt, myb = rank // 2, rank % 2
     zown = R("z%d" % myt, 2048 * myb, 2048 * myb + 2048)
@@ -385,7 +302,7 @@ def rank_program(g, core, T, topo):
         else:
             ts(R("nxp", 0, 512), R("nxi"), 64 * MAG, ALU.add, 64 * MAG, ALU.subtract)
             tt(R("nxp", 512, 1024), R("nxi"), R("nxp", 0, 512), ALU.subtract)
-            hand([(DB[myt], "hn", R("nxp"))])
+            hand([(CARRY[myt][2], "hn", R("nxp"))])
 
     hs = helpers_of(T, topo, core)
     rest = [e for e in topo.engines(core, hs[0]) if e not in off]
@@ -399,38 +316,15 @@ def rank_program(g, core, T, topo):
 
     def sends():
         piece = lambda i: R(zown[0], zown[1] + PIECE[myt][i][0], zown[1] + PIECE[myt][i][1])
-        loads = loads_of(T, rank)
-
-        def own(load, x):
-            lsum[0] += noff
-            op("G", lambda: first_step(g, T, topo, core, core, load), [], [x], sem="remote")
-        if myt == 0 and TWO:
-            h = noff // 2
-            for step in ORD:
-                if step == 0 and NXD:
-                    send(blk("nxs", rank, 512), "narr0")
-                    continue
-                lsum[0] += 2 * noff
-                op("G", lambda step=step: g.remote_dma_fused([RemoteDMATransfer(
-                    dst_ids=[dst(topo, helpers_of(T, topo, at)[d])], dma_engine_mask=bits(es[h * d:h * d + h]),
-                    remote_sem=T.sem[first_frame(T, rank, step, d)[0]], srcs=[first_frame(T, rank, step, d)[1]],
-                    dsts=[first_frame(T, rank, step, d)[1]]) for at, es in ((core, rest), (twin(T, topo, core), off)) for d in range(2)],
-                    local_sem=T.sem.lsem), [], [zown if step else blk("nxs", rank, 512)], sem="remote")
-            return
-        if myt == 0 and NXD:
+        if myt == 0:
             send(blk("nxs", rank, 512), "narr0")
-        elif myt == 0:
-            own(loads[0], blk("nxs", rank, 512))
-        hand([(0, "hz0", piece(0)), (HZ1[myt], "hz1", piece(1))])
-        if myt == 0 and OWN:
-            own(loads[3], piece(2))
-        else:
-            hand([(DB[myt], "hz2", piece(2))])
+        hand([(CARRY[myt][i], "hz%d" % i, piece(i)) for i in range(2)])
+        hand([(CARRY[myt][2], "hz2", piece(2))])
 
     for t in range(3):
         fz = [q for q in (2 * t, 2 * t + 1) if q != rank]
-        arrive("zarr%d" % t, (4 if t == 0 and TWO else 3 if t == 0 and DIR or WHOLE[t] else 6) * noff * len(fz), [blk("z%d" % t, q % 2, 2048) for q in fz])
-        arrive("narr%d" % t, (1 if t == 0 and NXD or WHOLE[t] else 2) * noff * len(fz), [blk("nxs", q, 512) if t == 0 else col("nxv", q) for q in fz])
+        arrive("zarr%d" % t, 3 * noff * len(fz), [blk("z%d" % t, q % 2, 2048) for q in fz])
+        arrive("narr%d" % t, noff * len(fz), [blk("nxs", q, 512) if t == 0 else col("nxv", q) for q in fz])
     if myt == 0:
         nx_out()
     sends()
@@ -443,6 +337,7 @@ def rank_program(g, core, T, topo):
     iota(R("Pti", 112, 144), [[1, 4], [16, 8]], 0)
     iota(R("Pti", 144, 152), [[0, 4], [4, 2]], 0)
     iota(R("BM"), [[0, 8], [1, 4], [0, 4]], 0)
+    iota(R("B16"), [[1, 8], [0, 16]], 0)
 
     for a in range(4):
         ts(R("D1", a, 512, 4), R("hu", 0, 128), col("PF", 12 + a), ALU.mult)
@@ -472,7 +367,6 @@ def rank_program(g, core, T, topo):
         for a in range(4):
             ts(R("D1", 512 + a, 2048, 4), R("hu", 128, 512), col("PF", 12 + a), ALU.mult)
         for kk in range(4, 16):
-            bl, k = kk // 4, kk % 4
             mm(blk("ps5", kk, 32), blk("D1", kk), R("Su"))
 
     def nx_in(t):
@@ -484,7 +378,7 @@ def rank_program(g, core, T, topo):
                     [blk("nxw", b, 2048)], [blk("nxf", b, 512)])
                 continue
             for i in range(2):
-                src, r = (T.nxp[:, 512 * i:512 * i + 512], R("nxp")) if q == rank else (T.nxe[q, :, 512 * i:512 * i + 512] if WHOLE[t] else T.nxd[q, i], col("nxv", q))
+                src, r = (T.nxp[:, 512 * i:512 * i + 512], R("nxp")) if q == rank else (T.nxd[q, :, 512 * i:512 * i + 512], col("nxv", q))
                 dma("Y", T.nxb[i:128:4, 2048 * b:2048 * b + 2048], src, "dw%d" % t, 64, [blk("nxb", b, 2048)], [r])
 
     act(R("Y"), IND("E", 0, 1024, "LT", 0, 128), ACT.Identity, scale=-1.0)
@@ -505,10 +399,9 @@ def rank_program(g, core, T, topo):
         mm(R("ps2", 256, 384), R("lo"), blk("I%d" % w, 1), False, False)
         for m in range(3):
             mm(R("ps2", 256, 384), blk("le%d" % (t % 2), m), blk("I%d" % w, 2), False, m == 2)
-        ts(R("Li"), R("ps2", 256, 384), 512.0 - 512.0 / w, ALU.add, 1023.0, ALU.min)
 
-    def masks(t):
-        return [lambda: ts(R("td"), R("live"), -16384.0, ALU.mult, 16384.0 - 3.5 - WL[t] / 2, ALU.add)]
+    def dead_mask(t):
+        ts(R("td"), R("live"), -16384.0, ALU.mult, 16384.0 - 3.5 - WL[t] / 2, ALU.add)
 
     def succ_a(t, split):
         w, n, l, o, sel = ("nxb", 4096, "Ln", "Gb", "SCb") if t > 0 else ("tab", 1024, "Li", "G", "SC")
@@ -527,17 +420,22 @@ def rank_program(g, core, T, topo):
         for m in range(3):
             mm(blk("ps3", m), blk("C1", m), R("If"))
 
-    def lists_c():
+    def lists_c(t=0):
+        if t != 1:
+            tt(R("Dc"), R("ps1", 128, 384), R("C1", 0, 256), ALU.subtract)
         ts(R("Lc"), R("ps3", 0, 384), -64.0, ALU.add)
+        if t == 1:
+            tt(R("Dc"), R("ps1", 128, 384), R("C1", 0, 256), ALU.subtract)
 
-    def chunk(t, ch, by_v):
-        d = R(DN[t], 16 + 1024 * ch, 16 + 1024 * ch + 1024)
-        w = IND("z%d" % t, 0, 4096, "Lc", 64 * ch, 64 * ch + 64)
+    def chunk(t, ch, by_v, a=0, b=64):
+        d = R(DN[t], 16 + 1024 * ch + 16 * a, 16 + 1024 * ch + 16 * b)
+        w = IND("z%d" % t, 0, 4096, "Lc", 64 * ch + a, 64 * ch + b)
+        y = R("Y", 1024 * (ch % 2) + 16 * a, 1024 * (ch % 2) + 16 * b)
         if by_v:
-            tt(d, w, blk("Y", ch % 2, 1024), ALU.add)
+            tt(d, w, y, ALU.add)
         else:
             act(d, w, ACT.Identity)
-            add(d, blk("Y", ch % 2, 1024))
+            add(d, y)
 
     def gate(t, m):
         big = 2 * MAG
@@ -554,20 +452,22 @@ def rank_program(g, core, T, topo):
             return
         for ch in (2 * m, 2 * m + 1):
             if ch == 5:
-                weights(t, 0, VW0[t])
+                weights(t, 0, 2)
             ts(blk("ind", ch, 1024), R(DN[t], 16 + 1024 * ch, 16 + 1024 * ch + 1024), big, ALU.add, big, ALU.is_equal)
         for r in range(16):
-            mm(wp(m, r), R("ind", 2048 * m + r, 2048 * m + 2048, 16), R("B1"))
+            o = wp(m, r) if m < 2 else R("ps3", 384 + 32 * (r % 4) + r // 4, 384 + 32 * (r % 4) + 32, 4)
+            mm(o, R("ind", 2048 * m + r, 2048 * m + 2048, 16), R("B1"))
 
     def weights(t, a, b):
         for i in range(a, b):
             if i == 0 and t > 0:
                 ts(R("e8", 0, 8), R("ps1", 16, 24), 1.0 / 2048, ALU.mult, 0.5 + 2.0 ** -12, ALU.add)
+                ts(R("Li"), R("ps2", 256, 384), 512.0 - 512.0 / WL[t - 1], ALU.add, 1023.0, ALU.min)
             elif i == 1 and t > 0:
                 ts(R("Vw", 0, 640, 5), IND("e8", 0, 16, "Lw", 0, 8), MAG, ALU.add, MAG, ALU.subtract)
             elif i > 1:
                 m = (1, 0, 2)[i - 2]
-                ts(R("Vw", m + 1, 640, 5), R("ps7", m + 1, 512, 4), 4.0 if SI[t] and m == 0 else -4.0, ALU.add, 0.0, ALU.max)
+                ts(R("Vw", m + 1, 640, 5), R("ps7", m + 1, 512, 4) if m < 2 else R("ps3", 384, 512), 4.0 if SI[t] and m == 0 else -4.0, ALU.add, 0.0, ALU.max)
 
     def terms_a(t):
         act(R("E"), R("Y4"), ACT.Abs, scale=4.0)
@@ -580,43 +480,52 @@ def rank_program(g, core, T, topo):
                 if h == 0:
                     mm(R("ps0"), R("If"), R("E", 0, 2048, 4), True, False)
             else:
-                mm(blk("ps0", h, 256), R("If"), R("E", 1024 * h + k, 1024 * h + 1024, 4), False, False)
+                mm(blk("ps0", h, 256), R("If"), R("E", 1024 * h + k, 1024 * h + 1024, 4), False, t == 2 and i == 7)
 
     def terms_c():
         for i in range(12):
             mm(R("ps1", 32, 64), R("Ibf"), R("miss", 128 * (i // 4) + i % 4, 128 * (i // 4) + 128, 4), i == 0, i == 11)
         act(R("mc"), R("ps1", 32, 64), ACT.Identity, scale=math.exp(-1.0) - 1.0)
         act(R("nxf", 0, 512), IND("mc", 0, 32, "Lm", 0, 32), ACT.Identity)
-        terms_b(2)
 
     def terms_d():
         for sl in range(4):
-            mm(R("ps0", sl, 512, 4), blk("nxf", sl), R("If"), False, sl == 3)
+            mm(R("ps0", sl, 512, 4), blk("nxf", sl), R("If"), False, False)
 
-    def bound(t):
-        for q in range(6):
-            b = (6 * t + q) * PW
-            mm(R("ps4", 0, 256), R("Ibf"), R("pay", b, b + 256), q == 0, q == 5)
+    begun = {}
+
+    def bound_a(t, i):
+        w = WL[t]
+        n = 256 // w
+        for j in range(begun.get(t, 0), i + 1):
+            if j == 0:
+                for q in range(6):
+                    b = (6 * t + q) * PW
+                    mm(R("ps4", 0, 256), R("Ibf"), R("pay", b, b + 256), q == 0, q == 5)
+                ts(R("mk"), R("ps4", 0, 256), 1.0, ALU.min)
+            if j == 1:
+                scan(R("incl", 0, 256), R("rst%d" % w), R("mk"))
+                for p0, p1 in [(0, 128)] if w == 32 else [(0, 64), (64, 128)]:
+                    mm(R("ps4", 384, 384 + n, 1, p0, p1), R("Tri", p0, p1, 1, p0, p1), R("incl", w - 1, 256, w, p0, p1))
+            if j == 2 and t < 2:
+                ts(R("incl", 256, 256 + n), R("ps4", 384, 384 + n), 32 * MAG, ALU.add, 32 * MAG, ALU.subtract)
+        begun[t] = max(begun.get(t, 0), i + 1)
+
+    def bound(t, extra=((), (), (), ())):
         w = WL[t]
         n = 256 // w
         parts = [(0, 128)] if w == 32 else [(0, 64), (64, 128)]
         rst = R("rst%d" % w)
-        if MKS:
-            act(R("mk"), R("ps4", 0, 256), ACT.Sign)
-        else:
-            ts(R("mk"), R("ps4", 0, 256), 1.0, ALU.min)
-        scan(R("incl", 0, 256), rst, R("mk"))
         pre = R("ps4", 384, 384 + n)
-        for p0, p1 in parts:
-            mm(R("ps4", 384, 384 + n, 1, p0, p1), R("Tri", p0, p1, 1, p0, p1), R("incl", w - 1, 256, w, p0, p1))
+        bound_a(t, 2)
+        if t == 2:
+            terms_b(2, TB2)
+            act(R("tab", 0, 512), R("ps0"), ACT.Copy)
+            dma("S", T.ye[:], T.tab[:, 0:512], "doe", 16, [], [R("tab", 0, 512)])
 
         def digits():
-            ts(R("incl", 256, 256 + n), pre, 32 * MAG, ALU.add, 32 * MAG, ALU.subtract)
             tt(R("incl", 264, 264 + n), pre, R("incl", 256, 256 + n), ALU.subtract)
-            if XS:
-                act(R("X", 0, 512), IND("incl", 0, 288, "Lp%d" % w, 0, 32), ACT.Identity)
-            else:
-                cp(R("X", 0, 512), IND("incl", 0, 288, "Lp%d" % w, 0, 32))
+            act(R("X", 0, 512), IND("incl", 0, 288, "Lp%d" % w, 0, 32), ACT.Identity)
 
         def table():
             for tl in range(w // 4):
@@ -624,30 +533,33 @@ def rank_program(g, core, T, topo):
                     c, st = (p1 - p0) * tl, w // 8
                     mm(R("ps%d" % (5 + c // 512), c % 512, c % 512 + p1 - p0, 1, p0, p1),
                        R("X", tl, tl + 512 - st + 1, st, p0, p1), R("Ibf", p0, p1, 1, p0, p1))
-        if t < 2 and XF == 0:
-            digits()
         for gi in range(n):
+            if t < 2 and gi == 2:
+                digits()
             ts(blk("ib", gi, w), blk("incl", gi, w), col("ps4", 384 + gi), ALU.add, 1024.0, ALU.is_le)
+        if t == 2:
+            for j in range(2):
+                mm(col("ps1", 0), R("ib", j, 256, 2), col("Ones", 0), j == 0, j == 1)
+            cp(col("mk", 0), col("ps1", 0))
+            mm(col("ps1", 1), R("B16"), col("mk", 0))
+            return
+        for f in extra[0]:
+            f()
         scan(R("mk"), rst, R("ib"))
+        for f in list(extra[1]) + list(extra[2]):
+            f()
         for h, (p0, p1) in enumerate(parts):
             mm(R("ps1", n * h, n * h + n), R("Ones") if w == 32 else blk("Hf", h), R("mk", w - 1, 256, w))
-        if t < 2 and XF == 1:
-            digits()
-        if t < 2:
-            terms_b(t, 0, TB0)
-            table()
+        table()
         cp(R("th", 0, 8), R("ps1", 0, 8))
-        if t < 2:
-            tt(R("live"), IND("th", 0, 16, "Lth", 0, 8), R("pairb"), ALU.is_gt)
-
+        for f in extra[3]:
+            f()
+        tt(R("live"), IND("th", 0, 16, "Lth", 0, 8), R("pairb"), ALU.is_gt)
 
     def misses_out(t):
         b = (6 * t + rank) * PW + 256
         act(R("pay", b, b + 8), R("ps4", 256, 264), ACT.Copy)
-        if MH:
-            hand([(1, "hm%d" % t, R("pay", b, b + 8))])
-        else:
-            send(R("pay", b, b + 8), "earr%d" % t)
+        hand([(1, "hm%d" % t, R("pay", b, b + 8))])
         arrive("earr%d" % t, 5 * noff, [R("pay", (6 * t + q) * PW + 256, (6 * t + q) * PW + 264) for q in range(6) if q != rank])
 
     def miss_weight(t):
@@ -658,7 +570,10 @@ def rank_program(g, core, T, topo):
     def places_b():
         act(R("tabb", 0, 512), R("ps5"), ACT.Copy)
         act(R("tabb", 512, 1024), R("ps6"), ACT.Copy)
-        act(R("Gb"), IND("tabb", 0, 1024, "Li", 0, 128), ACT.Identity)
+        act(R("Gb", 0, 2048 - 16 * PG), IND("tabb", 0, 1024, "Li", 0, 128 - PG), ACT.Identity)
+
+    def places_v():
+        cp(R("Gb", 2048 - 16 * PG, 2048), IND("tabb", 0, 1024, "Li", 128 - PG, 128))
         for r in range(16):
             mm(R("ps3", r, 384, 16), R("Gb", r, 2048, 16), R("Sd", 0, 24))
         mm(R("ps6", 0, 128), R("Ibf"), R("td"), True, False)
@@ -668,18 +583,20 @@ def rank_program(g, core, T, topo):
     def places_c(t):
         tt(R("pb"), R("ps3", 0, 384), R("le%d" % (t % 2)), ALU.mult)
 
-    def draw(t, fill, between):
+    def draw(t, between):
         le = "le%d" % (t % 2)
         sl = lambda n, m, k: R(n, 128 * m + k, 128 * m + 128, 4)
-        lazy = []
 
-        def gap(n):
-            done = 0
-            while lazy and done < n:
-                lazy.pop(0)()
-                done += 1
-            if not done and fill:
-                fill.pop(0)()
+        def gap(n, calls=()):
+            for f in calls:
+                f()
+            for _ in range(max(0, n - len(calls)) if t == 0 else 0):
+                if len(hot) > NS[0]:
+                    hot.pop(0)()
+
+        def idle(i):
+            if t > 0:
+                bound_a(t - 1, i)
 
         def ne(j, k, m, x=None, y=None):
             b = 96 * (j * (7 - j) // 2 + k - j - 1) + 32 * m
@@ -690,69 +607,70 @@ def rank_program(g, core, T, topo):
             v = R("Vw", 160 * k + m + 1, 160 * k + 160, 5)
             tt(v, v, R("ne", b, b + 32), ALU.mult)
 
-        weights(t, VW0[t], 5)
-        gap(1)
+        weights(t, 2, 5)
+        if t == 0:
+            dead_mask(0)
+        nes = lambda j, k: [lambda m=m: ne(j, k, m) for m in range(3)]
+        muls = lambda j, k: [lambda m=m: mul(j, k, m) for m in range(3)]
+        later = {(1, 0): nes(0, 2), (1, 1): muls(0, 2), (1, 2): nes(0, 3), (1, 4): muls(0, 3), (2, 0): nes(1, 3), (2, 1): muls(1, 3)}
+
+        def wait(k, i, n):
+            gap(n, later.get((k, i), []))
+        gap(HF)
         for k in range(4):
             b0 = 384 * (k % 3)
             d = lambda i: R("dr", b0 + 32 * i, b0 + 32 * i + 32)
             pm = lambda m: R("Pm", 160 * k + m, 160 * k + 160, 5)
-            n = 2 * k
             scan(blk("Pm", k, 160), blk("U5", 4 * t + k, 160), blk("Vw", k, 160))
-            gap(n + GA)
-            if t > 0 and k == 3 and PLK[t] == 4:
-                places_c(t - 1)
+            wait(k, 0, HF + 1)
+            if k == 0:
+                idle(0)
             for m in range(3):
                 tt(sl(le, m, k), pm(m), pm(4), ALU.is_le)
             if t == 2 and k == 3:
-                if PLK[t] == 3:
-                    places_c(t - 1)
                 break
+            gap(HF - 2)
             tt(d(5), sl(le, 0, k), sl("C1", 0, k), ALU.mult)
             tt(d(6), sl(le, 1, k), sl("Dc", 0, k), ALU.mult)
             tt(d(7), sl(le, 2, k), sl("Dc", 1, k), ALU.mult)
-            if 0 < k < 3:
-                gap(n - GA)
+            if k == 3:
+                tt(blk("miss", t), R("live"), blk(le, 0), ALU.is_gt)
+            else:
+                wait(k, 1, HF - 1)
+            if k == 0:
+                idle(1)
             tt(d(8), d(5), d(6), ALU.add)
+            if k == 0:
+                idle(2)
             if k == 0 and t > 0:
                 tt(sl("took", 0, k), d(8), d(7), ALU.add)
-                between()
-                tt(sl("took", 0, 0), sl("took", 0, 0), sl("live", 0, 0), ALU.mult)
+                between([nes(0, 1), [lambda: ts(R("dr", 288, 384), R("ne", 0, 96), 16384.0, ALU.mult)],
+                         [lambda m=m: tt(d(m), d(9 + m), sl("pairb", 0, 0), ALU.max) for m in range(3)],
+                         [lambda: tt(R("ne", 0, 96), IND("th", 0, 16, "Lg", 0, 6), R("dr", 0, 96), ALU.is_le)]])
                 u5 = lambda k2: R("U5", 640 * t + 160 * k2 + 4, 640 * t + 160 * k2 + 160, 5)
-                um = lambda k2: tt(u5(k2), u5(k2), sl("live", 0, k2), ALU.mult)
-                um(1)
-                for m in range(3):
-                    ne(k, k + 1, m)
                 for m in range(3):
                     mul(k, k + 1, m)
-                um(2)
-            elif k < 3 and not SUB:
-                tt(sl("took", 0, k), d(8), d(7), ALU.add)
-                for m in range(3):
-                    ne(k, k + 1, m)
-                for m in range(3):
-                    mul(k, k + 1, m)
+                tt(u5(1), u5(1), sl("live", 0, 1), ALU.mult)
+                tt(sl("took", 0, 0), sl("took", 0, 0), sl("live", 0, 0), ALU.mult)
+                tt(u5(2), u5(2), sl("live", 0, 2), ALU.mult)
+                dead_mask(t)
+                places_b()
             elif k < 3:
                 for m in range(3):
                     tt(d(9 + m), sl("C1", m, k + 1), d(7), ALU.subtract)
+                wait(k, 2, HF - 2)
                 for m in range(3):
                     ne(k, k + 1, m, d(9 + m), d(8))
-                if k > 0:
-                    gap(n)
+                tt(sl("took", 0, k), d(8), d(7), ALU.add)
+                wait(k, 3, HF - 3)
                 for m in range(3):
                     mul(k, k + 1, m)
-                tt(sl("took", 0, k), d(8), d(7), ALU.add)
+                wait(k, 4, HF)
+                if t > 0 and k == 1:
+                    places_v()
             else:
-                gap(1)
+                tt(R("tc"), blk("miss", t), R("N1"), ALU.mult)
                 tt(sl("took", 0, k), d(8), d(7), ALU.add)
-            for k2 in range(k + 2, 4):
-                lazy += [lambda m=m, k2=k2, k=k: ne(k, k2, m) for m in range(3)]
-                lazy += [lambda m=m, k2=k2, k=k: mul(k, k2, m) for m in range(3)]
-            if t > 0 and k == PLK[t] > 0:
-                places_c(t - 1)
-
-        assert not lazy
-        while fill:
-            fill.pop(0)()
 
     def marks_out(t):
         b = (6 * t + rank) * PW
@@ -774,22 +692,23 @@ def rank_program(g, core, T, topo):
             parts += [(R("Ibf"), blk(le, m)) for m in range(3)] + [(R("Ibf"), blk("pb", m)) for m in range(3 if t > 0 else 0)]
             for i, (a, b) in enumerate(parts):
                 mm(pr, a, b, i == 0 and t == 0, i == len(parts) - 1)
-        if PLK[t] or t == 0:
+        if t == 2:
+            places_c(t - 1)
+        if t != 1:
             pair_sum()
-        if t < 2:
-            tt(blk("miss", t), R("live"), blk(le, 0), ALU.is_gt)
-            tt(R("tc"), blk("miss", t), R("N1"), ALU.mult)
         for m in range(3):
             mm(R("ps2", 128, 256), blk(le, m), R("I2k"), m == 0, False)
         mm(R("ps2", 128, 256), R("td"), R("Ibf"), False, False)
         mm(R("ps2", 128, 256), R("Ones"), R("Dg"), False, True)
         if t < 2:
-            mm(R("ps2", 0, 128), R("took"), R("If"), True, False)
-            mm(R("ps2", 0, 128), R("tc"), R("If"), False, True)
+            mm(R("ps2", 0, 128), R("tc"), R("If"), True, False)
+            mm(R("ps2", 0, 128), R("took"), R("If"), False, True)
 
-        if t > 0 and not PLK[t]:
+        if t == 1:
             places_c(t - 1)
             pair_sum()
+        if t == 2:
+            tt(blk("miss", t), R("live"), blk(le, 0), ALU.is_gt)
         if t > 0:
             terms_b(t - 1, TB1)
 
@@ -797,8 +716,10 @@ def rank_program(g, core, T, topo):
             if t > 0:
                 ts(R("hi"), pr, w * MAG, ALU.add, w * MAG, ALU.subtract)
             tt(R("lo"), pr, R("hi"), ALU.subtract)
-        if PF1[t]:
+        if t != 1:
             pairs()
+        for j in range(LO0 if t == 0 else 0):
+            ts(blk("OHl", j), R("lo"), j - 15.5, ALU.is_equal)
         if t < 2:
             ts(R("Ln"), R("ps2", 0, 128), -64.0, ALU.add)
         ts(R(ls), R("ps2", 128, 256), col("PF", 6 if w == 32 else 25), ALU.add, float(DW - 16), ALU.min)
@@ -820,40 +741,40 @@ def rank_program(g, core, T, topo):
             y4(Y4A[t][1])
             succ_b()
             y4(128)
-        if not PF1[t]:
+        if t == 1:
             pairs()
         c0 = 128 - len(hot) if t == 0 else 0
         if w == 32:
-            f = [lambda j=j: ts(blk("OHl", j), R("lo"), j - 15.5, ALU.is_equal) for j in range(32)]
+            f = [lambda j=j: ts(blk("OHl", j), R("lo"), j - 15.5, ALU.is_equal) for j in range(LO0 if t == 0 else 0, 32)]
             f += hots()[c0:128 - NS[t]]
         else:
             f = [lambda j=j: ts(blk("OHh", j), R("hi"), 64.0 * j, ALU.is_equal) for j in range(64)]
             f += [lambda j=j: ts(blk("OHh", 64 + j), R("lo"), j - 31.5, ALU.is_equal) for j in range(64)]
-        if t > 0:
-            hots_s(128 - NS[t])
         if t == 2:
             act(R("Y4"), IND(dd, 0, DW, ls, 0, 128), ACT.Identity, scale=-0.25)
             add(R("Y"), R("Y4"))
             terms_a(2)
+            hots_s(128 - NS[t])
+            terms_c()
         for i, fn in enumerate(f):
             if t < 2 and i == LCAT[t]:
-                lists_c()
+                lists_c(t)
             fn()
+        ts(R("pairb"), pr, w / 2 - 0.5, ALU.add)
+        if t == 0:
+            tt(R("N1"), R("tc"), R("took"), ALU.add)
         if t < 2 and LCAT[t] >= len(f):
             lists_c()
         late_g = [gi for gi in range(8) if 16 * gi + 16 > c0 and 16 * gi < 128 - NS[t]] if t == 0 else []
         for c in [16 * gi + r for gi in sorted(range(8), key=lambda gi: gi in late_g) for r in range(16)]:
+            if t == 2 and c % 16 == 0 and c >= 128 - 16 * TBH:
+                terms_b(2, c // 16 - 8 + TBH, c // 16 - 7 + TBH)
             if w == 32:
                 mm(R("ps4", 32 * (c // 16), 32 * (c // 16) + 32), blk("OHh", c), R("OHl", c, 4096, 128), c % 16 == 0, c % 16 == 15)
             else:
                 gh, gl = c // 64, c // 16 % 4
                 mm(R("ps4", 64 * gl, 64 * gl + 64, 1, 64 * gh, 64 * gh + 64), R("OHh", c, 8192, 128),
                    R("OHh", 8192 + c, 16384, 128), c % 16 == 0, c % 16 == 15)
-        if t == 2:
-            tt(blk("miss", t), R("live"), blk(le, 0), ALU.is_gt)
-        ts(R("pairb"), pr, w / 2 - 0.5, ALU.add)
-        if t == 0:
-            tt(R("N1"), R("tc"), R("took"), ALU.add)
 
     def gates(t):
         sent = t == 0
@@ -861,14 +782,15 @@ def rank_program(g, core, T, topo):
             if not sent and i == PAYAT[t - 1]:
                 marks_out(t - 1)
                 sent = True
-            chunk(t, ch, False)
+            chunk(t, ch, False, 0, 64 - NVH[t] if ch == 5 else 64)
         if not sent:
             marks_out(t - 1)
-        tt(R("Dc"), R("ps1", 128, 384), R("C1", 0, 256), ALU.subtract)
         for ch in sorted(range(NV[t]), key=lambda ch: ch % 2):
             chunk(t, ch, True)
+        if NVH[t]:
+            chunk(t, 5, True, 64 - NVH[t], 64)
         for i, m in enumerate((0, 1, 3, 2)):
-            if t > 0 and i == MWAT:
+            if t > 0 and i == 2:
                 place_list(t - 1)
                 miss_weight(t - 1)
             gate(t, m)
@@ -895,12 +817,12 @@ def rank_program(g, core, T, topo):
         ms(R(d, DW - 16, DW), 4000.0)
     ts(R("SC", 24, 32), R("S4i", 0, 8), col("PF", 24), ALU.is_equal)
 
-
     def late():
         iota(R("ib"), [[0, 256]], 0, 1)
         for n, a, b in (("X", 512, 528), ("incl", 256, 288), ("e8", 0, 16), ("th", 0, 16)):
             iota(R(n, a, b), [[0, b - a]], 0)
         sel(R("Tri"), R("ib", 0, 128), [[1, 128]], ALU.is_gt, 0, -1)
+        sel(R("r3"), R("ib", 0, 192), [[0, 64], [1, 3]], ALU.is_gt, 0, 0)
         for w in sorted(set(WL)):
             sel(R("rst%d" % w), R("ib"), [[0, 256 // w], [1, w]], ALU.is_gt, 0, 0)
         if 64 in WL:
@@ -925,13 +847,16 @@ def rank_program(g, core, T, topo):
         ts(R("ta", 8, 16), R("ta", 0, 8), 8.0, ALU.is_lt)
         ts(R("Lx"), R("Pti", 112, 144), col("PF", 22), ALU.add)
         tt(R("ta", 16, 24), R("ta", 0, 8), R("ta", 8, 16), ALU.mult)
-        ts(R("BM"), R("BM"), col("PF", 4), ALU.not_equal, 16384.0, ALU.mult)
-        ts(R("R12", 0, 32), R("CI", 0, 32), col("PF", 5), ALU.is_equal, 512.0, ALU.mult)
-        ts(R("R12", 32, 64), R("CI", 0, 32), col("PF", 5), ALU.is_equal, 1024.0, ALU.mult)
+        ts(R("BM"), R("BM"), col("PF", 4), ALU.is_equal)
+        ts(R("R12"), R("CI", 0, 32), col("PF", 5), ALU.is_equal)
+        ts(R("B16"), R("B16"), col("PF", 2), ALU.is_equal)
+        ts(R("Z3", 0, 96, 3), R("CI", 0, 32), 16.0, ALU.mult)
+        ts(R("Z3", 96, 192, 3), R("CI", 0, 32), 16.0, ALU.mult)
         cp(R("Lw"), R("ta", 16, 24))
+        ts(R("Lg"), R("ta", 0, 8), -1.0, ALU.add)
 
     late()
-    hots_s(128 - NS0[0], 128)
+    hots_s(128 - NS0, 128)
     if myt == 1:
         nx_out()
     for _ in range(HU if myt > 1 else 0):
@@ -939,9 +864,9 @@ def rank_program(g, core, T, topo):
     nx_in(0)
 
     def go():
-        if myt != 1 or not (TWO or DIR):
+        if myt != 1:
             return
-        op("G", None, [], [R(GON)])
+        op("G", None, [], [R("G")])
         told = sorted(set(x[0] for x in loads_of(T, rank)))
         lsum[0] += len(told)
         op("G", lambda: g.remote_dma_fused([RemoteDMATransfer(
@@ -953,23 +878,19 @@ def rank_program(g, core, T, topo):
     succ_a(0, 64)
     for j in range(2):
         act(blk("U5", j, 960), R("E", 0, 960), ACT.Identity, bias=1.0, scale=0.0)
-    hots_s(128 - NS0[0] - NS0[1], 128 - NS0[0])
     succ_b()
     act(R("U5", 0, 1920, 5), R("E", 0, 384), ACT.Identity, scale=0.0)
     go()
     act(R("N1"), R("ps1", 384, 512), ACT.Copy)
-    act(R("U5", 4, 1920, 5), R("ps5", 128, 512), ACT.Identity, scale=1.0 / 64)
     if myt > 1:
         nx_out()
     for _ in range(HX + (24 if myt < 2 else 0)):
         hot.pop(0)()
-    fill = masks(0)
     lists_c()
-    for _ in range(HW):
-        hot.pop(0)()
     for t in range(3):
         gates(t)
         if t == 0:
+            act(R("U5", 4, 1920, 5), R("ps5", 128, 512), ACT.Identity, scale=1.0 / 64)
             for j in range(4):
                 act(blk("nxb", j, 1024), R("E", 0, 1024), ACT.Identity, bias=64.0, scale=0.0)
             act(R("I2k"), R("Ibf"), ACT.Identity, scale=2048.0)
@@ -978,41 +899,34 @@ def rank_program(g, core, T, topo):
             for w in sorted(set(WL)):
                 for j, v in enumerate((1.0 / w, 1024.0 / w, -1024.0 / w)):
                     act(blk("I%d" % w, j), R("Ibf"), ACT.Identity, scale=v)
-            hots_s(128 - NS[0], 128 - NS0[0] - NS0[1])
-        if t == 0:
+            hots_s(128 - NS[0], 128 - NS0)
             nx_in(1)
 
-        def between():
+        def between(extra):
             if t == 1:
                 op("Y", None, [], [R("Vw")])
                 nx_in(2)
-            bound(t - 1)
-            terms_b(t - 1, TB0, TB1)
-            masks(t)[0]()
-            places_b()
-        draw(t, fill, between)
+            bound(t - 1, extra)
+            terms_b(t - 1, 0, TB1)
+        draw(t, between)
         after_draw(t)
 
     marks_out(2)
-    terms_c()
+    terms_b(2, TBH, TB2)
+    terms_d()
     for k in range(4):
-        tt(R("dr", 384 + 128 * k, 512 + 128 * k), IND("pairb", 0, 128, "Lx", 8 * k, 8 * k + 8), R("BM"), ALU.add)
+        tt(R("dr", 384 + 128 * k, 512 + 128 * k), IND("pairb", 0, 128, "Lx", 8 * k, 8 * k + 8), R("BM"), ALU.mult)
+        mm(blk("ps2", 2 * (k % 2) + k // 2, 32), R("dr", 384 + 128 * k, 512 + 128 * k), R("R12"))
     for pr, n in enumerate(("G", "D1")):
         ms(R(n, 0, 16), 0.0)
         act(R(n, 16, 528), R("Y", 2 * pr, 2048, 4), ACT.Identity, scale=-1.0)
-        ts(R(n, 528, 1040), R("Y", 2 * pr + 1, 2048, 4), -1.0, ALU.mult)
+        act(R(n, 528, 1040), R("Y", 2 * pr + 1, 2048, 4), ACT.Identity, scale=-1.0)
         tt(R(n, 1040, 1552), R(n, 16, 528), R(n, 528, 1040), ALU.add)
     bound(2)
-    terms_d()
-    act(R("tab", 0, 512), R("ps0"), ACT.Copy)
-    dma("Y", T.ye[:], T.tab[:, 0:512], "doe", 16, [], [R("tab", 0, 512)])
-    tt(R("OHh", 0, 512), IND("th", 0, 16, "Lth", 0, 32), R("dr", 384, 896), ALU.is_gt)
-    for pr in range(2):
-        o = R("ps2", 32 * pr, 32 * pr + 32)
-        mm(o, blk("OHh", 2 * pr), R("R12", 0, 32), True, False)
-        mm(o, blk("OHh", 2 * pr + 1), R("R12", 32, 64), False, False)
-        mm(o, R("Ones"), R("Dg", 0, 32), False, True)
-    ts(R("Ln", 0, 64), R("ps2", 0, 64), col("PF", 17), ALU.add)
+    for j in range(2):
+        ts(R("Z3", j + 1, 192, 3), blk("ps2", j, 64), col("ps1", 1), ALU.is_lt, 512.0 * (j + 1), ALU.mult)
+    scan(R("dr", 0, 192), R("r3"), R("Z3"))
+    ts(R("Ln", 0, 64), R("dr", 2, 192, 3), col("PF", 17), ALU.add)
     for h in range(2):
         act(blk("Y4", h, 256), IND("G", 0, 1552, "Ln", 16 * h, 16 * h + 16), ACT.Identity)
     for h in range(2):

@@ -1,4 +1,3 @@
-import math
 import numpy as np
 from concourse.bass import DstId, RemoteDMATransfer
 from concourse.mybir import AluOpType, ActivationFunctionType
@@ -14,45 +13,56 @@ DN = ("Db", "D1", "D1")
 WL = (32, 64, 32)
 ZA = (640, 768, 768)
 CARRY = ((0, 2, 1), (0, 0, 1), (0, 0, 0))
-NV = (3, 3, 3)
-NVH = (12, 12, 0)
-SI = (False, True, True)
-PAYAT = (2, 3)
+NV = (3, 4, 4)
+NVH = (12, 0, 0)
+SI = ((), (0, 2, 1), (0, 2, 1))
+TESTS = ((0, 1, 6, 2, 3, 7, 4, 5, 8), (4, 3, 7, 5, 6, 8), (4, 3, 7, 5, 6, 8))
+PAYAT = ((2, 2), (3, 2))
 LCAT = (99, 86)
-Y4A = ((64, 96), (0, 24))
-SPL = (32, 128)
+Y4A = ((64, 96), (48, 64))
+Y4V = ((0, 0), (0, 0))
+MH = (None, None, None)
+SPL = (48, 128)
 PG = 16
-HU = 24
-HV = 12
-HX = 24
+HU = 30
+HV = 24
+HX = (4, 24, 0)
 HF = 3
 LO0 = 8
-NS0 = 8
-NS = (32, 0, 6)
-TB1 = 6
-TBH = 2
-TB2 = 7
+NS0 = (2, 8, 8)
+NS = (48, 0, 32)
+TA = 1024
+TB3 = 4
+TB1 = 4
+HELD = ("ps5", "ps7", "ps1")
+SUM0 = 352
+TABS = ("G", "nxw")
+D9 = True
+WIDE = False
+AH = (1, 0)
+TB2 = 4
+YV = 32
 
 SB = {
     "z0": (4096, B), "z1": (4096, B), "z2": (4096, B),
-    "nxi": (512, I), "nxs": (1024, U), "nxp": (1024, B), "nxf": (1024, F), "nxw": (4096, F), "nxb": (4096, B), "Gb": (2048, B),
-    "SCb": (24, B),
-    "hu": (512, I), "n0l": (64, I),
+    "nxi": (512, I), "nxs": (1024, U), "nxp": (1024, B), "nxw": (4096, F), "nxb": (4096, B), "Gb": (2048, B),
+    "SCb": (24, B), "SDb": (24, B), "SD": (24, F),
+    "hu": (512, I), "n0w": (1024, I),
     "D1": (DW, F), "ind": (6144, B), "OHh": (16384, B), "OHl": (4096, B),
     "Y": (2048, F), "Y4": (2048, F), "G": (2048, F), "Db": (DW, B), "E": (2048, F),
     "tab": (1024, F), "pay": (18 * PW, B),
-    "U5": (1920, B), "C1": (384, F), "Dc": (256, F), "Vw": (640, B), "Pm": (640, F), "le0": (384, B), "le1": (384, B),
+    "U5": (1920, B), "C1": (384, F), "Vw": (640, B), "Pm": (640, F), "le0": (384, B), "le1": (384, B),
     "N1": (128, F), "live": (128, B), "took": (128, F), "T1": (128, F),
     "ta": (128, F), "tc": (128, F), "td": (128, B), "pairb": (128, F), "tabb": (1024, B),
     "dr": (3 * 384, F), "ne": (6 * 96, F), "e8": (16, F), "th": (16, F),
     "pd": (160, F), "pb": (384, B), "hi": (128, B), "lo": (128, B),
     "miss": (384, B), "mk": (256, B), "incl": (288, B), "X": (528, B), "rst32": (256, B), "rst64": (256, B), "ib": (256, B),
-    "C32": (128, B), "mc": (32, F), "Lm": (32, U), "Hf": (256, B),
+    "C32": (128, B), "C16": (128, B), "Df": (128, F), "mc": (32, F), "Lm": (32, U), "Hf": (256, B),
     "Ln": (128, U), "Ls0": (128, U), "Ls1": (128, U), "Li": (128, U), "LT": (128, U), "Lc": (384, U),
     "Lp32": (32, U), "Lp64": (32, U), "Lw": (8, U), "Lg": (8, U), "Lth": (32, U), "Lx": (32, U),
-    "CI": (128, F), "S4i": (32, F), "Pti": (152, F), "PIi": (4, I), "PJ": (8, I), "PF": (28, F), "BM": (128, F),
+    "CI": (128, F), "S4i": (32, F), "Pti": (152, F), "PIi": (4, I), "PJ": (8, I), "PF": (32, F), "BM": (128, F),
     "Ibf": (128, B), "If": (128, F), "I2k": (128, B), "I32": (384, B), "I64": (384, B), "Dg": (128, B),
-    "Ones": (128, B), "Tri": (128, B), "B1": (8, B), "Bh": (8, B), "SC": (32, F), "Sd": (32, B), "Su": (32, F), "R12": (32, F),
+    "Ones": (128, B), "Tri": (128, B), "B1": (8, B), "Bh": (8, B), "SC": (24, F), "Sd": (32, B), "Su": (32, F), "R12": (32, F),
     "B16": (128, B), "Z3": (192, F), "r3": (192, B),
 }
 SCRATCH = {k: ("sbuf", [128, v[0]], v[1]) for k, v in SB.items()}
@@ -60,11 +70,11 @@ SB["nxv"] = (6, F)
 SCRATCH["nxd"] = ("dram", [6, 128, 1024], B)
 for _i in range(8):
     SCRATCH["ps%d" % _i] = ("psum", [128, 512], F)
-SEMAPHORES = (["cV", "cS", "cP", "cG", "lsem", "dz", "dnx", "dhu", "duu", "dn0", "dx0", "doe", "dox"]
+SEMAPHORES = (["cV", "cS", "cP", "cG", "lsem", "dz", "dnx", "dhu", "duu", "dn0", "dx0", "doe", "dox", "dfill"]
               + ["zarr%d" % t for t in range(3)] + ["narr%d" % t for t in range(3)]
               + ["harr%d" % t for t in range(3)] + ["dw%d" % t for t in range(3)]
-              + ["earr0", "earr1", "dox2", "go", "hm0", "hm1"] + ["h" + n for n in ("n", "z0", "z1", "z2")]
-              + ["r%s_%d" % (n, q) for n in ("n", "z0", "z1", "z2") for q in range(2, 6)] + ["ga%d" % i for i in range(14)])
+              + ["earr0", "earr1", "dox2", "go", "hm0", "hm1", "hk0", "hk1", "hk2"] + ["h" + n for n in ("n", "z0", "z1", "z2")]
+              + ["r%s_%d" % (n, q) for n in ("n", "z0", "z1", "z2") for q in range(2, 6)] + ["ga%d" % i for i in range(16)])
 
 
 def bits(es):
@@ -150,10 +160,12 @@ def helper_program(g, core, T, topo):
                 if me in spread(T, topo, c):
                     g.wait_ge(T.sem["r%s_%d" % (name, T.rank_of(c))], len(es))
                     write(([me] if rank is not None else [], rest, arr, mid, home), (spread(T, topo, c)[me], es, arr, mid, home))
-    for t in range(2 if which == 1 and rank is not None else 0):
-        x = T.pay[:, (6 * t + rank) * PW + 256:(6 * t + rank) * PW + 264]
-        g.wait_ge(T.sem["hm%d" % t], len(rest))
-        write((T.cores[rank + 1:] + T.cores[:rank], es, "earr%d" % t, x, x))
+    for t in range(3 if rank is not None else 0):
+        for d, a, b, sm, arr in ((1 if t < 2 else None, 256, 264, "hm", "earr"), (MH[t], 0, 256, "hk", "harr")):
+            if d == which:
+                x = T.pay[:, (6 * t + rank) * PW + a:(6 * t + rank) * PW + b]
+                g.wait_ge(T.sem["%s%d" % (sm, t)], len(rest))
+                write((T.cores[rank + 1:] + T.cores[:rank], es, "%s%d" % (arr, t), x, x))
     if sent[0]:
         g.wait_ge(T.sem.lsem, sent[0])
 
@@ -264,11 +276,13 @@ def rank_program(g, core, T, topo):
             dma(e, o, i, "dnx", 144, [R("nxi")] if gi == 8 else [], [])
 
     if myt == 0:
-        load_nx()
         dma("Y", ap(zown), T.z[:], "dz", 16, [zown], [])
     dma("S", T.hu[:, 0:128], T.hyp[:], "dhu", 16, [R("hu", 0, 128)], [])
+    if myt == 0:
+        load_nx()
     dma("S", T.E[:, 0:1024], T.x0[:], "dx0", 16, [R("E", 0, 1024)], [])
-    dma("Y", T.n0l[:, :], T.n0[:], "dn0", 16, [R("n0l")], [])
+    op("V", lambda: g.vector.memset(T.n0w[:, :], 0), [R("n0w")], [])
+    dma("S", T.n0w[0:128:16, :], T.n0[:], "dn0", 16, [R("n0w")], [])
     if myt > 0:
         dma("Y", ap(zown), T.z[:], "dz", 16, [zown], [])
         load_nx()
@@ -296,6 +310,47 @@ def rank_program(g, core, T, topo):
     ms(R("live"), 1.0)
     ts(R("Su"), R("CI", 0, 32), col("PF", 7), ALU.is_equal)
 
+    def early():
+        for j, src, v, o in ((16, 0, 16.0, ALU.mult), (6, 1, 19.5 - 2032.0, ALU.add), (25, 1, 35.5 - 2032.0, ALU.add),
+                             (26, 0, -2.0, ALU.add), (17, 1, -496.0, ALU.add), (23, 1, 8.0, ALU.is_lt), (27, 1, 8.0, ALU.is_ge),
+                             (9, 3, 1.0, ALU.add), (10, 5, 4.0, ALU.mult), (11, 4, 3.0, ALU.is_lt), (22, 4, 4.0, ALU.mult),
+                             (8, 1, 4.0, ALU.mult), (18, 0, -1.0, ALU.add), (19, 0, 127.0, ALU.add)):
+            ts(col("PF", j), col("PF", src), v, o)
+        ts(col("PF", 31), col("PF", 0), 64.0, ALU.is_lt, 8.0, ALU.mult)
+        ts(R("B1"), R("CI", 0, 8), col("PF", 2), ALU.is_equal)
+        ms(R("Db", 0, 16), 0.0)
+        for d in DN[:2]:
+            ms(R(d, DW - 16, DW), 4000.0)
+        ts(col("PF", 30), col("PF", 31), -4.0, ALU.add)
+        ts(R("dr", 0, 128), R("CI"), col("PF", 18), ALU.is_equal, -0.5, ALU.mult)
+        ts(R("dr", 128, 256), R("CI"), col("PF", 19), ALU.is_equal, 0.5, ALU.mult)
+        ts(R("Df"), R("If"), 0.5, ALU.mult)
+        ts(R("SCb"), R("S4i", 0, 24), col("PF", 10), ALU.is_equal, col("PF", 11), ALU.mult)
+        ts(R("pd", 0, 32), R("S4i"), col("PF", 0), ALU.is_equal, 4.0, ALU.mult)
+        ts(R("pd", 32, 48), R("S4i", 0, 16), col("PF", 26), ALU.is_equal, 4.0, ALU.mult)
+        tt(R("dr", 256, 384), R("dr", 0, 128), R("dr", 128, 256), ALU.add)
+        for a, b in (("SD", "SC"), ("SDb", "SCb")):
+            cp(R(a, 0, 8), R(b, 0, 8))
+            tt(R(a, 8, 24), R(b, 8, 24), R(b, 0, 16), ALU.subtract)
+        tt(R("pd", 48, 56), R("pd", 32, 40), R("pd", 40, 48), ALU.add)
+        tt(R("Df"), R("Df"), R("dr", 256, 384), ALU.add)
+        tt(R("Sd", 0, 24), R("pd", 8, 32), R("pd", 0, 24), ALU.subtract)
+        ts(R("Lm"), R("S4i"), 0.25, ALU.mult)
+        tt(R("Sd", 24, 32), R("pd", 48, 56), R("pd", 0, 8), ALU.add)
+        ts(R("R12"), R("CI", 0, 32), col("PF", 5), ALU.is_equal)
+        ts(R("Z3", 0, 96, 3), R("CI", 0, 32), 16.0, ALU.mult)
+        ts(R("Z3", 96, 192, 3), R("CI", 0, 32), 16.0, ALU.mult)
+
+    for a in range(4):
+        ts(R("D1", a, 512, 4), R("hu", 0, 128), col("PF", 12 + a), ALU.mult)
+    for k in range(4):
+        mm(R("ps5", k, 128, 4), blk("D1", k), R("Su"))
+    cp(R("Ibf"), R("If"))
+    if myt == 0:
+        early()
+    cp(R("took"), R("ps5", 0, 128))
+    mm(R("ps2", 0, 128), R("took"), R("If"))
+
     def nx_out():
         if myt == 0:
             cp(blk("nxs", rank, 512), R("nxi"))
@@ -316,9 +371,9 @@ def rank_program(g, core, T, topo):
 
     def sends():
         piece = lambda i: R(zown[0], zown[1] + PIECE[myt][i][0], zown[1] + PIECE[myt][i][1])
+        hand([(CARRY[myt][i], "hz%d" % i, piece(i)) for i in range(2)])
         if myt == 0:
             send(blk("nxs", rank, 512), "narr0")
-        hand([(CARRY[myt][i], "hz%d" % i, piece(i)) for i in range(2)])
         hand([(CARRY[myt][2], "hz2", piece(2))])
 
     for t in range(3):
@@ -339,29 +394,25 @@ def rank_program(g, core, T, topo):
     iota(R("BM"), [[0, 8], [1, 4], [0, 4]], 0)
     iota(R("B16"), [[1, 8], [0, 16]], 0)
 
-    for a in range(4):
-        ts(R("D1", a, 512, 4), R("hu", 0, 128), col("PF", 12 + a), ALU.mult)
-    for k in range(4):
-        mm(R("ps5", k, 128, 4), blk("D1", k), R("Su"))
     for j in range(1, 4):
-        act(blk("nxw", j, 1024), blk("nxw", 0, 1024), ACT.Identity, bias=1024.0 * j)
-    cp(R("Ibf"), R("If"))
-    ts(R("took"), R("ps5", 0, 128), -31.5, ALU.add)
-    mm(R("ps2", 0, 128), R("took"), R("If"))
+        act(blk("nxw", j, 1024), blk("nxw", 0, 1024), ACT.Identity)
     ts(R("pairb"), R("ps5", 0, 128), 4.0, ALU.mult, -15.5, ALU.add)
     ts(R("C32"), R("CI"), 32.0, ALU.mult)
+    ts(R("C16"), R("CI"), 32.0, ALU.mult, -16.0, ALU.add)
     ts(R("hi"), R("pairb"), 32 * MAG, ALU.add, 32 * MAG, ALU.subtract)
     ts(R("T1"), R("ps5", 0, 128), 4.0, ALU.mult, 4.0, ALU.add)
-    ts(R("LT"), R("ps2", 0, 128), 31.5, ALU.add)
-    ts(R("ta"), R("ps2", 0, 128), 64 * MAG, ALU.add, 64 * MAG, ALU.subtract)
-    ts(R("tc"), R("ps2", 0, 128), 16.0, ALU.mult, 504.0, ALU.add)
-    ts(R("ta"), R("ta"), -1023.0 / 64, ALU.mult)
+    cp(R("LT"), R("ps2", 0, 128))
     ms(R("Ones"), 1.0)
-    tt(R("tc"), R("tc"), R("ta"), ALU.add)
     ms(R("Vw", 0, 640, 5), 2.0)
     ms(R("Vw", 4, 640, 5), 0.0)
-    cp(R("Li"), R("tc"))
-    cp(R("Ln", 0, 64), R("n0l"))
+    act(blk("G", 0, 1024), IND("n0w", 0, 1024, "LT", 0, 64), ACT.Identity)
+    cp(blk("G", 1, 1024), IND("n0w", 0, 1024, "LT", 64, 128))
+    for r in range(16):
+        mm(R("ps1", r, 128, 16), R("G", r, 2048, 16), R("SC", 0, 8))
+    act(blk("Y", 0, 1024), IND("E", 0, 1024, "LT", 0, 64), ACT.Identity, scale=-1.0)
+    act(R("N1"), R("ps1", 0, 128), ACT.Identity, bias=64.0)
+    mm(R("ps3", 0, 128), R("N1"), R("If"))
+    act(blk("Y", 1, 1024), IND("E", 0, 1024, "LT", 64, 128), ACT.Identity, scale=-1.0)
 
     def u_in():
         for a in range(4):
@@ -373,25 +424,22 @@ def rank_program(g, core, T, topo):
         for b in range(2):
             q = 2 * t + b
             if t == 0:
-                ts(blk("nxf", b, 512), blk("nxs", b, 512), 64.0, ALU.add)
-                dma("Y", T.nxw[0:128:4, 2048 * b:2048 * b + 2048], T.nxf[:, 512 * b:512 * b + 512], "dw0", 32,
-                    [blk("nxw", b, 2048)], [blk("nxf", b, 512)])
+                ts(blk("Y4", b, 512), blk("nxs", b, 512), 64.0, ALU.add)
+                dma("Y", T.nxw[0:128:4, 2048 * b:2048 * b + 2048], T.Y4[:, 512 * b:512 * b + 512], "dw0", 32,
+                    [blk("nxw", b, 2048)], [blk("Y4", b, 512)])
                 continue
             for i in range(2):
                 src, r = (T.nxp[:, 512 * i:512 * i + 512], R("nxp")) if q == rank else (T.nxd[q, :, 512 * i:512 * i + 512], col("nxv", q))
                 dma("Y", T.nxb[i:128:4, 2048 * b:2048 * b + 2048], src, "dw%d" % t, 64, [blk("nxb", b, 2048)], [r])
 
-    act(R("Y"), IND("E", 0, 1024, "LT", 0, 128), ACT.Identity, scale=-1.0)
+    act(col("PF", 28), col("PF", 0), ACT.Exp, bias=-1.0, scale=0.0)
 
     def hots():
         return [lambda c=c: ts(blk("OHh", c), R("C32"), col("hi", c), ALU.is_equal) for c in range(128)]
 
     def hots_s(c0, c1=128):
         for c in range(c0, c1):
-            act(blk("OHh", c), R("C32"), ACT.Abs, bias=col("hi", c), scale=-1.0)
-            if c % 8 == 7:
-                a = max(c0, c - 7)
-                act(R("OHh", 128 * a, 128 * c + 128), R("OHh", 128 * a, 128 * c + 128), ACT.Relu, bias=1.0, scale=-1.0)
+            act(blk("OHh", c), R("C16"), ACT.Sign, bias=col("hi", c), scale=-1.0)
 
     def place_list(t):
         w = WL[t]
@@ -404,10 +452,7 @@ def rank_program(g, core, T, topo):
         ts(R("td"), R("live"), -16384.0, ALU.mult, 16384.0 - 3.5 - WL[t] / 2, ALU.add)
 
     def succ_a(t, split):
-        w, n, l, o, sel = ("nxb", 4096, "Ln", "Gb", "SCb") if t > 0 else ("tab", 1024, "Li", "G", "SC")
-        if t == 0:
-            act(R("tab", 0, 512), IND("nxw", 0, 4096, "Ln", 0, 32), ACT.Identity)
-            cp(R("tab", 512, 1024), IND("nxw", 0, 4096, "Ln", 32, 64))
+        w, n, l, o, sel = ("nxb", 4096, "Ln", "Gb", "SCb") if t > 0 else ("nxw", 4096, "Ln", "G", "SC")
         if split:
             act(R(o, 0, 16 * split), IND(w, 0, n, l, 0, split), ACT.Identity)
         if split < 128:
@@ -415,17 +460,20 @@ def rank_program(g, core, T, topo):
         for r in range(16):
             mm(R("ps1", r, 16 * SB[sel][0], 16), R(o, r, 2048, 16), R(sel))
 
-    def succ_b():
-        act(R("C1"), R("ps1", 0, 384), ACT.Copy)
-        for m in range(3):
-            mm(blk("ps3", m), blk("C1", m), R("If"))
+    def succ_b(t):
+        for m in (1, 0, 2):
+            act(blk("C1", m), blk("ps1", m), ACT.Copy)
+            mm(listed(m), blk("C1", m), R("If"))
 
-    def lists_c(t=0):
-        if t != 1:
-            tt(R("Dc"), R("ps1", 128, 384), R("C1", 0, 256), ALU.subtract)
-        ts(R("Lc"), R("ps3", 0, 384), -64.0, ALU.add)
-        if t == 1:
-            tt(R("Dc"), R("ps1", 128, 384), R("C1", 0, 256), ALU.subtract)
+    listed = lambda m: blk("ps7", 0) if m == 1 else blk("ps3", m)
+
+    def succ_c(t):
+        for r in range(16):
+            mm(R("ps1", r, 384, 16), R("Gb" if t > 0 else "G", r, 2048, 16), R("SDb" if t > 0 else "SD"))
+
+    def lists_c(ms_=(1, 0, 2)):
+        for m in ms_:
+            ts(blk("Lc", m), listed(m), -64.0, ALU.add)
 
     def chunk(t, ch, by_v, a=0, b=64):
         d = R(DN[t], 16 + 1024 * ch + 16 * a, 16 + 1024 * ch + 16 * b)
@@ -439,58 +487,69 @@ def rank_program(g, core, T, topo):
 
     def gate(t, m):
         big = 2 * MAG
-        wp = lambda m, r: R("ps7", 128 * (r % 4) + 4 * (r // 4) + m + 1, 128 * (r % 4) + 128, 16)
-        if m == 0 and SI[t]:
-            for ch in range(2):
-                act(blk("G", ch, 1024), R(DN[t], 16 + 1024 * ch, 16 + 1024 * ch + 1024), ACT.Abs)
-                act(blk("ind", ch, 1024), blk("G", ch, 1024), ACT.Sign, bias=1.0 + 2.0 ** -12, scale=-1.0)
-            return
-        if m == 3:
-            if SI[t]:
-                for r in range(16):
-                    mm(wp(0, r), R("ind", r, 2048, 16), R("Bh"))
-            return
-        for ch in (2 * m, 2 * m + 1):
+        d = lambda ch, a=0, b=1024: R(DN[t], 16 + 1024 * ch + a, 16 + 1024 * ch + b)
+        for ch in m:
+            if ch in SI[t]:
+                at = 1024 * (SI[t].index(ch) % 2)
+                for a in (0, 512):
+                    act(R("G", at + a, at + a + 512), d(ch, a, a + 512), ACT.Abs)
+                for a in (0, 512):
+                    act(R("ind", 1024 * ch + a, 1024 * ch + a + 512), R("G", at + a, at + a + 512), ACT.Sign, bias=1.0 + 2.0 ** -12, scale=-1.0)
+                continue
             if ch == 5:
                 weights(t, 0, 2)
-            ts(blk("ind", ch, 1024), R(DN[t], 16 + 1024 * ch, 16 + 1024 * ch + 1024), big, ALU.add, big, ALU.is_equal)
-        for r in range(16):
-            o = wp(m, r) if m < 2 else R("ps3", 384 + 32 * (r % 4) + r // 4, 384 + 32 * (r % 4) + 32, 4)
-            mm(o, R("ind", 2048 * m + r, 2048 * m + 2048, 16), R("B1"))
+            ts(blk("ind", ch, 1024), d(ch), big, ALU.add, big, ALU.is_equal)
+
+    def count(t, m, rs=range(16)):
+        both = (2 * m in SI[t]) == (2 * m + 1 in SI[t])
+        for h, n in ((0, 2),) if both else ((0, 1), (1, 1)):
+            for r in rs:
+                o = ("ps7", 128 * (r % 4) + 4 * (r // 4) + m + 1, 128 * (r % 4) + 128, 16) if m < 2 or r % 4 else ("ps3", 384 + r // 4, 416, 4)
+                a = 2048 * m + 1024 * h
+                mm(R(*o, 64 * h, 64 * (h + n)), R("ind", a + r, a + 1024 * n, 16), R("Bh" if 2 * m + h in SI[t] else "B1"))
 
     def weights(t, a, b):
         for i in range(a, b):
             if i == 0 and t > 0:
-                ts(R("e8", 0, 8), R("ps1", 16, 24), 1.0 / 2048, ALU.mult, 0.5 + 2.0 ** -12, ALU.add)
+                ts(R("e8", 0, 8), R("ps1", 400, 408), 1.0 / 2048, ALU.mult, 0.5 + 2.0 ** -12, ALU.add)
                 ts(R("Li"), R("ps2", 256, 384), 512.0 - 512.0 / WL[t - 1], ALU.add, 1023.0, ALU.min)
             elif i == 1 and t > 0:
                 ts(R("Vw", 0, 640, 5), IND("e8", 0, 16, "Lw", 0, 8), MAG, ALU.add, MAG, ALU.subtract)
-            elif i > 1:
-                m = (1, 0, 2)[i - 2]
-                ts(R("Vw", m + 1, 640, 5), R("ps7", m + 1, 512, 4) if m < 2 else R("ps3", 384, 512), 4.0 if SI[t] and m == 0 else -4.0, ALU.add, 0.0, ALU.max)
+            elif i in (2, 3):
+                m = 3 - i
+                less = col("PF", 30) if 2 * m in SI[t] and 2 * m + 1 not in SI[t] else 4.0 if 2 * m in SI[t] else -4.0
+                ts(R("Vw", m + 1, 640, 5), R("ps7", m + 1, 512, 4), less, ALU.add, 0.0, ALU.max)
+            elif i == 4:
+                count(t, 2, [r for r in range(16) if r % 4])
+                ts(R("Vw", 3, 160, 5), R("ps3", 384, 416), -4.0, ALU.add, 0.0, ALU.max)
+            elif i == 5:
+                ts(R("Vw", 163, 640, 5), R("ps7", 131, 512, 4), -4.0, ALU.add, 0.0, ALU.max)
 
-    def terms_a(t):
-        act(R("E"), R("Y4"), ACT.Abs, scale=4.0)
-        act(R("E"), R("E"), ACT.Exp, scale=-1.0)
+    def terms_a(t, a=0, b=2048):
+        halves = ((a, (a + b) // 2), ((a + b) // 2, b))
+        for a, b in halves:
+            act(R("E", a, b), R("Y4", a, b), ACT.Abs, scale=4.0)
+        for a, b in halves:
+            act(R("E", a, b), R("E", a, b), ACT.Exp, scale=-1.0)
 
     def terms_b(t, a=0, b=8):
         for i in range(a, b):
-            k, h = i // 2, i % 2
-            if t == 0 and k == 0:
-                if h == 0:
-                    mm(R("ps0"), R("If"), R("E", 0, 2048, 4), True, False)
-            else:
-                mm(blk("ps0", h, 256), R("If"), R("E", 1024 * h + k, 1024 * h + 1024, 4), False, t == 2 and i == 7)
+            k, h = i % 4, i // 4
+            mm(blk("ps0", h, 256), R("If"), R("E", 1024 * h + k, 1024 * h + 1024, 4), False, t == 2 and i == 7)
 
     def terms_c():
         for i in range(12):
-            mm(R("ps1", 32, 64), R("Ibf"), R("miss", 128 * (i // 4) + i % 4, 128 * (i // 4) + 128, 4), i == 0, i == 11)
-        act(R("mc"), R("ps1", 32, 64), ACT.Identity, scale=math.exp(-1.0) - 1.0)
-        act(R("nxf", 0, 512), IND("mc", 0, 32, "Lm", 0, 32), ACT.Identity)
+            mm(R("ps6", 384, 416), R("Ibf"), R("miss", 128 * (i // 4) + i % 4, 128 * (i // 4) + 128, 4), i == 0, i == 11)
+
+    def terms_c2(step):
+        if step == 0:
+            act(R("mc"), R("ps6", 384, 416), ACT.Identity, scale=col("PF", 29))
+            return
+        act(R("nxw", 2048, 2560), IND("mc", 0, 32, "Lm", 0, 32), ACT.Identity)
 
     def terms_d():
         for sl in range(4):
-            mm(R("ps0", sl, 512, 4), blk("nxf", sl), R("If"), False, False)
+            mm(R("ps0", sl, 512, 4), blk("nxw", 16 + sl), R("If"), False, False)
 
     begun = {}
 
@@ -519,9 +578,7 @@ def rank_program(g, core, T, topo):
         pre = R("ps4", 384, 384 + n)
         bound_a(t, 2)
         if t == 2:
-            terms_b(2, TB2)
-            act(R("tab", 0, 512), R("ps0"), ACT.Copy)
-            dma("S", T.ye[:], T.tab[:, 0:512], "doe", 16, [], [R("tab", 0, 512)])
+            terms_b(2, TB2, TB2 + 1)
 
         def digits():
             tt(R("incl", 264, 264 + n), pre, R("incl", 256, 256 + n), ALU.subtract)
@@ -539,9 +596,11 @@ def rank_program(g, core, T, topo):
             ts(blk("ib", gi, w), blk("incl", gi, w), col("ps4", 384 + gi), ALU.add, 1024.0, ALU.is_le)
         if t == 2:
             for j in range(2):
-                mm(col("ps1", 0), R("ib", j, 256, 2), col("Ones", 0), j == 0, j == 1)
-            cp(col("mk", 0), col("ps1", 0))
-            mm(col("ps1", 1), R("B16"), col("mk", 0))
+                mm(col("ps3", 256), R("ib", j, 256, 2), col("Ones", 0), j == 0, j == 1)
+            extra()
+            cp(col("mk", 0), col("ps3", 256))
+            mm(col("ps3", 257), R("B16"), col("mk", 0))
+            terms_b(2, TB2 + 1)
             return
         for f in extra[0]:
             f()
@@ -549,9 +608,9 @@ def rank_program(g, core, T, topo):
         for f in list(extra[1]) + list(extra[2]):
             f()
         for h, (p0, p1) in enumerate(parts):
-            mm(R("ps1", n * h, n * h + n), R("Ones") if w == 32 else blk("Hf", h), R("mk", w - 1, 256, w))
+            mm(R("ps2", n * h, n * h + n), R("Ones") if w == 32 else blk("Hf", h), R("mk", w - 1, 256, w))
         table()
-        cp(R("th", 0, 8), R("ps1", 0, 8))
+        cp(R("th", 0, 8), R("ps2", 0, 8))
         for f in extra[3]:
             f()
         tt(R("live"), IND("th", 0, 16, "Lth", 0, 8), R("pairb"), ALU.is_gt)
@@ -565,7 +624,7 @@ def rank_program(g, core, T, topo):
     def miss_weight(t):
         for q in range(6):
             b = (6 * t + q) * PW
-            mm(R("ps1", 16, 24), R("Ones"), R("pay", b + 256, b + 264), q == 0, q == 5)
+            mm(R("ps1", 400, 408), R("Ones"), R("pay", b + 256, b + 264), q == 0, q == 5)
 
     def places_b():
         act(R("tabb", 0, 512), R("ps5"), ACT.Copy)
@@ -583,6 +642,19 @@ def rank_program(g, core, T, topo):
     def places_c(t):
         tt(R("pb"), R("ps3", 0, 384), R("le%d" % (t % 2)), ALU.mult)
 
+    def slots(t):
+        o = blk("ps7" if t < 2 else "ps2", 1)
+        for m in range(3):
+            mm(o, blk("le%d" % (t % 2), m), R("I2k"), m == 0, False)
+        mm(o, R("td"), R("Ibf"), False, False)
+        mm(o, R("Ones"), R("Dg"), False, True)
+
+    def high(t):
+        ts(R("hi"), R("ps6", 0, 128), WL[t] * MAG, ALU.add, WL[t] * MAG, ALU.subtract)
+
+    def slot_list(t):
+        ts(R("Ls%d" % (t % 2)), blk("ps7" if t < 2 else "ps2", 1), col("PF", 6 if WL[t] == 32 else 25), ALU.add, float(DW - 16), ALU.min)
+
     def draw(t, between):
         le = "le%d" % (t % 2)
         sl = lambda n, m, k: R(n, 128 * m + k, 128 * m + 128, 4)
@@ -595,8 +667,8 @@ def rank_program(g, core, T, topo):
                     hot.pop(0)()
 
         def idle(i):
-            if t > 0:
-                bound_a(t - 1, i)
+            if t > 0 and i >= AH[0]:
+                bound_a(t - 1, i - AH[0])
 
         def ne(j, k, m, x=None, y=None):
             b = 96 * (j * (7 - j) // 2 + k - j - 1) + 32 * m
@@ -612,7 +684,14 @@ def rank_program(g, core, T, topo):
             dead_mask(0)
         nes = lambda j, k: [lambda m=m: ne(j, k, m) for m in range(3)]
         muls = lambda j, k: [lambda m=m: mul(j, k, m) for m in range(3)]
-        later = {(1, 0): nes(0, 2), (1, 1): muls(0, 2), (1, 2): nes(0, 3), (1, 4): muls(0, 3), (2, 0): nes(1, 3), (2, 1): muls(1, 3)}
+        later = {(1, 0): nes(0, 2), (1, 5): muls(0, 2)[:2], (1, 1): muls(0, 2)[2:] + nes(0, 3)[:1], (1, 2): nes(0, 3)[1:], (1, 4): muls(0, 3),
+                 (2, 0): nes(1, 3), (2, 5): muls(1, 3)[:2], (2, 1): muls(1, 3)[2:]}
+        if not WIDE:
+            later = {(1, 0): nes(0, 2), (1, 1): muls(0, 2), (1, 2): nes(0, 3), (1, 4): muls(0, 3), (2, 0): nes(1, 3), (2, 1): muls(1, 3)}
+        if not D9:
+            a, b = nes(0, 2) + muls(0, 2) + nes(0, 3) + muls(0, 3), nes(1, 3) + muls(1, 3)
+            later = {(1, 0): a[0:3], (1, 5): a[6:8], (1, 1): a[3:5], (1, 2): a[5:6] + a[8:9], (1, 3): a[9:11], (1, 4): a[11:],
+                     (2, 0): b[0:2], (2, 5): b[2:3], (2, 1): b[3:4], (2, 2): b[4:5], (2, 3): b[5:]}
 
         def wait(k, i, n):
             gap(n, later.get((k, i), []))
@@ -625,14 +704,32 @@ def rank_program(g, core, T, topo):
             wait(k, 0, HF + 1)
             if k == 0:
                 idle(0)
+            if k == 3:
+                if t > 0:
+                    places_c(t - 1)
+                parts = [(R("If"), R("T1")), (R("Ibf"), R("td"))] if t == 0 else [(R("Ibf"), blk("pb", m)) for m in range(3)]
+                for i, (a, b) in enumerate(parts):
+                    mm(R("ps6", 0, 128), a, b, i == 0 and t == 0, False)
             for m in range(3):
                 tt(sl(le, m, k), pm(m), pm(4), ALU.is_le)
-            if t == 2 and k == 3:
-                break
-            gap(HF - 2)
-            tt(d(5), sl(le, 0, k), sl("C1", 0, k), ALU.mult)
-            tt(d(6), sl(le, 1, k), sl("Dc", 0, k), ALU.mult)
-            tt(d(7), sl(le, 2, k), sl("Dc", 1, k), ALU.mult)
+            if k == 3:
+                if t < 2:
+                    slots(t)
+                for m in range(3):
+                    mm(R("ps6", 0, 128), R("Ibf"), blk(le, m), False, m == 2)
+                if t == 2:
+                    slots(t)
+                    break
+            if WIDE:
+                wait(k, 5, HF - 1)
+                tt(R("dr", b0 + 160, b0 + 256), R("ps1", k, 384, 4), R(le, k, 384, 4), ALU.mult)
+            else:
+                if k == 0:
+                    weights(t, 5, 6)
+                else:
+                    wait(k, 5, HF - 2)
+                for m in range(3):
+                    tt(d(5 + m), sl("ps1", m, k), sl(le, m, k), ALU.mult)
             if k == 3:
                 tt(blk("miss", t), R("live"), blk(le, 0), ALU.is_gt)
             else:
@@ -644,9 +741,14 @@ def rank_program(g, core, T, topo):
                 idle(2)
             if k == 0 and t > 0:
                 tt(sl("took", 0, k), d(8), d(7), ALU.add)
-                between([nes(0, 1), [lambda: ts(R("dr", 288, 384), R("ne", 0, 96), 16384.0, ALU.mult)],
+                extra = [nes(0, 1), [lambda: ts(R("dr", 288, 384), R("ne", 0, 96), 16384.0, ALU.mult)],
                          [lambda m=m: tt(d(m), d(9 + m), sl("pairb", 0, 0), ALU.max) for m in range(3)],
-                         [lambda: tt(R("ne", 0, 96), IND("th", 0, 16, "Lg", 0, 6), R("dr", 0, 96), ALU.is_le)]])
+                         [lambda: tt(R("ne", 0, 96), IND("th", 0, 16, "Lg", 0, 6), R("dr", 0, 96), ALU.is_le)]]
+                for i in range(AH[1]):
+                    for f in extra[i]:
+                        f()
+                    extra[i] = []
+                between(extra)
                 u5 = lambda k2: R("U5", 640 * t + 160 * k2 + 4, 640 * t + 160 * k2 + 160, 5)
                 for m in range(3):
                     mul(k, k + 1, m)
@@ -655,6 +757,20 @@ def rank_program(g, core, T, topo):
                 tt(u5(2), u5(2), sl("live", 0, 2), ALU.mult)
                 dead_mask(t)
                 places_b()
+                if TA < 2048:
+                    terms_a(t - 1, TA)
+            elif k < 3 and not D9:
+                wait(k, 2, HF - 1)
+                tt(sl("took", 0, k), d(8), d(7), ALU.add)
+                wait(k, 3, HF - 1)
+                for m in range(3):
+                    ne(k, k + 1, m)
+                wait(k, 6, 0)
+                for m in range(3):
+                    mul(k, k + 1, m)
+                wait(k, 4, HF)
+                if t > 0 and k == 1:
+                    places_v()
             elif k < 3:
                 for m in range(3):
                     tt(d(9 + m), sl("C1", m, k + 1), d(7), ALU.subtract)
@@ -669,17 +785,22 @@ def rank_program(g, core, T, topo):
                 if t > 0 and k == 1:
                     places_v()
             else:
+                slot_list(t)
                 tt(R("tc"), blk("miss", t), R("N1"), ALU.mult)
                 tt(sl("took", 0, k), d(8), d(7), ALU.add)
+                if t == 1:
+                    high(t)
+                    ts(R("pairb"), R("ps6", 0, 128), WL[t] / 2 - 0.5, ALU.add)
+                tt(R("lo"), R("ps6", 0, 128), R("hi"), ALU.subtract)
 
     def marks_out(t):
         b = (6 * t + rank) * PW
         n = 256
-        if t == 2:
-            ts(R("pay", b, b + 256), R("ps4", 0, 256), 1.0, ALU.min)
+        ts(R("pay", b, b + 256), R("ps4", 0, 256), 1.0, ALU.min)
+        if MH[t] is None:
+            send(R("pay", b, b + n), "harr%d" % t)
         else:
-            act(R("pay", b, b + 256), R("ps4", 0, 256), ACT.Sign)
-        send(R("pay", b, b + n), "harr%d" % t)
+            hand([(MH[t], "hk%d" % t, R("pay", b, b + n))])
         arrive("harr%d" % t, 5 * noff, [R("pay", (6 * t + q) * PW, (6 * t + q) * PW + n) for q in range(6) if q != rank])
 
     def after_draw(t):
@@ -687,135 +808,140 @@ def rank_program(g, core, T, topo):
         w = WL[t]
         pr = R("ps6", 0, 128)
 
-        def pair_sum():
-            parts = [(R("If"), R("T1")), (R("Ibf"), R("td"))] if t == 0 else []
-            parts += [(R("Ibf"), blk(le, m)) for m in range(3)] + [(R("Ibf"), blk("pb", m)) for m in range(3 if t > 0 else 0)]
-            for i, (a, b) in enumerate(parts):
-                mm(pr, a, b, i == 0 and t == 0, i == len(parts) - 1)
-        if t == 2:
-            places_c(t - 1)
-        if t != 1:
-            pair_sum()
-        for m in range(3):
-            mm(R("ps2", 128, 256), blk(le, m), R("I2k"), m == 0, False)
-        mm(R("ps2", 128, 256), R("td"), R("Ibf"), False, False)
-        mm(R("ps2", 128, 256), R("Ones"), R("Dg"), False, True)
         if t < 2:
             mm(R("ps2", 0, 128), R("tc"), R("If"), True, False)
             mm(R("ps2", 0, 128), R("took"), R("If"), False, True)
-
         if t == 1:
-            places_c(t - 1)
-            pair_sum()
+            terms_b(0, TB1)
         if t == 2:
             tt(blk("miss", t), R("live"), blk(le, 0), ALU.is_gt)
-        if t > 0:
-            terms_b(t - 1, TB1)
-
-        def pairs():
-            if t > 0:
-                ts(R("hi"), pr, w * MAG, ALU.add, w * MAG, ALU.subtract)
-            tt(R("lo"), pr, R("hi"), ALU.subtract)
-        if t != 1:
-            pairs()
-        for j in range(LO0 if t == 0 else 0):
-            ts(blk("OHl", j), R("lo"), j - 15.5, ALU.is_equal)
+            terms_b(1, TB1, TB3)
+            for k in range(3):
+                mm(R(HELD[k]), R("If"), R("Y", k, 2048, 4))
+            high(t)
+            ts(R("pairb"), pr, w / 2 - 0.5, ALU.add)
+            ms(R(TABS[0], 0, 16), 0.0)
+            ts(R("ib", 0, 128), R("hi"), 8192.0, ALU.min)
+            slot_list(2)
+            ms(R(TABS[1], 0, 16), 0.0)
+            tt(R("lo"), pr, R("ib", 0, 128), ALU.subtract)
+            terms_c()
+        early = [lambda j=j: ts(blk("OHl", j), R("lo"), j - 15.5, ALU.is_equal) for j in range(LO0)] if t == 0 else \
+            [lambda j=j: ts(blk("OHh", j), R("hi"), 64.0 * j, ALU.is_equal) for j in range(LO0 if t == 1 else 0)]
+        for fn in early:
+            fn()
         if t < 2:
             ts(R("Ln"), R("ps2", 0, 128), -64.0, ALU.add)
-        ts(R(ls), R("ps2", 128, 256), col("PF", 6 if w == 32 else 25), ALU.add, float(DW - 16), ALU.min)
-        if t < 2:
             for r in range(16):
                 mm(R("ps4", 256, 264), R("Ibf"), R("miss", 128 * t + r, 128 * t + 128, 16), r == 0, r == 15)
             y0 = [0]
 
-            def y4(y1):
+            def y4(y1, by_v=False):
                 for a, b in ((y0[0], min(y1, 64)), (max(y0[0], 64), y1)):
                     if a < b:
-                        act(R("Y4", 16 * a, 16 * b), IND(dd, 0, DW, ls, a, b), ACT.Identity, scale=-0.25)
+                        if by_v:
+                            ts(R("Y4", 16 * a, 16 * b), IND(dd, 0, DW, ls, a, b), -0.25, ALU.mult)
+                        else:
+                            act(R("Y4", 16 * a, 16 * b), IND(dd, 0, DW, ls, a, b), ACT.Identity, scale=-0.25)
                         if b % 64 == 0:
                             add(blk("Y", b // 64 - 1, 1024), blk("Y4", b // 64 - 1, 1024))
-                y0[0] = y1
-            y4(Y4A[t][0])
-            succ_a(t + 1, SPL[t])
-            misses_out(t)
-            y4(Y4A[t][1])
-            succ_b()
-            y4(128)
-        if t == 1:
-            pairs()
+                y0[0] = max(y0[0], y1)
+
+            def onward():
+                y4(Y4A[t][0])
+                succ_a(t + 1, SPL[t])
+                misses_out(t)
+                y4(Y4A[t][1])
+                succ_b(t + 1)
+                y4(128)
+            if not Y4V[t][1]:
+                onward()
         c0 = 128 - len(hot) if t == 0 else 0
         if w == 32:
             f = [lambda j=j: ts(blk("OHl", j), R("lo"), j - 15.5, ALU.is_equal) for j in range(LO0 if t == 0 else 0, 32)]
             f += hots()[c0:128 - NS[t]]
         else:
-            f = [lambda j=j: ts(blk("OHh", j), R("hi"), 64.0 * j, ALU.is_equal) for j in range(64)]
+            f = [lambda j=j: ts(blk("OHh", j), R("hi"), 64.0 * j, ALU.is_equal) for j in range(LO0, 64)]
             f += [lambda j=j: ts(blk("OHh", 64 + j), R("lo"), j - 31.5, ALU.is_equal) for j in range(64)]
         if t == 2:
-            act(R("Y4"), IND(dd, 0, DW, ls, 0, 128), ACT.Identity, scale=-0.25)
-            add(R("Y"), R("Y4"))
-            terms_a(2)
-            hots_s(128 - NS[t])
-            terms_c()
+            hots_s(128 - NS[2], 124)
+            terms_c2(0)
+            hots_s(124)
+            terms_c2(1)
         for i, fn in enumerate(f):
+            if t < 2 and Y4V[t][1] and i == Y4V[t][0]:
+                y4(Y4V[t][1], True)
+                onward()
             if t < 2 and i == LCAT[t]:
-                lists_c(t)
+                lists_c((1,))
+            if t < 2 and i == LCAT[t] + 6:
+                lists_c((0, 2))
             fn()
-        ts(R("pairb"), pr, w / 2 - 0.5, ALU.add)
+        if t == 0:
+            ts(R("pairb"), pr, w / 2 - 0.5, ALU.add)
         if t == 0:
             tt(R("N1"), R("tc"), R("took"), ALU.add)
         if t < 2 and LCAT[t] >= len(f):
             lists_c()
-        late_g = [gi for gi in range(8) if 16 * gi + 16 > c0 and 16 * gi < 128 - NS[t]] if t == 0 else []
-        for c in [16 * gi + r for gi in sorted(range(8), key=lambda gi: gi in late_g) for r in range(16)]:
-            if t == 2 and c % 16 == 0 and c >= 128 - 16 * TBH:
-                terms_b(2, c // 16 - 8 + TBH, c // 16 - 7 + TBH)
-            if w == 32:
-                mm(R("ps4", 32 * (c // 16), 32 * (c // 16) + 32), blk("OHh", c), R("OHl", c, 4096, 128), c % 16 == 0, c % 16 == 15)
-            else:
-                gh, gl = c // 64, c // 16 % 4
-                mm(R("ps4", 64 * gl, 64 * gl + 64, 1, 64 * gh, 64 * gh + 64), R("OHh", c, 8192, 128),
-                   R("OHh", 8192 + c, 16384, 128), c % 16 == 0, c % 16 == 15)
 
-    def gates(t):
-        sent = t == 0
-        for i, ch in enumerate(range(NV[t], 6)):
-            if not sent and i == PAYAT[t - 1]:
-                marks_out(t - 1)
-                sent = True
-            chunk(t, ch, False, 0, 64 - NVH[t] if ch == 5 else 64)
-        if not sent:
-            marks_out(t - 1)
-        for ch in sorted(range(NV[t]), key=lambda ch: ch % 2):
-            chunk(t, ch, True)
-        if NVH[t]:
-            chunk(t, 5, True, 64 - NVH[t], 64)
-        for i, m in enumerate((0, 1, 3, 2)):
-            if t > 0 and i == 2:
-                place_list(t - 1)
-                miss_weight(t - 1)
-            gate(t, m)
+        def hist(gi):
+            for c in range(16 * gi, 16 * gi + 16):
+                if w == 32:
+                    o = blk(sb, gi - nv, 32) if gi >= nv else blk("ps4", gi, 32)
+                    mm(o, blk("OHh", c), R("OHl", c, 4096, 128), c % 16 == 0, c % 16 == 15)
+                else:
+                    gh, gl = c // 64, c // 16 % 4
+                    mm(R("ps4", 64 * gl, 64 * gl + 64, 1, 64 * gh, 64 * gh + 64), R("OHh", c, 8192, 128),
+                       R("OHh", 8192 + c, 16384, 128), c % 16 == 0, c % 16 == 15)
+        nv, sb = 8 - NS[t] // 16, "ps3" if t == 2 else "ps5"
+        end = lambda gi: (3 * 16 * (gi - nv + 1) if gi >= nv else 32 + 16 * (gi + 1)) if t == 2 else (gi < nv) + (nv > gi >= c0 // 16)
+        turn = sorted(range(8), key=end)
+        sums = R("tab", 0, 32 * (8 - nv))
+        for gi in turn:
+            if gi == turn[-1] and t == 2:
+                mm(R("ps4", 32 * nv, 256), R("Df"), sums)
+            hist(gi)
+            if gi == 7 and nv < 8 and t == 2:
+                act(sums, R(sb, 0, 32 * (8 - nv)), ACT.Copy)
+
+        def close():
+            if nv < 8 and t < 2:
+                cp(sums, R(sb, 0, 32 * (8 - nv)))
+                mm(R("ps4", 32 * nv, 256), R("Df"), sums)
+        return close
+
+    def gates(t, close):
+        mine = [(ch, True, 0, 64) for ch in sorted(range(NV[t]), key=lambda ch: ch % 2)] + [(5, True, 64 - NVH[t], 64)] * (NVH[t] > 0)
+        his = [(ch, False, 0, 64 - NVH[t] if ch == 5 else 64) for ch in range(NV[t], 6)]
+        a, b = PAYAT[t - 1] if t > 0 else (0, 0)
+        for x in his[:b] + mine[:max(0, a - 1)]:
+            chunk(t, *x)
         if t > 0:
-            terms_a(t - 1)
+            close()
+            chunk(t, *mine[a - 1])
+            marks_out(t - 1)
+        for x in his[b:] + mine[a:]:
+            chunk(t, *x)
+        succ_c(t)
+        gate(t, SI[t])
+        if t > 0:
+            place_list(t - 1)
+            miss_weight(t - 1)
+        for x in TESTS[t]:
+            if x < 6:
+                gate(t, (x,))
+            else:
+                count(t, x - 6, range(0, 16, 4 if x == 8 else 1))
+        if t > 0:
+            terms_a(t - 1, 0, TA)
 
     hot = hots()
-    ts(col("PF", 24), col("PF", 0), -3.0, ALU.add)
-    ts(col("PF", 16), col("PF", 0), 16.0, ALU.mult)
-    ts(col("PF", 6), col("PF", 1), 19.5 - 2032.0, ALU.add)
-    ts(col("PF", 25), col("PF", 1), 35.5 - 2032.0, ALU.add)
-    ts(col("PF", 26), col("PF", 0), -2.0, ALU.add)
-    ts(col("PF", 17), col("PF", 1), -496.0, ALU.add)
-    ts(col("PF", 23), col("PF", 1), 8.0, ALU.is_lt)
-    ts(col("PF", 27), col("PF", 1), 8.0, ALU.is_ge)
-    ts(col("PF", 9), col("PF", 3), 1.0, ALU.add)
-    ts(col("PF", 10), col("PF", 5), 4.0, ALU.mult)
-    ts(col("PF", 11), col("PF", 4), 3.0, ALU.is_lt)
-    ts(col("PF", 22), col("PF", 4), 4.0, ALU.mult)
-    ts(col("PF", 8), col("PF", 1), 4.0, ALU.mult)
-    ts(R("B1"), R("CI", 0, 8), col("PF", 2), ALU.is_equal)
-    for d in DN[:2]:
-        ms(R(d, 0, 16), 0.0)
-        ms(R(d, DW - 16, DW), 4000.0)
-    ts(R("SC", 24, 32), R("S4i", 0, 8), col("PF", 24), ALU.is_equal)
+    if myt > 0:
+        early()
+    ms(blk("nxb", 0, 1024), 64.0)
+    ms(R("X", 0, 512), 0.0)
+    mm(R("ps0"), R("Ibf"), R("X", 0, 512), True, False)
+    ms(R("D1", 0, 16), 0.0)
 
     def late():
         iota(R("ib"), [[0, 256]], 0, 1)
@@ -828,40 +954,31 @@ def rank_program(g, core, T, topo):
         if 64 in WL:
             sel(blk("Hf", 0), R("ib", 0, 128), [[0, 128]], ALU.is_gt, 64, -1)
             sel(blk("Hf", 1), R("ib", 0, 128), [[0, 128]], ALU.is_ge, -64, 1)
-        ts(R("Lm"), R("S4i"), 0.25, ALU.mult)
-        ts(R("SCb"), R("S4i", 0, 24), col("PF", 10), ALU.is_equal, col("PF", 11), ALU.mult)
-        ts(R("pd", 0, 32), R("S4i"), col("PF", 0), ALU.is_equal, 4.0, ALU.mult)
-        ts(R("pd", 32, 48), R("S4i", 0, 16), col("PF", 26), ALU.is_equal, 4.0, ALU.mult)
-        tt(R("Sd", 0, 24), R("pd", 8, 32), R("pd", 0, 24), ALU.subtract)
-        tt(R("pd", 48, 56), R("pd", 32, 40), R("pd", 40, 48), ALU.add)
         ts(R("pd", 64, 96), R("Pti", 0, 32), col("PF", 8), ALU.add, col("PF", 23), ALU.mult)
         ts(R("pd", 96, 128), R("Pti", 32, 64), col("PF", 27), ALU.mult)
-        tt(R("Sd", 24, 32), R("pd", 48, 56), R("pd", 0, 8), ALU.add)
-        tt(R("pd", 128, 160), R("pd", 64, 96), R("pd", 96, 128), ALU.add)
+        ts(R("ta", 0, 8), R("Pti", 144, 152), col("PF", 9), ALU.add)
         if 64 in WL:
             ts(R("Lp64", 0, 32, 2), R("Pti", 64, 80), col("PF", 8), ALU.add)
             cp(R("Lp64", 1, 32, 2), R("Pti", 32, 48))
-        cp(R("Lp32"), R("pd", 128, 160))
-        ts(R("ta", 0, 8), R("Pti", 144, 152), col("PF", 9), ALU.add)
         cp(R("Lth"), R("Pti", 80, 112))
+        tt(R("pd", 128, 160), R("pd", 64, 96), R("pd", 96, 128), ALU.add)
         ts(R("ta", 8, 16), R("ta", 0, 8), 8.0, ALU.is_lt)
         ts(R("Lx"), R("Pti", 112, 144), col("PF", 22), ALU.add)
-        tt(R("ta", 16, 24), R("ta", 0, 8), R("ta", 8, 16), ALU.mult)
         ts(R("BM"), R("BM"), col("PF", 4), ALU.is_equal)
-        ts(R("R12"), R("CI", 0, 32), col("PF", 5), ALU.is_equal)
-        ts(R("B16"), R("B16"), col("PF", 2), ALU.is_equal)
-        ts(R("Z3", 0, 96, 3), R("CI", 0, 32), 16.0, ALU.mult)
-        ts(R("Z3", 96, 192, 3), R("CI", 0, 32), 16.0, ALU.mult)
-        cp(R("Lw"), R("ta", 16, 24))
         ts(R("Lg"), R("ta", 0, 8), -1.0, ALU.add)
+        cp(R("Lp32"), R("pd", 128, 160))
+        tt(R("ta", 16, 24), R("ta", 0, 8), R("ta", 8, 16), ALU.mult)
+        ts(R("B16"), R("B16"), col("PF", 2), ALU.is_equal)
+        cp(R("Lw"), R("ta", 16, 24))
 
-    late()
-    hots_s(128 - NS0, 128)
-    if myt == 1:
-        nx_out()
-    for _ in range(HU if myt > 1 else 0):
+    if myt > 0:
+        late()
+    hots_s(128 - NS0[myt], 128)
+    for _ in range(HU):
         hot.pop(0)()
     nx_in(0)
+    for j in range(1, 4):
+        dma("Y", ap(blk("nxb", j, 1024)), ap(blk("nxb", 0, 1024)), "dfill", 48, [blk("nxb", j, 1024)], [blk("nxb", 0, 1024)])
 
     def go():
         if myt != 1:
@@ -872,34 +989,38 @@ def rank_program(g, core, T, topo):
         op("G", lambda: g.remote_dma_fused([RemoteDMATransfer(
             dst_ids=[dst(topo, hs[i])], dma_engine_mask=bits(rest[i:i + 1]), remote_sem=T.sem.go) for i in told],
             local_sem=T.sem.lsem), [], [], sem="remote")
-    u_in()
-    for _ in range(HV):
+    ts(R("Ln"), R("ps3", 0, 128), -64.0, ALU.add)
+    if myt == 1:
+        nx_out()
+    for _ in range(HV if myt != 1 else 0):
         hot.pop(0)()
     succ_a(0, 64)
     for j in range(2):
         act(blk("U5", j, 960), R("E", 0, 960), ACT.Identity, bias=1.0, scale=0.0)
-    succ_b()
+    succ_b(0)
+    u_in()
     act(R("U5", 0, 1920, 5), R("E", 0, 384), ACT.Identity, scale=0.0)
     go()
-    act(R("N1"), R("ps1", 384, 512), ACT.Copy)
     if myt > 1:
         nx_out()
-    for _ in range(HX + (24 if myt < 2 else 0)):
+    if myt == 0:
+        late()
+    ts(col("PF", 29), col("PF", 28), -1.0, ALU.add)
+    for _ in range(HX[myt]):
         hot.pop(0)()
     lists_c()
+    close = None
     for t in range(3):
-        gates(t)
+        gates(t, close)
         if t == 0:
             act(R("U5", 4, 1920, 5), R("ps5", 128, 512), ACT.Identity, scale=1.0 / 64)
-            for j in range(4):
-                act(blk("nxb", j, 1024), R("E", 0, 1024), ACT.Identity, bias=64.0, scale=0.0)
             act(R("I2k"), R("Ibf"), ACT.Identity, scale=2048.0)
             act(R("Dg"), R("Ibf"), ACT.Identity, scale=col("PF", 16))
             act(R("Bh"), R("B1"), ACT.Identity, scale=0.5)
             for w in sorted(set(WL)):
                 for j, v in enumerate((1.0 / w, 1024.0 / w, -1024.0 / w)):
                     act(blk("I%d" % w, j), R("Ibf"), ACT.Identity, scale=v)
-            hots_s(128 - NS[0], 128 - NS0)
+            hots_s(128 - NS[0], 128 - NS0[myt])
             nx_in(1)
 
         def between(extra):
@@ -909,28 +1030,42 @@ def rank_program(g, core, T, topo):
             bound(t - 1, extra)
             terms_b(t - 1, 0, TB1)
         draw(t, between)
-        after_draw(t)
+        close = after_draw(t)
 
+    close()
+    for a, b in ((0, 64), (64, 128 - YV)):
+        if a < b:
+            act(R("Y4", 16 * a, 16 * b), IND("D1", 0, DW, "Ls0", a, b), ACT.Identity, scale=0.25)
     marks_out(2)
-    terms_b(2, TBH, TB2)
+    if YV:
+        ts(R("Y4", 2048 - 16 * YV, 2048), IND("D1", 0, DW, "Ls0", 128 - YV, 128), 0.25, ALU.mult)
+    terms_b(1, TB3)
     terms_d()
+    terms_a(2, 0, 1024)
+    terms_a(2, 1024, 2048)
     for k in range(4):
         tt(R("dr", 384 + 128 * k, 512 + 128 * k), IND("pairb", 0, 128, "Lx", 8 * k, 8 * k + 8), R("BM"), ALU.mult)
         mm(blk("ps2", 2 * (k % 2) + k // 2, 32), R("dr", 384 + 128 * k, 512 + 128 * k), R("R12"))
-    for pr, n in enumerate(("G", "D1")):
-        ms(R(n, 0, 16), 0.0)
-        act(R(n, 16, 528), R("Y", 2 * pr, 2048, 4), ACT.Identity, scale=-1.0)
-        act(R(n, 528, 1040), R("Y", 2 * pr + 1, 2048, 4), ACT.Identity, scale=-1.0)
-        tt(R(n, 1040, 1552), R(n, 16, 528), R(n, 528, 1040), ALU.add)
-    bound(2)
+    terms_b(2, 0, TB2)
+    for h in range(2):
+        for k in range(4):
+            a = 16 + 512 * (k % 2) + 256 * h
+            y = blk(HELD[k], h, 256) if k < 3 else R("Y", 1024 * h + k, 1024 * h + 1024, 4)
+            tt(R(TABS[k // 2], a, a + 256), R("Y4", 1024 * h + k, 1024 * h + 1024, 4), y, ALU.subtract)
+    both = lambda n, a=0, b=512: tt(R(n, 1040 + a, 1040 + b), R(n, 16 + a, 16 + b), R(n, 528 + a, 528 + b), ALU.add)
+    both("G")
+    both("nxw", 0, SUM0)
+    bound(2, lambda: both("nxw", SUM0) if SUM0 < 512 else None)
     for j in range(2):
-        ts(R("Z3", j + 1, 192, 3), blk("ps2", j, 64), col("ps1", 1), ALU.is_lt, 512.0 * (j + 1), ALU.mult)
+        ts(R("Z3", j + 1, 192, 3), blk("ps2", j, 64), col("ps3", 257), ALU.is_lt, 512.0 * (j + 1), ALU.mult)
     scan(R("dr", 0, 192), R("r3"), R("Z3"))
     ts(R("Ln", 0, 64), R("dr", 2, 192, 3), col("PF", 17), ALU.add)
     for h in range(2):
         act(blk("Y4", h, 256), IND("G", 0, 1552, "Ln", 16 * h, 16 * h + 16), ACT.Identity)
+    act(R("tab", 0, 512), R("ps0"), ACT.Copy)
+    dma("S", T.ye[:], T.tab[:, 0:512], "doe", 16, [], [R("tab", 0, 512)])
     for h in range(2):
-        tt(blk("tab", 2 + h, 256), IND("D1", 0, 1552, "Ln", 32 + 16 * h, 48 + 16 * h), blk("Y4", h, 256), ALU.add)
+        tt(blk("tab", 2 + h, 256), IND("nxw", 0, 1552, "Ln", 32 + 16 * h, 48 + 16 * h), blk("Y4", h, 256), ALU.add)
         dma("YS"[h], T.yx[:, 256 * h:256 * h + 256], T.tab[:, 512 + 256 * h:768 + 256 * h], ("dox", "dox2")[h], 16, [],
             [blk("tab", 2 + h, 256)])
 

import numpy as np
from concourse.bass import DstId, RemoteDMATransfer
from concourse.mybir import AluOpType, ActivationFunctionType

ALU = AluOpType
ACT = ActivationFunctionType
F, B, I, U = "float32", "bfloat16", "int32", "uint16"
PW = 264
DW = 6176
MAG = 1.5 * 2.0 ** 23
CORES_IN_ALL = 128
DN = ("Db", "D1", "D1")
WL = (32, 64, 32)
ZA = (640, 768, 768)
CARRY = ((0, 2, 1), (0, 0, 1), (0, 0, 0))
NV = (3, 4, 4)
NVH = (12, 0, 0)
SI = ((), (0, 2, 1), (0, 2, 1))
TESTS = ((0, 1, 6, 2, 3, 7, 4, 5, 8), (4, 3, 7, 5, 6, 8), (4, 3, 7, 5, 6, 8))
PAYAT = ((2, 2), (3, 2))
LCAT = (99, 86)
Y4A = ((64, 96), (48, 64))
Y4V = ((0, 0), (0, 0))
MH = (None, None, None)
SPL = (48, 128)
PG = 16
HU = 30
HV = 24
HX = (4, 24, 0)
HF = 3
LO0 = 8
NS0 = (2, 8, 8)
NS = (48, 0, 32)
TA = 1024
TB3 = 4
TB1 = 4
HELD = ("ps5", "ps7", "ps1")
SUM0 = 352
TABS = ("G", "nxw")
D9 = True
WIDE = False
AH = (1, 0)
TB2 = 4
YV = 32

SB = {
    "z0": (4096, B), "z1": (4096, B), "z2": (4096, B),
    "nxi": (512, I), "nxs": (1024, U), "nxp": (1024, B), "nxw": (4096, F), "nxb": (4096, B), "Gb": (2048, B),
    "SCb": (24, B), "SDb": (24, B), "SD": (24, F),
    "hu": (512, I), "n0w": (1024, I),
    "D1": (DW, F), "ind": (6144, B), "OHh": (16384, B), "OHl": (4096, B),
    "Y": (2048, F), "Y4": (2048, F), "G": (2048, F), "Db": (DW, B), "E": (2048, F),
    "tab": (1024, F), "pay": (18 * PW, B),
    "U5": (1920, B), "C1": (384, F), "Vw": (640, B), "Pm": (640, F), "le0": (384, B), "le1": (384, B),
    "N1": (128, F), "live": (128, B), "took": (128, F), "T1": (128, F),
    "ta": (128, F), "tc": (128, F), "td": (128, B), "pairb": (128, F), "tabb": (1024, B),
    "dr": (3 * 384, F), "ne": (6 * 96, F), "e8": (16, F), "th": (16, F),
    "pd": (160, F), "pb": (384, B), "hi": (128, B), "lo": (128, B),
    "miss": (384, B), "mk": (256, B), "incl": (288, B), "X": (528, B), "rst32": (256, B), "rst64": (256, B), "ib": (256, B),
    "C32": (128, B), "C16": (128, B), "Df": (128, F), "mc": (32, F), "Lm": (32, U), "Hf": (256, B),
    "Ln": (128, U), "Ls0": (128, U), "Ls1": (128, U), "Li": (128, U), "LT": (128, U), "Lc": (384, U),
    "Lp32": (32, U), "Lp64": (32, U), "Lw": (8, U), "Lg": (8, U), "Lth": (32, U), "Lx": (32, U),
    "CI": (128, F), "S4i": (32, F), "Pti": (152, F), "PIi": (4, I), "PJ": (8, I), "PF": (32, F), "BM": (128, F),
    "Ibf": (128, B), "If": (128, F), "I2k": (128, B), "I32": (384, B), "I64": (384, B), "Dg": (128, B),
    "Ones": (128, B), "Tri": (128, B), "B1": (8, B), "Bh": (8, B), "SC": (24, F), "Sd": (32, B), "Su": (32, F), "R12": (32, F),
    "B16": (128, B), "Z3": (192, F), "r3": (192, B),
}
SCRATCH = {k: ("sbuf", [128, v[0]], v[1]) for k, v in SB.items()}
SB["nxv"] = (6, F)
SCRATCH["nxd"] = ("dram", [6, 128, 1024], B)
for _i in range(8):
    SCRATCH["ps%d" % _i] = ("psum", [128, 512], F)
SEMAPHORES = (["cV", "cS", "cP", "cG", "lsem", "dz", "dnx", "dhu", "duu", "dn0", "dx0", "doe", "dox", "dfill"]
              + ["zarr%d" % t for t in range(3)] + ["narr%d" % t for t in range(3)]
              + ["harr%d" % t for t in range(3)] + ["dw%d" % t for t in range(3)]
              + ["earr0", "earr1", "dox2", "go", "hm0", "hm1", "hk0", "hk1", "hk2"] + ["h" + n for n in ("n", "z0", "z1", "z2")]
              + ["r%s_%d" % (n, q) for n in ("n", "z0", "z1", "z2") for q in range(2, 6)] + ["ga%d" % i for i in range(16)])


def bits(es):
    m = 0
    for e in es:
        m |= 1 << e
    return m


def helpers_of(T, topo, c):
    hs = [h for h in topo.cores_of(c) if h != c and T.rank_of(h) is None and all(topo.may_write(h, d) for d in T.cores if d != c)]
    far = [h for h in hs if topo.die(h) != topo.die(c)]
    return [far[0], [h for h in hs if h not in far][0], far[1]]


def dst(topo, c):
    a = topo.addr(c)
    return DstId(rid=a[0], pnc=a[1])


PIECE = [[(0, a), (a, 2 * a), (2 * a, 2048)] for a in ZA]


def spread(T, topo, c):
    mate = lambda a, b: topo.mates(topo.chip(a), topo.chip(b))
    plane = [x for x in T.cores if topo.same_plane(topo.chip(x), topo.chip(c))]
    mates = [x for x in T.cores if mate(x, c)]
    far = [x for x in T.cores if x != c and x not in plane + mates]
    lone = [f for f in far if not any(mate(f, p) for p in plane)]
    way = {p: [f for f in far if mate(f, p)] for p in plane}
    way.update({twin(T, topo, f): [f] for f in lone})
    way.update({x: [] for x in mates})
    return dict(sorted(way.items(), key=lambda x: not x[1]))


def twin(T, topo, c):
    for k in range(CORES_IN_ALL):
        if topo.mates(topo.chip(k), topo.chip(c)):
            return topo.cores_of(k)[topo.cores_of(c).index(c)]


def loads_of(T, q):
    t, out = q // 2, []
    if t > 0:
        out.append((CARRY[t][2], "n", T.nxp[:, :], T.nxb[:, 1024 * (q - 2):1024 * (q - 1)], T.nxd[q], "narr%d" % t))
    for i, (a, b) in enumerate(PIECE[t]):
        home = T["z%d" % t][:, 2048 * (q % 2) + a:2048 * (q % 2) + b]
        out.append((CARRY[t][i], "z%d" % i, home, T.OHh[:, 2048 * q + a:2048 * q + b], home, "zarr%d" % t))
    return out


def helper_program(g, core, T, topo):
    mine = [c for c in T.cores + [twin(T, topo, x) for x in T.cores] if core in helpers_of(T, topo, c)]
    if not mine:
        return
    me = mine[0]
    which = helpers_of(T, topo, me).index(core)
    rank = T.rank_of(me)
    es = topo.engines(core, [d for d in T.cores if d != me][0])
    rest = [e for e in topo.engines(core, me) if e not in es]
    sent = [0]

    def write(*parts):
        parts = [x for x in parts if x[0]]
        g.remote_dma_fused([RemoteDMATransfer(dst_ids=[dst(topo, d) for d in to], dma_engine_mask=bits(e), remote_sem=T.sem[sm],
                                              srcs=[a], dsts=[b for _ in to]) for to, e, sm, a, b in parts], local_sem=T.sem.lsem)
        sent[0] += sum(len(x[1]) for x in parts)

    for t in range(3):
        pair = [(T.cores[q], [x for x in loads_of(T, q) if x[0] == which]) for q in (2 * t, 2 * t + 1)]
        for _, name, src, mid, home, arr in dict(pair).get(me, []):
            if t == 1:
                g.wait_ge(T.sem.go, 1)
            g.wait_ge(T.sem["h" + name], len(rest) // (2 if name in ("z0", "z1") else 1))
            if t == 0:
                to = sorted(T.cores[rank + 1:] + T.cores[:rank], key=lambda d: topo.same_plane(topo.chip(d), topo.chip(me)) == (which == 0))
                write((to, es, arr, src, home))
            else:
                write(([helpers_of(T, topo, x)[which] for x in spread(T, topo, me)], es, "r%s_%d" % (name, rank), src, mid))
        for li in range(len(pair[0][1]) if t > 0 else 0):
            for c, loads in pair:
                _, name, src, mid, home, arr = loads[li]
                if me in spread(T, topo, c):
                    g.wait_ge(T.sem["r%s_%d" % (name, T.rank_of(c))], len(es))
                    write(([me] if rank is not None else [], rest, arr, mid, home), (spread(T, topo, c)[me], es, arr, mid, home))
    for t in range(3 if rank is not None else 0):
        for d, a, b, sm, arr in ((1 if t < 2 else None, 256, 264, "hm", "earr"), (MH[t], 0, 256, "hk", "harr")):
            if d == which:
                x = T.pay[:, (6 * t + rank) * PW + a:(6 * t + rank) * PW + b]
                g.wait_ge(T.sem["%s%d" % (sm, t)], len(rest))
                write((T.cores[rank + 1:] + T.cores[:rank], es, "%s%d" % (arr, t), x, x))
    if sent[0]:
        g.wait_ge(T.sem.lsem, sent[0])


def rank_program(g, core, T, topo):
    rank = T.rank_of(core)
    if rank is None:
        helper_program(g, core, T, topo)
        return
    ops = []
    Q = {"V": g.vector, "S": g.scalar, "P": g.tensor, "G": g, "Y": g.sync}

    def R(n, a=0, b=None, s=1, p0=0, p1=128):
        if b is None:
            b = SB[n][0] if n in SB else 512
        return (n, a, b, s, p0, p1, None)

    def IND(n, a, b, o, oa, ob):
        return (n, a, b, 1, 0, 128, (o, oa, ob))

    def ap(x):
        if not isinstance(x, tuple):
            return x
        v = T[x[0]][x[4]:x[5], x[1]:x[2]:x[3]] if x[3] != 1 else T[x[0]][x[4]:x[5], x[1]:x[2]]
        if x[6] is not None:
            v = v.indirect(T[x[6][0]][:, x[6][1]:x[6][2]])
        return v

    def op(e, fn, w, r, sem=None):
        rr = []
        for x in r:
            if isinstance(x, tuple):
                rr.append(x)
                if x[6] is not None:
                    rr.append(R(x[6][0], x[6][1], x[6][2]))
        ops.append({"e": e, "fn": fn, "w": w, "r": rr, "sem": sem})

    def arrive(sem, val, w):
        ops.append({"e": None, "w": w, "sem": (sem, val)})

    def ts(o, i, s1, o0, s2=None, o1=None):
        if o1 is None:
            op("V", lambda: g.vector.tensor_scalar(ap(o), ap(i), ap(s1), None, o0), [o], [i, s1])
        else:
            op("V", lambda: g.vector.tensor_scalar(ap(o), ap(i), ap(s1), ap(s2), o0, o1), [o], [i, s1, s2])

    def tt(o, a, b, o0):
        op("V", lambda: g.vector.tensor_tensor(ap(o), ap(a), ap(b), o0), [o], [a, b])

    def cp(o, i):
        op("V", lambda: g.vector.tensor_copy(ap(o), ap(i)), [o], [i])

    def ms(o, v):
        op("V", lambda: g.vector.memset(ap(o), v), [o], [])

    def scan(o, d0, d1):
        op("V", lambda: g.vector.tensor_tensor_scan(ap(o), ap(d0), ap(d1), 0.0, ALU.mult, ALU.add), [o], [d0, d1])

    def act(o, i, f, bias=0.0, scale=1.0):
        op("S", lambda: g.scalar.activation(ap(o), ap(i), f, bias=ap(bias), scale=ap(scale)), [o], [i, bias, scale])

    def sel(o, i, pat, cmp, base, cm):
        op("G", lambda: g.affine_select(ap(o), ap(i), pat, cmp, 0.0, base, cm), [o], [i])

    def mm(o, l, r, st=True, sp=True):
        op("P", lambda: g.tensor.matmul(ap(o), ap(l), ap(r), st, sp), [o], [l, r])

    def dma(e, o, i, sem, val, w, r):
        op(e, lambda: Q[e].dma_start(o, i), w, r, sem=(sem, val))

    nadd = [0]

    def add(o, i):
        nadd[0] += 1
        op("G", lambda: g.dma_start(ap(o), ap(i), accum_op=ALU.add), [o], [o, i], sem=("ga%d" % (nadd[0] - 1), 16))

    def iota(o, pat, cm, base=0):
        if SB[o[0]][1] == I:
            op("G", lambda: g.iota(ap(o), pat, base, cm), [o], [])
        else:
            op("G", lambda: g.iota(ap(o), pat, base, cm, allow_small_or_imprecise_dtypes=True), [o], [])

    others = T.cores[rank + 1:] + T.cores[:rank]
    off = topo.engines(core, others[0])
    noff = len(off)
    lsum = [0]

    def send(src, sem):
        lsum[0] += noff
        op("G", lambda: g.remote_dma_fused([RemoteDMATransfer(
            dst_ids=[dst(topo, d) for d in others], dma_engine_mask=bits(off), remote_sem=T.sem[sem],
            srcs=[ap(src)], dsts=[ap(src) for _ in others])], local_sem=T.sem.lsem), [], [src], sem="remote")

    myt, myb = rank // 2, rank % 2
    zown = R("z%d" % myt, 2048 * myb, 2048 * myb + 2048)
    col = lambda n, j: R(n, j, j + 1)
    blk = lambda n, j, w=128: R(n, w * j, w * j + w)

    def load_nx():
        for gi in range(9):
            e = "S" if gi % 2 == 0 else "Y"
            if gi < 7:
                o, i = T.nxi[16 * gi:16 * gi + 16, :], T.nx[3 * gi:3 * gi + 4, :]
            elif gi == 7:
                o, i = T.nxi[112:124, :], T.nx[21:24, :]
            else:
                o, i = T.nxi[124:128, :], T.nx[0:1, :]
            dma(e, o, i, "dnx", 144, [R("nxi")] if gi == 8 else [], [])

    if myt == 0:
        dma("Y", ap(zown), T.z[:], "dz", 16, [zown], [])
    dma("S", T.hu[:, 0:128], T.hyp[:], "dhu", 16, [R("hu", 0, 128)], [])
    if myt == 0:
        load_nx()
    dma("S", T.E[:, 0:1024], T.x0[:], "dx0", 16, [R("E", 0, 1024)], [])
    op("V", lambda: g.vector.memset(T.n0w[:, :], 0), [R("n0w")], [])
    dma("S", T.n0w[0:128:16, :], T.n0[:], "dn0", 16, [R("n0w")], [])
    if myt > 0:
        dma("Y", ap(zown), T.z[:], "dz", 16, [zown], [])
        load_nx()

    iota(R("PIi", 0, 1), [[1, 1]], 1)
    iota(R("CI"), [[1, 128]], 0)
    iota(R("S4i"), [[4, 4], [16, 8]], 0)
    iota(blk("nxw", 0, 1024), [[1, 1024]], 0, 64)

    def g_early():
        dma("G", T.hu[:, 128:512], T.uu[:], "duu", 16, [R("hu", 128, 512)], [])
    if myt > 0:
        g_early()
    ts(col("PJ", 0), col("PIi", 0), 15, ALU.bitwise_and)
    ts(col("PJ", 1), col("PIi", 0), 4, ALU.arith_shift_right)
    ts(col("PJ", 2), col("PIi", 0), 2, ALU.arith_shift_right, 3, ALU.bitwise_and)
    ts(col("PJ", 3), col("PIi", 0), 3, ALU.bitwise_and)
    ts(col("PJ", 4), col("PIi", 0), 2, ALU.arith_shift_right)
    cp(col("PF", 0), col("PIi", 0))
    cp(R("PF", 1, 6), R("PJ", 0, 5))
    ts(R("If"), R("CI"), col("PF", 0), ALU.is_equal)
    ts(R("SC", 0, 24), R("S4i", 0, 24), col("PF", 0), ALU.is_equal)
    ts(R("PF", 12, 16), R("CI", 0, 4), col("PF", 3), ALU.is_equal)
    ts(col("PF", 7), col("PF", 2), 4.0, ALU.mult, col("PF", 4), ALU.add)
    ms(R("live"), 1.0)
    ts(R("Su"), R("CI", 0, 32), col("PF", 7), ALU.is_equal)

    def early():
        for j, src, v, o in ((16, 0, 16.0, ALU.mult), (6, 1, 19.5 - 2032.0, ALU.add), (25, 1, 35.5 - 2032.0, ALU.add),
                             (26, 0, -2.0, ALU.add), (17, 1, -496.0, ALU.add), (23, 1, 8.0, ALU.is_lt), (27, 1, 8.0, ALU.is_ge),
                             (9, 3, 1.0, ALU.add), (10, 5, 4.0, ALU.mult), (11, 4, 3.0, ALU.is_lt), (22, 4, 4.0, ALU.mult),
                             (8, 1, 4.0, ALU.mult), (18, 0, -1.0, ALU.add), (19, 0, 127.0, ALU.add)):
            ts(col("PF", j), col("PF", src), v, o)
        ts(col("PF", 31), col("PF", 0), 64.0, ALU.is_lt, 8.0, ALU.mult)
        ts(R("B1"), R("CI", 0, 8), col("PF", 2), ALU.is_equal)
        ms(R("Db", 0, 16), 0.0)
        for d in DN[:2]:
            ms(R(d, DW - 16, DW), 4000.0)
        ts(col("PF", 30), col("PF", 31), -4.0, ALU.add)
        ts(R("dr", 0, 128), R("CI"), col("PF", 18), ALU.is_equal, -0.5, ALU.mult)
        ts(R("dr", 128, 256), R("CI"), col("PF", 19), ALU.is_equal, 0.5, ALU.mult)
        ts(R("Df"), R("If"), 0.5, ALU.mult)
        ts(R("SCb"), R("S4i", 0, 24), col("PF", 10), ALU.is_equal, col("PF", 11), ALU.mult)
        ts(R("pd", 0, 32), R("S4i"), col("PF", 0), ALU.is_equal, 4.0, ALU.mult)
        ts(R("pd", 32, 48), R("S4i", 0, 16), col("PF", 26), ALU.is_equal, 4.0, ALU.mult)
        tt(R("dr", 256, 384), R("dr", 0, 128), R("dr", 128, 256), ALU.add)
        for a, b in (("SD", "SC"), ("SDb", "SCb")):
            cp(R(a, 0, 8), R(b, 0, 8))
            tt(R(a, 8, 24), R(b, 8, 24), R(b, 0, 16), ALU.subtract)
        tt(R("pd", 48, 56), R("pd", 32, 40), R("pd", 40, 48), ALU.add)
        tt(R("Df"), R("Df"), R("dr", 256, 384), ALU.add)
        tt(R("Sd", 0, 24), R("pd", 8, 32), R("pd", 0, 24), ALU.subtract)
        ts(R("Lm"), R("S4i"), 0.25, ALU.mult)
        tt(R("Sd", 24, 32), R("pd", 48, 56), R("pd", 0, 8), ALU.add)
        ts(R("R12"), R("CI", 0, 32), col("PF", 5), ALU.is_equal)
        ts(R("Z3", 0, 96, 3), R("CI", 0, 32), 16.0, ALU.mult)
        ts(R("Z3", 96, 192, 3), R("CI", 0, 32), 16.0, ALU.mult)

    for a in range(4):
        ts(R("D1", a, 512, 4), R("hu", 0, 128), col("PF", 12 + a), ALU.mult)
    for k in range(4):
        mm(R("ps5", k, 128, 4), blk("D1", k), R("Su"))
    cp(R("Ibf"), R("If"))
    if myt == 0:
        early()
    cp(R("took"), R("ps5", 0, 128))
    mm(R("ps2", 0, 128), R("took"), R("If"))

    def nx_out():
        if myt == 0:
            cp(blk("nxs", rank, 512), R("nxi"))
        else:
            ts(R("nxp", 0, 512), R("nxi"), 64 * MAG, ALU.add, 64 * MAG, ALU.subtract)
            tt(R("nxp", 512, 1024), R("nxi"), R("nxp", 0, 512), ALU.subtract)
            hand([(CARRY[myt][2], "hn", R("nxp"))])

    hs = helpers_of(T, topo, core)
    rest = [e for e in topo.engines(core, hs[0]) if e not in off]

    def hand(what):
        n = len(rest) // len(what)
        lsum[0] += len(rest)
        op("G", lambda: g.remote_dma_fused([RemoteDMATransfer(
            dst_ids=[dst(topo, hs[d])], dma_engine_mask=bits(rest[n * i:n * i + n]), remote_sem=T.sem[sm], srcs=[ap(x)], dsts=[ap(x)])
            for i, (d, sm, x) in enumerate(what)], local_sem=T.sem.lsem), [], [x for _, _, x in what], sem="remote")

    def sends():
        piece = lambda i: R(zown[0], zown[1] + PIECE[myt][i][0], zown[1] + PIECE[myt][i][1])
        hand([(CARRY[myt][i], "hz%d" % i, piece(i)) for i in range(2)])
        if myt == 0:
            send(blk("nxs", rank, 512), "narr0")
        hand([(CARRY[myt][2], "hz2", piece(2))])

    for t in range(3):
        fz = [q for q in (2 * t, 2 * t + 1) if q != rank]
        arrive("zarr%d" % t, 3 * noff * len(fz), [blk("z%d" % t, q % 2, 2048) for q in fz])
        arrive("narr%d" % t, noff * len(fz), [blk("nxs", q, 512) if t == 0 else col("nxv", q) for q in fz])
    if myt == 0:
        nx_out()
    sends()
    if myt == 0:
        g_early()
    iota(R("Pti", 0, 32), [[32, 8], [1, 4]], 0)
    iota(R("Pti", 32, 64), [[1, 8], [8, 4]], 0, 256)
    iota(R("Pti", 64, 80), [[64, 4], [1, 4]], 0)
    iota(R("Pti", 80, 112), [[0, 4], [1, 8]], 0)
    iota(R("Pti", 112, 144), [[1, 4], [16, 8]], 0)
    iota(R("Pti", 144, 152), [[0, 4], [4, 2]], 0)
    iota(R("BM"), [[0, 8], [1, 4], [0, 4]], 0)
    iota(R("B16"), [[1, 8], [0, 16]], 0)

    for j in range(1, 4):
        act(blk("nxw", j, 1024), blk("nxw", 0, 1024), ACT.Identity)
    ts(R("pairb"), R("ps5", 0, 128), 4.0, ALU.mult, -15.5, ALU.add)
    ts(R("C32"), R("CI"), 32.0, ALU.mult)
    ts(R("C16"), R("CI"), 32.0, ALU.mult, -16.0, ALU.add)
    ts(R("hi"), R("pairb"), 32 * MAG, ALU.add, 32 * MAG, ALU.subtract)
    ts(R("T1"), R("ps5", 0, 128), 4.0, ALU.mult, 4.0, ALU.add)
    cp(R("LT"), R("ps2", 0, 128))
    ms(R("Ones"), 1.0)
    ms(R("Vw", 0, 640, 5), 2.0)
    ms(R("Vw", 4, 640, 5), 0.0)
    act(blk("G", 0, 1024), IND("n0w", 0, 1024, "LT", 0, 64), ACT.Identity)
    cp(blk("G", 1, 1024), IND("n0w", 0, 1024, "LT", 64, 128))
    for r in range(16):
        mm(R("ps1", r, 128, 16), R("G", r, 2048, 16), R("SC", 0, 8))
    act(blk("Y", 0, 1024), IND("E", 0, 1024, "LT", 0, 64), ACT.Identity, scale=-1.0)
    act(R("N1"), R("ps1", 0, 128), ACT.Identity, bias=64.0)
    mm(R("ps3", 0, 128), R("N1"), R("If"))
    act(blk("Y", 1, 1024), IND("E", 0, 1024, "LT", 64, 128), ACT.Identity, scale=-1.0)

    def u_in():
        for a in range(4):
            ts(R("D1", 512 + a, 2048, 4), R("hu", 128, 512), col("PF", 12 + a), ALU.mult)
        for kk in range(4, 16):
            mm(blk("ps5", kk, 32), blk("D1", kk), R("Su"))

    def nx_in(t):
        for b in range(2):
            q = 2 * t + b
            if t == 0:
                ts(blk("Y4", b, 512), blk("nxs", b, 512), 64.0, ALU.add)
                dma("Y", T.nxw[0:128:4, 2048 * b:2048 * b + 2048], T.Y4[:, 512 * b:512 * b + 512], "dw0", 32,
                    [blk("nxw", b, 2048)], [blk("Y4", b, 512)])
                continue
            for i in range(2):
                src, r = (T.nxp[:, 512 * i:512 * i + 512], R("nxp")) if q == rank else (T.nxd[q, :, 512 * i:512 * i + 512], col("nxv", q))
                dma("Y", T.nxb[i:128:4, 2048 * b:2048 * b + 2048], src, "dw%d" % t, 64, [blk("nxb", b, 2048)], [r])

    act(col("PF", 28), col("PF", 0), ACT.Exp, bias=-1.0, scale=0.0)

    def hots():
        return [lambda c=c: ts(blk("OHh", c), R("C32"), col("hi", c), ALU.is_equal) for c in range(128)]

    def hots_s(c0, c1=128):
        for c in range(c0, c1):
            act(blk("OHh", c), R("C16"), ACT.Sign, bias=col("hi", c), scale=-1.0)

    def place_list(t):
        w = WL[t]
        mm(R("ps2", 256, 384), R("hi"), blk("I%d" % w, 0), True, False)
        mm(R("ps2", 256, 384), R("lo"), blk("I%d" % w, 1), False, False)
        for m in range(3):
            mm(R("ps2", 256, 384), blk("le%d" % (t % 2), m), blk("I%d" % w, 2), False, m == 2)

    def dead_mask(t):
        ts(R("td"), R("live"), -16384.0, ALU.mult, 16384.0 - 3.5 - WL[t] / 2, ALU.add)

    def succ_a(t, split):
        w, n, l, o, sel = ("nxb", 4096, "Ln", "Gb", "SCb") if t > 0 else ("nxw", 4096, "Ln", "G", "SC")
        if split:
            act(R(o, 0, 16 * split), IND(w, 0, n, l, 0, split), ACT.Identity)
        if split < 128:
            cp(R(o, 16 * split, 2048), IND(w, 0, n, l, split, 128))
        for r in range(16):
            mm(R("ps1", r, 16 * SB[sel][0], 16), R(o, r, 2048, 16), R(sel))

    def succ_b(t):
        for m in (1, 0, 2):
            act(blk("C1", m), blk("ps1", m), ACT.Copy)
            mm(listed(m), blk("C1", m), R("If"))

    listed = lambda m: blk("ps7", 0) if m == 1 else blk("ps3", m)

    def succ_c(t):
        for r in range(16):
            mm(R("ps1", r, 384, 16), R("Gb" if t > 0 else "G", r, 2048, 16), R("SDb" if t > 0 else "SD"))

    def lists_c(ms_=(1, 0, 2)):
        for m in ms_:
            ts(blk("Lc", m), listed(m), -64.0, ALU.add)

    def chunk(t, ch, by_v, a=0, b=64):
        d = R(DN[t], 16 + 1024 * ch + 16 * a, 16 + 1024 * ch + 16 * b)
        w = IND("z%d" % t, 0, 4096, "Lc", 64 * ch + a, 64 * ch + b)
        y = R("Y", 1024 * (ch % 2) + 16 * a, 1024 * (ch % 2) + 16 * b)
        if by_v:
            tt(d, w, y, ALU.add)
        else:
            act(d, w, ACT.Identity)
            add(d, y)

    def gate(t, m):
        big = 2 * MAG
        d = lambda ch, a=0, b=1024: R(DN[t], 16 + 1024 * ch + a, 16 + 1024 * ch + b)
        for ch in m:
            if ch in SI[t]:
                at = 1024 * (SI[t].index(ch) % 2)
                for a in (0, 512):
                    act(R("G", at + a, at + a + 512), d(ch, a, a + 512), ACT.Abs)
                for a in (0, 512):
                    act(R("ind", 1024 * ch + a, 1024 * ch + a + 512), R("G", at + a, at + a + 512), ACT.Sign, bias=1.0 + 2.0 ** -12, scale=-1.0)
                continue
            if ch == 5:
                weights(t, 0, 2)
            ts(blk("ind", ch, 1024), d(ch), big, ALU.add, big, ALU.is_equal)

    def count(t, m, rs=range(16)):
        both = (2 * m in SI[t]) == (2 * m + 1 in SI[t])
        for h, n in ((0, 2),) if both else ((0, 1), (1, 1)):
            for r in rs:
                o = ("ps7", 128 * (r % 4) + 4 * (r // 4) + m + 1, 128 * (r % 4) + 128, 16) if m < 2 or r % 4 else ("ps3", 384 + r // 4, 416, 4)
                a = 2048 * m + 1024 * h
                mm(R(*o, 64 * h, 64 * (h + n)), R("ind", a + r, a + 1024 * n, 16), R("Bh" if 2 * m + h in SI[t] else "B1"))

    def weights(t, a, b):
        for i in range(a, b):
            if i == 0 and t > 0:
                ts(R("e8", 0, 8), R("ps1", 400, 408), 1.0 / 2048, ALU.mult, 0.5 + 2.0 ** -12, ALU.add)
                ts(R("Li"), R("ps2", 256, 384), 512.0 - 512.0 / WL[t - 1], ALU.add, 1023.0, ALU.min)
            elif i == 1 and t > 0:
                ts(R("Vw", 0, 640, 5), IND("e8", 0, 16, "Lw", 0, 8), MAG, ALU.add, MAG, ALU.subtract)
            elif i in (2, 3):
                m = 3 - i
                less = col("PF", 30) if 2 * m in SI[t] and 2 * m + 1 not in SI[t] else 4.0 if 2 * m in SI[t] else -4.0
                ts(R("Vw", m + 1, 640, 5), R("ps7", m + 1, 512, 4), less, ALU.add, 0.0, ALU.max)
            elif i == 4:
                count(t, 2, [r for r in range(16) if r % 4])
                ts(R("Vw", 3, 160, 5), R("ps3", 384, 416), -4.0, ALU.add, 0.0, ALU.max)
            elif i == 5:
                ts(R("Vw", 163, 640, 5), R("ps7", 131, 512, 4), -4.0, ALU.add, 0.0, ALU.max)

    def terms_a(t, a=0, b=2048):
        halves = ((a, (a + b) // 2), ((a + b) // 2, b))
        for a, b in halves:
            act(R("E", a, b), R("Y4", a, b), ACT.Abs, scale=4.0)
        for a, b in halves:
            act(R("E", a, b), R("E", a, b), ACT.Exp, scale=-1.0)

    def terms_b(t, a=0, b=8):
        for i in range(a, b):
            k, h = i % 4, i // 4
            mm(blk("ps0", h, 256), R("If"), R("E", 1024 * h + k, 1024 * h + 1024, 4), False, t == 2 and i == 7)

    def terms_c():
        for i in range(12):
            mm(R("ps6", 384, 416), R("Ibf"), R("miss", 128 * (i // 4) + i % 4, 128 * (i // 4) + 128, 4), i == 0, i == 11)

    def terms_c2(step):
        if step == 0:
            act(R("mc"), R("ps6", 384, 416), ACT.Identity, scale=col("PF", 29))
            return
        act(R("nxw", 2048, 2560), IND("mc", 0, 32, "Lm", 0, 32), ACT.Identity)

    def terms_d():
        for sl in range(4):
            mm(R("ps0", sl, 512, 4), blk("nxw", 16 + sl), R("If"), False, False)

    begun = {}

    def bound_a(t, i):
        w = WL[t]
        n = 256 // w
        for j in range(begun.get(t, 0), i + 1):
            if j == 0:
                for q in range(6):
                    b = (6 * t + q) * PW
                    mm(R("ps4", 0, 256), R("Ibf"), R("pay", b, b + 256), q == 0, q == 5)
                ts(R("mk"), R("ps4", 0, 256), 1.0, ALU.min)
            if j == 1:
                scan(R("incl", 0, 256), R("rst%d" % w), R("mk"))
                for p0, p1 in [(0, 128)] if w == 32 else [(0, 64), (64, 128)]:
                    mm(R("ps4", 384, 384 + n, 1, p0, p1), R("Tri", p0, p1, 1, p0, p1), R("incl", w - 1, 256, w, p0, p1))
            if j == 2 and t < 2:
                ts(R("incl", 256, 256 + n), R("ps4", 384, 384 + n), 32 * MAG, ALU.add, 32 * MAG, ALU.subtract)
        begun[t] = max(begun.get(t, 0), i + 1)

    def bound(t, extra=((), (), (), ())):
        w = WL[t]
        n = 256 // w
        parts = [(0, 128)] if w == 32 else [(0, 64), (64, 128)]
        rst = R("rst%d" % w)
        pre = R("ps4", 384, 384 + n)
        bound_a(t, 2)
        if t == 2:
            terms_b(2, TB2, TB2 + 1)

        def digits():
            tt(R("incl", 264, 264 + n), pre, R("incl", 256, 256 + n), ALU.subtract)
            act(R("X", 0, 512), IND("incl", 0, 288, "Lp%d" % w, 0, 32), ACT.Identity)

        def table():
            for tl in range(w // 4):
                for p0, p1 in parts:
                    c, st = (p1 - p0) * tl, w // 8
                    mm(R("ps%d" % (5 + c // 512), c % 512, c % 512 + p1 - p0, 1, p0, p1),
                       R("X", tl, tl + 512 - st + 1, st, p0, p1), R("Ibf", p0, p1, 1, p0, p1))
        for gi in range(n):
            if t < 2 and gi == 2:
                digits()
            ts(blk("ib", gi, w), blk("incl", gi, w), col("ps4", 384 + gi), ALU.add, 1024.0, ALU.is_le)
        if t == 2:
            for j in range(2):
                mm(col("ps3", 256), R("ib", j, 256, 2), col("Ones", 0), j == 0, j == 1)
            extra()
            cp(col("mk", 0), col("ps3", 256))
            mm(col("ps3", 257), R("B16"), col("mk", 0))
            terms_b(2, TB2 + 1)
            return
        for f in extra[0]:
            f()
        scan(R("mk"), rst, R("ib"))
        for f in list(extra[1]) + list(extra[2]):
            f()
        for h, (p0, p1) in enumerate(parts):
            mm(R("ps2", n * h, n * h + n), R("Ones") if w == 32 else blk("Hf", h), R("mk", w - 1, 256, w))
        table()
        cp(R("th", 0, 8), R("ps2", 0, 8))
        for f in extra[3]:
            f()
        tt(R("live"), IND("th", 0, 16, "Lth", 0, 8), R("pairb"), ALU.is_gt)

    def misses_out(t):
        b = (6 * t + rank) * PW + 256
        act(R("pay", b, b + 8), R("ps4", 256, 264), ACT.Copy)
        hand([(1, "hm%d" % t, R("pay", b, b + 8))])
        arrive("earr%d" % t, 5 * noff, [R("pay", (6 * t + q) * PW + 256, (6 * t + q) * PW + 264) for q in range(6) if q != rank])

    def miss_weight(t):
        for q in range(6):
            b = (6 * t + q) * PW
            mm(R("ps1", 400, 408), R("Ones"), R("pay", b + 256, b + 264), q == 0, q == 5)

    def places_b():
        act(R("tabb", 0, 512), R("ps5"), ACT.Copy)
        act(R("tabb", 512, 1024), R("ps6"), ACT.Copy)
        act(R("Gb", 0, 2048 - 16 * PG), IND("tabb", 0, 1024, "Li", 0, 128 - PG), ACT.Identity)

    def places_v():
        cp(R("Gb", 2048 - 16 * PG, 2048), IND("tabb", 0, 1024, "Li", 128 - PG, 128))
        for r in range(16):
            mm(R("ps3", r, 384, 16), R("Gb", r, 2048, 16), R("Sd", 0, 24))
        mm(R("ps6", 0, 128), R("Ibf"), R("td"), True, False)
        for r in range(16):
            mm(R("ps6", r, 128, 16), R("Gb", r, 2048, 16), R("Sd", 24, 32), False, False)

    def places_c(t):
        tt(R("pb"), R("ps3", 0, 384), R("le%d" % (t % 2)), ALU.mult)

    def slots(t):
        o = blk("ps7" if t < 2 else "ps2", 1)
        for m in range(3):
            mm(o, blk("le%d" % (t % 2), m), R("I2k"), m == 0, False)
        mm(o, R("td"), R("Ibf"), False, False)
        mm(o, R("Ones"), R("Dg"), False, True)

    def high(t):
        ts(R("hi"), R("ps6", 0, 128), WL[t] * MAG, ALU.add, WL[t] * MAG, ALU.subtract)

    def slot_list(t):
        ts(R("Ls%d" % (t % 2)), blk("ps7" if t < 2 else "ps2", 1), col("PF", 6 if WL[t] == 32 else 25), ALU.add, float(DW - 16), ALU.min)

    def draw(t, between):
        le = "le%d" % (t % 2)
        sl = lambda n, m, k: R(n, 128 * m + k, 128 * m + 128, 4)

        def gap(n, calls=()):
            for f in calls:
                f()
            for _ in range(max(0, n - len(calls)) if t == 0 else 0):
                if len(hot) > NS[0]:
                    hot.pop(0)()

        def idle(i):
            if t > 0 and i >= AH[0]:
                bound_a(t - 1, i - AH[0])

        def ne(j, k, m, x=None, y=None):
            b = 96 * (j * (7 - j) // 2 + k - j - 1) + 32 * m
            tt(R("ne", b, b + 32), x or sl("C1", m, k), y or sl("took", 0, j), ALU.not_equal)

        def mul(j, k, m):
            b = 96 * (j * (7 - j) // 2 + k - j - 1) + 32 * m
            v = R("Vw", 160 * k + m + 1, 160 * k + 160, 5)
            tt(v, v, R("ne", b, b + 32), ALU.mult)

        weights(t, 2, 5)
        if t == 0:
            dead_mask(0)
        nes = lambda j, k: [lambda m=m: ne(j, k, m) for m in range(3)]
        muls = lambda j, k: [lambda m=m: mul(j, k, m) for m in range(3)]
        later = {(1, 0): nes(0, 2), (1, 5): muls(0, 2)[:2], (1, 1): muls(0, 2)[2:] + nes(0, 3)[:1], (1, 2): nes(0, 3)[1:], (1, 4): muls(0, 3),
                 (2, 0): nes(1, 3), (2, 5): muls(1, 3)[:2], (2, 1): muls(1, 3)[2:]}
        if not WIDE:
            later = {(1, 0): nes(0, 2), (1, 1): muls(0, 2), (1, 2): nes(0, 3), (1, 4): muls(0, 3), (2, 0): nes(1, 3), (2, 1): muls(1, 3)}
        if not D9:
            a, b = nes(0, 2) + muls(0, 2) + nes(0, 3) + muls(0, 3), nes(1, 3) + muls(1, 3)
            later = {(1, 0): a[0:3], (1, 5): a[6:8], (1, 1): a[3:5], (1, 2): a[5:6] + a[8:9], (1, 3): a[9:11], (1, 4): a[11:],
                     (2, 0): b[0:2], (2, 5): b[2:3], (2, 1): b[3:4], (2, 2): b[4:5], (2, 3): b[5:]}

        def wait(k, i, n):
            gap(n, later.get((k, i), []))
        gap(HF)
        for k in range(4):
            b0 = 384 * (k % 3)
            d = lambda i: R("dr", b0 + 32 * i, b0 + 32 * i + 32)
            pm = lambda m: R("Pm", 160 * k + m, 160 * k + 160, 5)
            scan(blk("Pm", k, 160), blk("U5", 4 * t + k, 160), blk("Vw", k, 160))
            wait(k, 0, HF + 1)
            if k == 0:
                idle(0)
            if k == 3:
                if t > 0:
                    places_c(t - 1)
                parts = [(R("If"), R("T1")), (R("Ibf"), R("td"))] if t == 0 else [(R("Ibf"), blk("pb", m)) for m in range(3)]
                for i, (a, b) in enumerate(parts):
                    mm(R("ps6", 0, 128), a, b, i == 0 and t == 0, False)
            for m in range(3):
                tt(sl(le, m, k), pm(m), pm(4), ALU.is_le)
            if k == 3:
                if t < 2:
                    slots(t)
                for m in range(3):
                    mm(R("ps6", 0, 128), R("Ibf"), blk(le, m), False, m == 2)
                if t == 2:
                    slots(t)
                    break
            if WIDE:
                wait(k, 5, HF - 1)
                tt(R("dr", b0 + 160, b0 + 256), R("ps1", k, 384, 4), R(le, k, 384, 4), ALU.mult)
            else:
                if k == 0:
                    weights(t, 5, 6)
                else:
                    wait(k, 5, HF - 2)
                for m in range(3):
                    tt(d(5 + m), sl("ps1", m, k), sl(le, m, k), ALU.mult)
            if k == 3:
                tt(blk("miss", t), R("live"), blk(le, 0), ALU.is_gt)
            else:
                wait(k, 1, HF - 1)
            if k == 0:
                idle(1)
            tt(d(8), d(5), d(6), ALU.add)
            if k == 0:
                idle(2)
            if k == 0 and t > 0:
                tt(sl("took", 0, k), d(8), d(7), ALU.add)
                extra = [nes(0, 1), [lambda: ts(R("dr", 288, 384), R("ne", 0, 96), 16384.0, ALU.mult)],
                         [lambda m=m: tt(d(m), d(9 + m), sl("pairb", 0, 0), ALU.max) for m in range(3)],
                         [lambda: tt(R("ne", 0, 96), IND("th", 0, 16, "Lg", 0, 6), R("dr", 0, 96), ALU.is_le)]]
                for i in range(AH[1]):
                    for f in extra[i]:
                        f()
                    extra[i] = []
                between(extra)
                u5 = lambda k2: R("U5", 640 * t + 160 * k2 + 4, 640 * t + 160 * k2 + 160, 5)
                for m in range(3):
                    mul(k, k + 1, m)
                tt(u5(1), u5(1), sl("live", 0, 1), ALU.mult)
                tt(sl("took", 0, 0), sl("took", 0, 0), sl("live", 0, 0), ALU.mult)
                tt(u5(2), u5(2), sl("live", 0, 2), ALU.mult)
                dead_mask(t)
                places_b()
                if TA < 2048:
                    terms_a(t - 1, TA)
            elif k < 3 and not D9:
                wait(k, 2, HF - 1)
                tt(sl("took", 0, k), d(8), d(7), ALU.add)
                wait(k, 3, HF - 1)
                for m in range(3):
                    ne(k, k + 1, m)
                wait(k, 6, 0)
                for m in range(3):
                    mul(k, k + 1, m)
                wait(k, 4, HF)
                if t > 0 and k == 1:
                    places_v()
            elif k < 3:
                for m in range(3):
                    tt(d(9 + m), sl("C1", m, k + 1), d(7), ALU.subtract)
                wait(k, 2, HF - 2)
                for m in range(3):
                    ne(k, k + 1, m, d(9 + m), d(8))
                tt(sl("took", 0, k), d(8), d(7), ALU.add)
                wait(k, 3, HF - 3)
                for m in range(3):
                    mul(k, k + 1, m)
                wait(k, 4, HF)
                if t > 0 and k == 1:
                    places_v()
            else:
                slot_list(t)
                tt(R("tc"), blk("miss", t), R("N1"), ALU.mult)
                tt(sl("took", 0, k), d(8), d(7), ALU.add)
                if t == 1:
                    high(t)
                    ts(R("pairb"), R("ps6", 0, 128), WL[t] / 2 - 0.5, ALU.add)
                tt(R("lo"), R("ps6", 0, 128), R("hi"), ALU.subtract)

    def marks_out(t):
        b = (6 * t + rank) * PW
        n = 256
        ts(R("pay", b, b + 256), R("ps4", 0, 256), 1.0, ALU.min)
        if MH[t] is None:
            send(R("pay", b, b + n), "harr%d" % t)
        else:
            hand([(MH[t], "hk%d" % t, R("pay", b, b + n))])
        arrive("harr%d" % t, 5 * noff, [R("pay", (6 * t + q) * PW, (6 * t + q) * PW + n) for q in range(6) if q != rank])

    def after_draw(t):
        le, ls, dd = "le%d" % (t % 2), "Ls%d" % (t % 2), DN[t]
        w = WL[t]
        pr = R("ps6", 0, 128)

        if t < 2:
            mm(R("ps2", 0, 128), R("tc"), R("If"), True, False)
            mm(R("ps2", 0, 128), R("took"), R("If"), False, True)
        if t == 1:
            terms_b(0, TB1)
        if t == 2:
            tt(blk("miss", t), R("live"), blk(le, 0), ALU.is_gt)
            terms_b(1, TB1, TB3)
            for k in range(3):
                mm(R(HELD[k]), R("If"), R("Y", k, 2048, 4))
            high(t)
            ts(R("pairb"), pr, w / 2 - 0.5, ALU.add)
            ms(R(TABS[0], 0, 16), 0.0)
            ts(R("ib", 0, 128), R("hi"), 8192.0, ALU.min)
            slot_list(2)
            ms(R(TABS[1], 0, 16), 0.0)
            tt(R("lo"), pr, R("ib", 0, 128), ALU.subtract)
            terms_c()
        early = [lambda j=j: ts(blk("OHl", j), R("lo"), j - 15.5, ALU.is_equal) for j in range(LO0)] if t == 0 else \
            [lambda j=j: ts(blk("OHh", j), R("hi"), 64.0 * j, ALU.is_equal) for j in range(LO0 if t == 1 else 0)]
        for fn in early:
            fn()
        if t < 2:
            ts(R("Ln"), R("ps2", 0, 128), -64.0, ALU.add)
            for r in range(16):
                mm(R("ps4", 256, 264), R("Ibf"), R("miss", 128 * t + r, 128 * t + 128, 16), r == 0, r == 15)
            y0 = [0]

            def y4(y1, by_v=False):
                for a, b in ((y0[0], min(y1, 64)), (max(y0[0], 64), y1)):
                    if a < b:
                        if by_v:
                            ts(R("Y4", 16 * a, 16 * b), IND(dd, 0, DW, ls, a, b), -0.25, ALU.mult)
                        else:
                            act(R("Y4", 16 * a, 16 * b), IND(dd, 0, DW, ls, a, b), ACT.Identity, scale=-0.25)
                        if b % 64 == 0:
                            add(blk("Y", b // 64 - 1, 1024), blk("Y4", b // 64 - 1, 1024))
                y0[0] = max(y0[0], y1)

            def onward():
                y4(Y4A[t][0])
                succ_a(t + 1, SPL[t])
                misses_out(t)
                y4(Y4A[t][1])
                succ_b(t + 1)
                y4(128)
            if not Y4V[t][1]:
                onward()
        c0 = 128 - len(hot) if t == 0 else 0
        if w == 32:
            f = [lambda j=j: ts(blk("OHl", j), R("lo"), j - 15.5, ALU.is_equal) for j in range(LO0 if t == 0 else 0, 32)]
            f += hots()[c0:128 - NS[t]]
        else:
            f = [lambda j=j: ts(blk("OHh", j), R("hi"), 64.0 * j, ALU.is_equal) for j in range(LO0, 64)]
            f += [lambda j=j: ts(blk("OHh", 64 + j), R("lo"), j - 31.5, ALU.is_equal) for j in range(64)]
        if t == 2:
            hots_s(128 - NS[2], 124)
            terms_c2(0)
            hots_s(124)
            terms_c2(1)
        for i, fn in enumerate(f):
            if t < 2 and Y4V[t][1] and i == Y4V[t][0]:
                y4(Y4V[t][1], True)
                onward()
            if t < 2 and i == LCAT[t]:
                lists_c((1,))
            if t < 2 and i == LCAT[t] + 6:
                lists_c((0, 2))
            fn()
        if t == 0:
            ts(R("pairb"), pr, w / 2 - 0.5, ALU.add)
        if t == 0:
            tt(R("N1"), R("tc"), R("took"), ALU.add)
        if t < 2 and LCAT[t] >= len(f):
            lists_c()

        def hist(gi):
            for c in range(16 * gi, 16 * gi + 16):
                if w == 32:
                    o = blk(sb, gi - nv, 32) if gi >= nv else blk("ps4", gi, 32)
                    mm(o, blk("OHh", c), R("OHl", c, 4096, 128), c % 16 == 0, c % 16 == 15)
                else:
                    gh, gl = c // 64, c // 16 % 4
                    mm(R("ps4", 64 * gl, 64 * gl + 64, 1, 64 * gh, 64 * gh + 64), R("OHh", c, 8192, 128),
                       R("OHh", 8192 + c, 16384, 128), c % 16 == 0, c % 16 == 15)
        nv, sb = 8 - NS[t] // 16, "ps3" if t == 2 else "ps5"
        end = lambda gi: (3 * 16 * (gi - nv + 1) if gi >= nv else 32 + 16 * (gi + 1)) if t == 2 else (gi < nv) + (nv > gi >= c0 // 16)
        turn = sorted(range(8), key=end)
        sums = R("tab", 0, 32 * (8 - nv))
        for gi in turn:
            if gi == turn[-1] and t == 2:
                mm(R("ps4", 32 * nv, 256), R("Df"), sums)
            hist(gi)
            if gi == 7 and nv < 8 and t == 2:
                act(sums, R(sb, 0, 32 * (8 - nv)), ACT.Copy)

        def close():
            if nv < 8 and t < 2:
                cp(sums, R(sb, 0, 32 * (8 - nv)))
                mm(R("ps4", 32 * nv, 256), R("Df"), sums)
        return close

    def gates(t, close):
        mine = [(ch, True, 0, 64) for ch in sorted(range(NV[t]), key=lambda ch: ch % 2)] + [(5, True, 64 - NVH[t], 64)] * (NVH[t] > 0)
        his = [(ch, False, 0, 64 - NVH[t] if ch == 5 else 64) for ch in range(NV[t], 6)]
        a, b = PAYAT[t - 1] if t > 0 else (0, 0)
        for x in his[:b] + mine[:max(0, a - 1)]:
            chunk(t, *x)
        if t > 0:
            close()
            chunk(t, *mine[a - 1])
            marks_out(t - 1)
        for x in his[b:] + mine[a:]:
            chunk(t, *x)
        succ_c(t)
        gate(t, SI[t])
        if t > 0:
            place_list(t - 1)
            miss_weight(t - 1)
        for x in TESTS[t]:
            if x < 6:
                gate(t, (x,))
            else:
                count(t, x - 6, range(0, 16, 4 if x == 8 else 1))
        if t > 0:
            terms_a(t - 1, 0, TA)

    hot = hots()
    if myt > 0:
        early()
    ms(blk("nxb", 0, 1024), 64.0)
    ms(R("X", 0, 512), 0.0)
    mm(R("ps0"), R("Ibf"), R("X", 0, 512), True, False)
    ms(R("D1", 0, 16), 0.0)

    def late():
        iota(R("ib"), [[0, 256]], 0, 1)
        for n, a, b in (("X", 512, 528), ("incl", 256, 288), ("e8", 0, 16), ("th", 0, 16)):
            iota(R(n, a, b), [[0, b - a]], 0)
        sel(R("Tri"), R("ib", 0, 128), [[1, 128]], ALU.is_gt, 0, -1)
        sel(R("r3"), R("ib", 0, 192), [[0, 64], [1, 3]], ALU.is_gt, 0, 0)
        for w in sorted(set(WL)):
            sel(R("rst%d" % w), R("ib"), [[0, 256 // w], [1, w]], ALU.is_gt, 0, 0)
        if 64 in WL:
            sel(blk("Hf", 0), R("ib", 0, 128), [[0, 128]], ALU.is_gt, 64, -1)
            sel(blk("Hf", 1), R("ib", 0, 128), [[0, 128]], ALU.is_ge, -64, 1)
        ts(R("pd", 64, 96), R("Pti", 0, 32), col("PF", 8), ALU.add, col("PF", 23), ALU.mult)
        ts(R("pd", 96, 128), R("Pti", 32, 64), col("PF", 27), ALU.mult)
        ts(R("ta", 0, 8), R("Pti", 144, 152), col("PF", 9), ALU.add)
        if 64 in WL:
            ts(R("Lp64", 0, 32, 2), R("Pti", 64, 80), col("PF", 8), ALU.add)
            cp(R("Lp64", 1, 32, 2), R("Pti", 32, 48))
        cp(R("Lth"), R("Pti", 80, 112))
        tt(R("pd", 128, 160), R("pd", 64, 96), R("pd", 96, 128), ALU.add)
        ts(R("ta", 8, 16), R("ta", 0, 8), 8.0, ALU.is_lt)
        ts(R("Lx"), R("Pti", 112, 144), col("PF", 22), ALU.add)
        ts(R("BM"), R("BM"), col("PF", 4), ALU.is_equal)
        ts(R("Lg"), R("ta", 0, 8), -1.0, ALU.add)
        cp(R("Lp32"), R("pd", 128, 160))
        tt(R("ta", 16, 24), R("ta", 0, 8), R("ta", 8, 16), ALU.mult)
        ts(R("B16"), R("B16"), col("PF", 2), ALU.is_equal)
        cp(R("Lw"), R("ta", 16, 24))

    if myt > 0:
        late()
    hots_s(128 - NS0[myt], 128)
    for _ in range(HU):
        hot.pop(0)()
    nx_in(0)
    for j in range(1, 4):
        dma("Y", ap(blk("nxb", j, 1024)), ap(blk("nxb", 0, 1024)), "dfill", 48, [blk("nxb", j, 1024)], [blk("nxb", 0, 1024)])

    def go():
        if myt != 1:
            return
        op("G", None, [], [R("G")])
        told = sorted(set(x[0] for x in loads_of(T, rank)))
        lsum[0] += len(told)
        op("G", lambda: g.remote_dma_fused([RemoteDMATransfer(
            dst_ids=[dst(topo, hs[i])], dma_engine_mask=bits(rest[i:i + 1]), remote_sem=T.sem.go) for i in told],
            local_sem=T.sem.lsem), [], [], sem="remote")
    ts(R("Ln"), R("ps3", 0, 128), -64.0, ALU.add)
    if myt == 1:
        nx_out()
    for _ in range(HV if myt != 1 else 0):
        hot.pop(0)()
    succ_a(0, 64)
    for j in range(2):
        act(blk("U5", j, 960), R("E", 0, 960), ACT.Identity, bias=1.0, scale=0.0)
    succ_b(0)
    u_in()
    act(R("U5", 0, 1920, 5), R("E", 0, 384), ACT.Identity, scale=0.0)
    go()
    if myt > 1:
        nx_out()
    if myt == 0:
        late()
    ts(col("PF", 29), col("PF", 28), -1.0, ALU.add)
    for _ in range(HX[myt]):
        hot.pop(0)()
    lists_c()
    close = None
    for t in range(3):
        gates(t, close)
        if t == 0:
            act(R("U5", 4, 1920, 5), R("ps5", 128, 512), ACT.Identity, scale=1.0 / 64)
            act(R("I2k"), R("Ibf"), ACT.Identity, scale=2048.0)
            act(R("Dg"), R("Ibf"), ACT.Identity, scale=col("PF", 16))
            act(R("Bh"), R("B1"), ACT.Identity, scale=0.5)
            for w in sorted(set(WL)):
                for j, v in enumerate((1.0 / w, 1024.0 / w, -1024.0 / w)):
                    act(blk("I%d" % w, j), R("Ibf"), ACT.Identity, scale=v)
            hots_s(128 - NS[0], 128 - NS0[myt])
            nx_in(1)

        def between(extra):
            if t == 1:
                op("Y", None, [], [R("Vw")])
                nx_in(2)
            bound(t - 1, extra)
            terms_b(t - 1, 0, TB1)
        draw(t, between)
        close = after_draw(t)

    close()
    for a, b in ((0, 64), (64, 128 - YV)):
        if a < b:
            act(R("Y4", 16 * a, 16 * b), IND("D1", 0, DW, "Ls0", a, b), ACT.Identity, scale=0.25)
    marks_out(2)
    if YV:
        ts(R("Y4", 2048 - 16 * YV, 2048), IND("D1", 0, DW, "Ls0", 128 - YV, 128), 0.25, ALU.mult)
    terms_b(1, TB3)
    terms_d()
    terms_a(2, 0, 1024)
    terms_a(2, 1024, 2048)
    for k in range(4):
        tt(R("dr", 384 + 128 * k, 512 + 128 * k), IND("pairb", 0, 128, "Lx", 8 * k, 8 * k + 8), R("BM"), ALU.mult)
        mm(blk("ps2", 2 * (k % 2) + k // 2, 32), R("dr", 384 + 128 * k, 512 + 128 * k), R("R12"))
    terms_b(2, 0, TB2)
    for h in range(2):
        for k in range(4):
            a = 16 + 512 * (k % 2) + 256 * h
            y = blk(HELD[k], h, 256) if k < 3 else R("Y", 1024 * h + k, 1024 * h + 1024, 4)
            tt(R(TABS[k // 2], a, a + 256), R("Y4", 1024 * h + k, 1024 * h + 1024, 4), y, ALU.subtract)
    both = lambda n, a=0, b=512: tt(R(n, 1040 + a, 1040 + b), R(n, 16 + a, 16 + b), R(n, 528 + a, 528 + b), ALU.add)
    both("G")
    both("nxw", 0, SUM0)
    bound(2, lambda: both("nxw", SUM0) if SUM0 < 512 else None)
    for j in range(2):
        ts(R("Z3", j + 1, 192, 3), blk("ps2", j, 64), col("ps3", 257), ALU.is_lt, 512.0 * (j + 1), ALU.mult)
    scan(R("dr", 0, 192), R("r3"), R("Z3"))
    ts(R("Ln", 0, 64), R("dr", 2, 192, 3), col("PF", 17), ALU.add)
    for h in range(2):
        act(blk("Y4", h, 256), IND("G", 0, 1552, "Ln", 16 * h, 16 * h + 16), ACT.Identity)
    act(R("tab", 0, 512), R("ps0"), ACT.Copy)
    dma("S", T.ye[:], T.tab[:, 0:512], "doe", 16, [], [R("tab", 0, 512)])
    for h in range(2):
        tt(blk("tab", 2 + h, 256), IND("nxw", 0, 1552, "Ln", 32 + 16 * h, 48 + 16 * h), blk("Y4", h, 256), ALU.add)
        dma("YS"[h], T.yx[:, 256 * h:256 * h + 256], T.tab[:, 512 + 256 * h:768 + 256 * h], ("dox", "dox2")[h], 16, [],
            [blk("tab", 2 + h, 256)])

    emit(g, T, Q, ops, lsum[0])


def emit(g, T, Q, ops, lsum):
    toks = []
    lw = {n: np.full(v[0], -1, np.int64) for n, v in SB.items()}
    rd = {n: {} for n in SB}
    bank = {}
    pw = {}
    clock = {e: {} for e in Q}
    count = {e: 0 for e in Q}
    need = {e: set() for e in Q}
    finals = {}
    for o in ops:
        e = o["e"]
        if e is None:
            toks.append((o["sem"][0], o["sem"][1], {}))
            finals[o["sem"][0]] = o["sem"][1]
            for x in o["w"]:
                lw[x[0]][x[1]:x[2]] = len(toks) - 1
            continue
        deps = set()
        for x in o["r"] + o["w"]:
            if x[0] not in SB:
                for e2, tk in bank.get(x[0], {}).items():
                    if e2 != e:
                        deps.add(tk)
                if e != "P" and (x[0], e) in pw:
                    deps.update(np.unique(pw[x[0], e][x[1]:x[2]:x[3]]).tolist())
            else:
                deps.update(np.unique(lw[x[0]][x[1]:x[2]:x[3]]).tolist())
        for x in o["w"]:
            if x[0] in SB:
                for arr in rd[x[0]].values():
                    deps.update(np.unique(arr[x[1]:x[2]:x[3]]).tolist())
        deps.discard(-1)
        waits = {}
        ck = clock[e]
        for tk in sorted(deps, reverse=True):
            key, val, c2 = toks[tk]
            if o["sem"] is not None and o["sem"] != "remote" and key == o["sem"][0]:
                continue
            if ck.get(key, 0) >= val:
                continue
            waits[key] = max(waits.get(key, 0), val)
            ck[key] = val
            for k2, v2 in c2.items():
                if ck.get(k2, 0) < v2:
                    ck[k2] = v2
        for key, val in waits.items():
            if key in need:
                need[key].add(val)
        o["waits"] = waits
        if o["fn"] is None or o["sem"] == "remote":
            continue
        if o["sem"] is None:
            count[e] += 1
            o["idx"] = count[e]
            toks.append((e, count[e], dict(ck)))
        else:
            toks.append((o["sem"][0], o["sem"][1], dict(ck)))
            finals[o["sem"][0]] = o["sem"][1]
        tk = len(toks) - 1
        rk = e if o["sem"] is None else o["sem"][0]
        for x in o["r"]:
            if x[0] in SB:
                if rk not in rd[x[0]]:
                    rd[x[0]][rk] = np.full(SB[x[0]][0], -1, np.int64)
                rd[x[0]][rk][x[1]:x[2]:x[3]] = tk
            else:
                bank.setdefault(x[0], {})[e] = tk
        for x in o["w"]:
            if x[0] in SB:
                lw[x[0]][x[1]:x[2]:x[3]] = tk
            else:
                bank.setdefault(x[0], {})[e] = tk
                pw.setdefault((x[0], e), np.full(512, -1, np.int64))[x[1]:x[2]:x[3]] = tk
    num = {e: {v: i + 1 for i, v in enumerate(sorted(need[e]))} for e in Q}
    for o in ops:
        e = o["e"]
        if e is None:
            continue
        for key, val in o["waits"].items():
            if key in num:
                Q[e].wait_ge(T.sem["c" + key], num[key][val])
            else:
                Q[e].wait_ge(T.sem[key], val)
        if o["fn"] is None:
            continue
        ins = o["fn"]()
        if o["sem"] is None:
            if o["idx"] in num[e]:
                ins.then_inc(T.sem["c" + e], 1)
        elif o["sem"] != "remote":
            ins.then_inc(T.sem[o["sem"][0]], 16)
    for key, val in finals.items():
        g.wait_ge(T.sem[key], val)
    for e in ("V", "S", "P", "G"):
        if need[e]:
            g.wait_ge(T.sem["c" + e], len(need[e]))
    g.wait_ge(T.sem.lsem, lsum)
